import numpy as np, ml_dtypes
CORES = [40,41,42,43,44,45,46,47]
N = 8
BF = ml_dtypes.bfloat16
def gentries(a):
    return np.ascontiguousarray(a.reshape(8, 16, -1).transpose(0, 2, 1)).reshape(8, -1)
def gtable(e):
    e = np.asarray(e); return np.ascontiguousarray(e.reshape(8, -1, 16).transpose(0, 2, 1)).reshape(128, -1).astype(np.int32)
W, K, L, T = 4608, 1024, 1, 2
TOP, NEG, EMPTY = 255, 9, 16
def parts(rng):
    j = rng.integers(0, W, (N, 8, 16, W), dtype=np.int32)
    x = rng.integers(0, 16, (N, 8, N, L, K)); x = np.where(rng.random(x.shape) < 0.125, EMPTY, x)
    return j, x, rng.integers(0, 16, (N, 8, K)), rng.integers(0, W, (N, 8, T, K))
def coef(rng, drift):
    c = drift + 50.0 * rng.standard_normal((N, 8, 1, W), dtype=np.float32) + 40.0 * rng.standard_normal((N, 8, 16, W), dtype=np.float32)
    return np.minimum(np.maximum(np.rint(c), -128), 127)
def pack(j, c, x, y, a):
    return {"jm": np.ascontiguousarray(j.reshape(N, 128, W)).astype(np.int32), "cf": (np.ascontiguousarray(c.reshape(N, 128, W)).astype(np.float32) + 0.0).astype(BF),
            "lt": np.ascontiguousarray(x.reshape(N, 8, N * L * K)).astype(np.float32).astype(BF), "y0": np.ascontiguousarray(y).astype(np.float32).astype(BF),
            "st": np.stack([gtable(q.reshape(8, T * K)) for q in a])}
def setup_inputs(rng):
    j, x, y, a = parts(rng)
    return pack(j, coef(rng, rng.choice(np.array([5.0, 15.0, 30.0, 45.0]), (N, 8, 1, 1))), x, y, a)
def setup_inputs_ties(rng):
    j, x, y, a = parts(rng); n = rng.choice(np.array([4, 6, 7, 8, 9]), (N, 8, 1, W))
    o = np.argsort(rng.random((N, 8, 16, W)), axis=2); c = np.where(o < n, -1, (rng.random(o.shape) < 0.8).astype(np.int64))
    p = rng.permutation(16)[:, None]
    c[:, 0] = np.where(p < 8, -1, 1); c[:, 1] = np.where(p < 9, -1, 1); c[:, 2] = np.where(p < 8, -1, 0)
    return pack(j, c, x, y, a)
def setup_inputs_clip(rng):
    j, x, y, a = parts(rng); s = np.where(rng.random((N, 8, 1, W)) < 0.75, 1, -1)
    c = s * rng.integers(100, 128, (N, 8, 16, W)); c = np.where(rng.random(c.shape) < 0.1, -c, c)
    c[:, 1::2, :5] = -np.abs(c[:, 1::2, :5]) - 1
    r = int(rng.integers(0, N)); x[:, 6, r] = rng.integers(0, 16, (N, L, K)); e = 127 // L
    for d in range(N):
        q = (r + d) % N; c[q, 6] = 1; c[q, 6, 1:8] = -1
        c[q, 6, 8] = -1 if d == 3 else 0
        c[q, 6, 0] = (-128, e, e, 255 - 2 * L * e)[d] if d < 4 else 0
    return pack(j, c, x, y, a)
def setup_inputs_gaps(rng):
    j, x, y, a = parts(rng); x = np.where(rng.random(x.shape) < 0.5, EMPTY, x)
    x[:, 0] = EMPTY; x[:, 1:4] = rng.integers(0, 16, (N, 3, N, L, K))
    for q in range(N):
        for s in range(N):
            if q != s: x[q, 2, s] = EMPTY
            if q != (s - 1) % N: x[q, 3, s] = EMPTY
    c = coef(rng, 20.0); r = int(rng.integers(0, N))
    c[r, 0] = -rng.integers(1, 129, (16, W)); c[r, 1] = -128; c[r, 1, 8:] += (rng.random(W) < 0.5).astype(np.float32)
    x[r, 1, r, 1:] = EMPTY
    return pack(j, c, x, y, a)
def setup_inputs_alike(rng):
    j, x, y, a = parts(rng)
    j[:, ::2] = rng.choice(np.array([0, W - 1, W // 2, 5], np.int32), (N, 4, 16, W)); j[:, 1] = np.arange(W)
    j[:, 6] = rng.integers(0, W, (N, 1, 1))
    x[:, 3] = rng.integers(0, 16, (N, 1, 1, 1)); y[:, 3] = rng.integers(0, 16, (N, 1))
    a[:, 2] = rng.integers(0, W, (N, 1, 1)); a[:, 5] = rng.choice(np.array([0, W - 1]), (N, T, K))
    c = coef(rng, 25.0); r = int(rng.integers(0, N)); c[r] = np.minimum(np.abs(c[r]), 127)
    return pack(j, c, x, y, a)
def setup_inputs_spread(rng):
    j, x, y, a = parts(rng)
    j = np.minimum((W * rng.random(j.shape) ** 3).astype(np.int64), W - 1); a = np.minimum((W * rng.random(a.shape) ** 3).astype(np.int64), W - 1)
    c = np.exp2(8.0 * rng.random((N, 8, 1, W))) * (0.5 * rng.standard_normal((N, 8, 16, W)) + 0.25)
    x = np.minimum((17 * rng.random(x.shape) ** 2).astype(np.int64), EMPTY); y = np.minimum((16 * rng.random(y.shape) ** 2).astype(np.int64), 15)
    return pack(j, np.minimum(np.maximum(np.rint(c), -128), 127), x, y, a)
def check_inputs(d):
    bad = []
    for k, lo, hi in (("jm", 0, W - 1), ("cf", -128, 127), ("lt", 0, 16), ("y0", 0, 15), ("st", 0, W - 1)):
        a = np.asarray(d[k]).astype(np.float32)
        if not (np.all(a == np.floor(a)) and np.min(a) >= lo and np.max(a) <= hi): bad.append("range of " + k)
        if np.any(np.signbit(a) & (a == 0)): bad.append("-0.0 in " + k)
    return bad
def reference(jm, cf, lt, y0, st):
    J = jm.astype(np.int64).reshape(N, 8, 16, W); C = cf.astype(np.float32).astype(np.int64).reshape(N, 8, 16, W)
    x = lt.astype(np.float32).astype(np.int64).reshape(N, 8, N, L, K); y = y0.astype(np.float32).astype(np.int64)
    start = np.stack([gentries(a) for a in st]).astype(np.int64).reshape(N, 8, T, K)
    new = np.full((N, 8, T, K), EMPTY, np.int64); v = np.zeros((N, 8, 16, K), np.int64); g = np.arange(8)[:, None]
    for t in range(T):
        for s in range(N):
            b = J[s][g, y[s], start[s, :, t]]; u = np.take_along_axis(C[s], b[:, None, :], 2)
            live = np.ones((8, K), bool)
            for d in range(N):
                q = (s + d) % N
                slots = [new[s, :, i] for i in range(t - 1, -1, -1)] if d == 0 else []
                for z in slots + [x[q, :, s, l] for l in range(L)]:
                    go = live & (z < EMPTY)
                    b = np.where(go, J[q][g, np.minimum(z, 15), b], b)
                    w = np.minimum(np.maximum(u + np.take_along_axis(C[q], b[:, None, :], 2), -TOP), TOP)
                    u = np.where(go[:, None, :], w, u)
                    hit = go & (np.add.reduce((u < 0).astype(np.int64), axis=1) >= NEG)
                    z[hit] = EMPTY; live = live & ~hit
            new[s, :, t] = np.where(live, y[s], EMPTY)
            y[s] = np.argmax(u, axis=1)
            v[s] = u
    return {"yl": x.reshape(N, 8, N * L * K).astype(np.float32).astype(BF), "yi": new.reshape(N, 8, T * K).astype(np.float32).astype(BF), "yv": v.reshape(N, 128, K).astype(np.float32).astype(BF)}

@@ -1,0 +1,685 @@
+import math
+from concourse.mybir import AluOpType, ActivationFunctionType
+
+ALU, AF = AluOpType, ActivationFunctionType
+N, W, NK = 8, 4608, 1024
+NCH = 2
+n = NK // NCH
+K = n // 16
+NH = 2
+h = n // NH
+PLAN = [[2, 2, 2, 2], [2, 2, 2, 2]]
+NT = max(max(p) for p in PLAN)
+CWID = W + 32
+PER = 72.0
+SC = math.log(2.0) / PER
+A = PER / math.log(2.0)
+HIT = -22.25
+STOP = 44.5
+JB = 6
+JBW = W // JB
+B16, F32, I32, U16 = "bfloat16", "float32", "int32", "uint16"
+
+ST = []
+for _w in range(2):
+    _o, _l = 0, []
+    for _m in PLAN[_w]:
+        _l.append((_o, _m))
+        _o += _m
+    ST.append(_l)
+
+
+def nslots(w, i):
+    return ST[w][i][1] + (1 if w == 1 and i == 0 else 0)
+
+
+SCRATCH, SEMAPHORES = {}, ["kpe", "kv", "ks", "kg", "ls", "lcf", "lst", "llt", "ly", "stores"]
+PLACE = {}
+
+
+def sb(name, cols, dtype=B16):
+    SCRATCH[name] = ("sbuf", [128, cols], dtype)
+    PLACE[name] = (name, 0)
+
+
+def tile(kind, key, cols, dtype=B16):
+    buf = "z" + kind
+    at = SCRATCH[buf][1][1] if buf in SCRATCH else 0
+    SCRATCH[buf] = ("sbuf", [128, at + cols], dtype)
+    PLACE[kind + key] = (buf, at)
+
+
+sb("JW", (1 + NT) * W)
+sb("CW", NT * CWID)
+sb("jmi", W, I32)
+sb("jmf", W, F32)
+sb("io5", 576, F32)
+for _k in ("ones", "RM", "SM", "AM"):
+    sb(_k, 2048)
+for _k in ("ID", "I4", "I8", "LTa", "LTb", "LTR"):
+    sb(_k, 128)
+sb("b8a", 8)
+sb("b8", 8)
+sb("ipi", 2, I32)
+sb("ipj", 2, I32)
+sb("ipf", 2, F32)
+sb("sti", 128, I32)
+sb("stu", 128, U16)
+for _k in ("y0l", "y1l", "yim"):
+    sb(_k, 64)
+sb("yit", 128)
+for _k in ("ohn", "ohy", "ohr"):
+    sb(_k, NK)
+SEMAPHORES += ["ljm%d" % _b for _b in range(JB)]
+for _e in range(NT):
+    sb("lt%d" % _e, 512)
+for _c in range(NCH):
+    for _k in ("mj", "sg", "cc", "vb", "ax"):
+        sb("%s%d" % (_k, _c), n)
+    sb("am%d" % _c, 2 * n)
+    sb("tt%d" % _c, K, F32)
+    sb("ta%d" % _c, 3 * K, F32)
+    sb("jl%d" % _c, K, U16)
+    sb("cl%d" % _c, K, U16)
+    for _k in ["ps", "w"] + ["pv%d" % _x for _x in range(NH)]:
+        SCRATCH["%s%d" % (_k, _c)] = ("psum", [128, 512], F32)
+        PLACE["%s%d" % (_k, _c)] = ("%s%d" % (_k, _c), 0)
+OHS = []
+for _w in range(2):
+    for _o, _m in ST[_w]:
+        for _e in range(_m):
+            if (_o, _e) not in OHS:
+                OHS.append((_o, _e))
+sb("oh", NK * len(OHS))
+MOVES = []
+for _i, (_o, _m) in enumerate(ST[0]):
+    for _k, (_p, _q) in enumerate(ST[1]):
+        _lo, _hi = max(_o, _p), min(_o + _m, _p + _q)
+        if _o != _p and _lo < _hi:
+            MOVES.append((_i, _k, _lo, _hi))
+            tile("mv", "%d%d" % (_i, _k), 64 * (_hi - _lo))
+            SEMAPHORES.append("rmv%d%d" % (_i, _k))
+for _w in range(2):
+    for _i, (_o, _m) in enumerate(ST[_w]):
+        _s = nslots(_w, _i)
+        _x = "%d%d" % (_w, _i)
+        tile("dd", _x, 64 * (_s + 1))
+        tile("es", _x, 64 * _s)
+        tile("ej", _x, 64 * _s, F32)
+        tile("hi", _x, 64 * _s)
+        tile("ls", _x, 64 * _m)
+        tile("do", _x, 64)
+        tile("di", _x, 64)
+        for _c in range(NCH):
+            _y = "%s%d" % (_x, _c)
+            tile("vo", _y, n)
+            tile("vi", _y, n)
+            SEMAPHORES += ["rv" + _y, "rd" + _y]
+            if _i + 1 < len(ST[_w]):
+                tile("to", _y, K, F32)
+                tile("ti", _y, K, F32)
+                SEMAPHORES.append("rt" + _y)
+for _i, (_o, _m) in enumerate(ST[1]):
+    for _e in range(1, _m):
+        tile("yr", "%d%d" % (_i, _e), 64)
+        SEMAPHORES.append("ry%d%d" % (_i, _e))
+for _e in range(1, NT):
+    SEMAPHORES += ["rj%d" % _e, "rc%d" % _e, "rl%d" % _e]
+
+VF, SF, CY, PCY, PF, WAKE, SELF, GAP, HOP, GBW = 5.0, 65.0, 0.95, 0.5, 20.0, 80.0, 40.0, 200.0, 1800.0, 250.0
+FIRST = 1e6
+URGE = {
+    0: {"cc": 600, "cl": 1000, "dd": 1200, "di": -9900, "do": 500, "jl": 3800, "jt": 200, "mj": 1400, "ps": 1400, "psc": -3400, "pv": 900,
+        "sg": 1000, "t": 300, "te": 600, "ti": 100, "to": 1000, "tt": 8900, "vb": -1800, "vi": -14900, "vo": 1700},
+    1: {"dd": 800, "ti": 12400, "mj": 1000, "vi": -5400, "psc": 17000, "te": -200, "t": 700, "jl": -3500, "cl": 3600, "pv": 300, "di": -9700,
+        "ps": 200, "to": 300, "tt": 6600, "sg": 200, "jt": -2400, "vb": 300, "do": 500, "vo": 200},
+    None: {"LTa": -3800, "out": -1500, "ax": -6000, "ipf": 2800, "b8a": -3500, "pad": -1900, "w": -5300, "ohr": 600, "y1l": 22900, "am": -3600,
+           "stu": -1000, "ipi": 15600, "jmf": 5000, "ej": -800, "sti": -6200, "hi": -5000, "ones": -3000, "yo": -26700, "yi": -10000, "yim": -3300,
+           "ID": -21000, "io": 10800, "y0l": 7600, "b": -16500, "ipj": -24300, "LTR": 2100, "jmi": 5800, "RM": 15700, "yiu": -11200, "ls": -8100,
+           "SM": 900, "ohn": -4900, "LTb": -11800, "y1m": 4200, "lt": 9700, "AM": -6200, "ohy": -100, "J": -6200, "I": -1800, "C": -7300, "oh": 300, "es": 600},
+}
+
+
+def program(R, T, topo):
+    ops = []
+    cur = [None]
+    me = T.cores[R]
+
+    def B(name, a, z, step=1):
+        buf, at = PLACE[name]
+        return T[buf][:, at + a:at + z:step] if step > 1 else T[buf][:, at + a:at + z]
+
+    def add(q, dur, reads, writes, calls, sem=None, lat=0.0, tail=0.0, dma=False, bonus=0.0):
+        ops.append({"q": q, "dur": dur, "r": list(reads), "w": list(writes), "calls": calls, "sem": sem, "lat": lat, "tail": tail, "dma": dma, "bonus": bonus, "ch": cur[0]})
+        return len(ops) - 1
+
+    def V(cyc, reads, writes, name, *a):
+        call = {"copy": lambda g: g.vector.tensor_copy(*a), "tt": lambda g: g.vector.tensor_tensor(*a),
+                "ts": lambda g: g.vector.tensor_scalar(*a), "set": lambda g: g.vector.memset(*a)}[name]
+        add("v", VF + CY * max(64, cyc), reads, writes, [call])
+
+    def S(cyc, reads, writes, *a, **kw):
+        add("s", SF + CY * max(64, cyc), reads, writes, [lambda g: g.scalar.activation(*a, **kw)])
+
+    def P(reads, writes, mms):
+        cost = PF
+        for m in mms:
+            cost += PCY * max(64, m[5])
+        add("pe", cost, reads, writes, [(lambda g, m=m: g.tensor.matmul(m[0], m[1], m[2], m[3], m[4])) for m in mms])
+
+    def pick(key, out, in_, pat, cmp_, base, cm, el, src):
+        add("g", 170 + 1.9 * el, [src], [key], [lambda g: g.affine_select(out, in_, pat, cmp_, 0.0, base, cm)], sem="kg")
+
+    def D(sem, nbytes, reads, writes, out, in_, bonus=0.0):
+        add("sync", 100.0, reads, writes, [lambda g: g.sync.dma_start(out, in_)], sem=sem, lat=1800.0, tail=nbytes / GBW, dma=True, bonus=bonus)
+
+    def send(dst, sem, nbytes, reads, landing, out, in_, bonus=0.0):
+        core = T.cores[dst % N]
+        rid, pid, _ = topo.addr(core)
+        mk = topo.mask(me, core)
+        k = add("g", 600.0, reads, [], [lambda g: g.remote_dma(out, in_, T.sem[sem], T.sem.ls, pid, rid, mk)], sem="remote", bonus=bonus)
+        j = add("net", 0.0, [], [landing], [], sem=sem, lat=HOP, tail=nbytes / GBW)
+        ops[j]["after"] = k
+        ops[k]["cnt"] = ops[j]["cnt"] = len(topo.engines(me, core))
+
+    for c in range(NCH):
+        D("ly", 16384 // NCH, [], [("y0l", c)], B("y0l", K * c, K * c + K), T.y0[:, n * c:n * c + n], bonus=9 * FIRST)
+    ltk = [("lt0", (R - x) % N, c) for x in range(N) for c in range(NCH)]
+    per = -(-len(ltk) // (JB - 1))
+    for b in range(JB):
+        D("ljm%d" % b, 128 * JBW * 4, [], [("jmi", b)], T.jmi[:, JBW * b:JBW * b + JBW], T.jm[:, JBW * b:JBW * b + JBW], bonus=FIRST * (8.5 - b))
+        for _, s, c in ltk[per * b:per * b + per]:
+            D("llt", 16384 // NCH, [], [("lt0", s, c)], B("lt0", 64 * s + K * c, 64 * s + K * c + K), T.lt[:, NK * s + n * c:NK * s + n * c + n], bonus=FIRST * (8.0 - b))
+        if b == 0:
+            D("lst", 65536, [], ["sti"], T.sti[:], T.st[:], bonus=8 * FIRST)
+    D("lcf", 128 * W * 2, [], [("C", 0)], T.CW[:, 0:W], T.cf[:], bonus=2 * FIRST)
+    yk = [("y0l", c) for c in range(NCH)]
+    V(1024, [], ["ones"], "set", T.ones[:], 1.0)
+    V(1024, [], ["SM0"], "set", T.SM[:], 0.0)
+    for e in range(NT):
+        V(32, [], [("pad", e)], "set", T.CW[:, CWID * e + W:CWID * e + CWID], 0.0)
+    add("g", 1200.0, [], ["io5"], [lambda g: g.iota(T.io5[:], [[1, 576]], 0, 0, allow_small_or_imprecise_dtypes=True)], sem="kg")
+    add("g", 130.0, [], ["ipi"], [lambda g: g.iota(T.ipi[:], [[0, 2]], 0, 1)], sem="kg")
+    V(2, ["ipi"], ["ipj"], "ts", T.ipj[:], T.ipi[:], 15, None, ALU.bitwise_and)
+    V(2, ["ipj"], ["ipf"], "copy", T.ipf[:], T.ipj[:])
+    pick("RM", T.RM[:], T.ones[:], [[-1, 16], [-16, 8], [0, 16]], ALU.is_equal, 0, 1, 2048, "ones")
+    pick("b8a", T.b8a[:], T.ones[:, 0:8], [[-16, 8]], ALU.is_ge, 0, 1, 8, "ones")
+    pick("b8", T.b8[:], T.b8a[:], [[16, 8]], ALU.is_ge, 15, -1, 8, "b8a")
+    pick("ID", T.ID[:], T.ones[:, 0:128], [[-1, 128]], ALU.is_equal, 0, 1, 128, "ones")
+    V(128, ["ID"], ["I4"], "ts", T.I4[:], T.ID[:], 18.0 * HIT / STOP, None, ALU.mult)
+    V(128, ["ID"], ["I8"], "ts", T.I8[:], T.ID[:], -36.0 * HIT / STOP, None, ALU.mult)
+    smk = [("SM", r) for r in range(16)]
+    for r in range(16):
+        V(8, ["b8", "SM0"], [("SM", r)], "ts", T.SM[:, 129 * r:128 * r + 128:16], T.b8[:], HIT, None, ALU.mult)
+    pick("LTa", T.LTa[:], T.ones[:, 0:128], [[-16, 8], [0, 16]], ALU.is_ge, 0, 1, 128, "ones")
+    pick("LTb", T.LTb[:], T.LTa[:], [[16, 8], [0, 16]], ALU.is_ge, 15, -1, 128, "LTa")
+    pick("LTR", T.LTR[:], T.LTb[:], [[1, 128]], ALU.is_gt, 0, -1, 128, "LTb")
+    for bi, be in enumerate((8, 4, 2, 1)):
+        for m, (step, base) in enumerate(((1000, 0), (-1000, 1000), (1000, -be), (-1000, 1000 - be))):
+            j = 4 * bi + m
+            pick(("AM", j), T.AM[:, 128 * j:128 * j + 128], T.ones[:, 0:128], [[-2 * be, 64 // be], [step, 2], [-1, be]], ALU.is_equal, base, 1, 128, "ones")
+    ik = [("I", b) for b in range(8)]
+    for b in range(8):
+        S(576, ["io5"], [("I", b)], T.JW[:, 576 * b:576 * b + 576], T.io5[:], AF.Exp, bias=float(576 * b * SC), scale=float(SC))
+    jk = {0: [("J", 0, b) for b in range(JB)]}
+    lk = {0: ltk}
+    for b in range(JB):
+        a, z = JBW * b, JBW * b + JBW
+        V(JBW, [("jmi", b)], [("jmf", b)], "copy", T.jmf[:, a:z], T.jmi[:, a:z])
+        S(JBW, [("jmf", b)], [("J", 0, b)], T.JW[:, W + a:W + z], T.jmf[:, a:z], AF.Exp, scale=float(SC))
+    for e in range(1, NT):
+        jk[e] = jk[e - 1] + [("J", e)]
+        lk[e] = [("lt", e)]
+        send(R - e, "rl%d" % e, 131072, ltk, ("lt", e), B("lt%d" % e, 0, 512), T.lt0[:], bonus=FIRST)
+    for e in range(1, NT):
+        pace = [("J", e - 1), ("C", e - 1)] if e > 1 else []
+        send(R - e, "rj%d" % e, 128 * W * 2, jk[0] + pace, ("J", e), T.JW[:, W * (1 + e):W * (2 + e)], T.JW[:, W:2 * W], bonus=FIRST if e == 1 else 0.0)
+        send(R - e, "rc%d" % e, 128 * W * 2, [("C", 0)] + pace, ("C", e), T.CW[:, CWID * e:CWID * e + W], T.CW[:, 0:W])
+    wn = [0]
+
+    def wbank():
+        wn[0] += 1
+        return "w%d" % (wn[0] % NCH)
+
+    def smat(r):
+        return T.SM[:, 128 * r:128 * r + 128]
+
+    def rep(src, natural, reads):
+        wb = wbank()
+        P(["RM"] + reads, [wb], [(B(wb, K * r, K * r + K) if natural else B(wb, r, n, 16), T.RM[:, 128 * r:128 * r + 128], src, True, True, K) for r in range(16)])
+        return wb
+
+    def onehot(out, key, src, natural, reads):
+        wb = rep(src, natural, reads)
+        V(n, ["ipf"], [wb, key], "ts", out, B(wb, 0, n), 15.0, T.ipf[:, 0:1], ALU.min, ALU.is_equal)
+
+    def oh_of(off, e, c):
+        a = NK * OHS.index((off, e)) + n * c
+        return T.oh[:, a:a + n], ("oh", off, e, c)
+
+    def slot_letters(off, e):
+        s = (R - off) % N
+        return B("lt%d" % e, 64 * s, 64 * s + 64)
+
+    def onehots(off, e):
+        s = 64 * ((R - off) % N)
+        for c in range(NCH):
+            out, key = oh_of(off, e, c)
+            onehot(out, key, B("lt%d" % e, s + K * c, s + K * c + K), False, lk[e])
+
+    def gates(w, i, x, e, src, reads):
+        es, ej = "es%d%d" % (w, i), "ej%d%d" % (w, i)
+        a = 64 * x
+        big = W * (1 + e) / A
+        V(32, reads, [(es, x)], "ts", B(es, a, a + 64), src, 15.5, STOP, ALU.is_gt, ALU.mult)
+        S(64, [(es, x)], [(ej, x)], B(ej, a, a + 64), B(es, a, a + 64), AF.Copy, bias=float(big), scale=float(-big / STOP))
+
+    for c in range(NCH):
+        onehot(B("ohn", n * c, n * c + n), ("ohn", c), B("y0l", K * c, K * c + K), True, yk)
+    V(128, ["sti"], ["stu"], "copy", T.stu[:], T.sti[:])
+
+    def image(c, lst, lkey, lo, hi, oh, ohk, tk, natural, out, okey):
+        mj, ps = "mj%d" % c, "ps%d" % c
+        V(1.5 * n, [lkey, ohk] + tk, [mj], "tt", B(mj, 0, n), T.JW[:, lo:hi].indirect(lst), oh, ALU.mult)
+        P(smk + [mj], [ps], [(B(ps, 0, K), smat(r), B(mj, K * r, K * r + K) if natural else B(mj, r, n, 16), r == 0, r == 15, K) for r in range(16)])
+        S(K, [], [ps, okey], out, B(ps, 0, K), AF.Ln, scale=float(1.0 / HIT))
+
+    def jlist(c, t, tkey, w, i, x):
+        ej, jl, ta = "ej%d%d" % (w, i), "jl%d" % c, B("ta%d" % c, 0, K)
+        a = 64 * x + K * c
+        V(K, [tkey, (ej, x)], [("jt", c)], "tt", ta, t, B(ej, a, a + K), ALU.add)
+        V(K, [("jt", c)], [jl], "ts", B(jl, 0, K), ta, float(A), None, ALU.mult)
+
+    def gate(c, t, tkey, w, i, x):
+        es = "es%d%d" % (w, i)
+        a = 64 * x + K * c
+        te = B("ta%d" % c, K, 2 * K)
+        V(2 * K, [tkey, (es, x)], [("te", c)], "tt", te, t, B(es, a, a + K), ALU.max)
+        return te, ("te", c)
+
+    def clist(c, te, tek, stop, skeys, touched):
+        t2, cl = B("ta%d" % c, 2 * K, 3 * K), "cl%d" % c
+        V(2 * K, [tek] + skeys, touched + [("t2", c)], "tt", t2, te, stop, ALU.max)
+        V(K, [("t2", c)], [cl], "ts", B(cl, 0, K), t2, float(A), float(A * STOP), ALU.mult, ALU.min)
+
+    def coefs(c, e, out, okey):
+        cl = "cl%d" % c
+        for q in range(NH):
+            S(1.5 * h, [cl, ("C", e), ("pad", e)], [(okey, q)], B(out, h * q, h * q + h),
+              T.CW[:, CWID * e:CWID * e + CWID].indirect(B(cl, K // NH * q, K // NH * (q + 1))), AF.Copy)
+
+    state = [{} for _ in range(NCH)]
+
+    def enter(w, i, off, c, dd):
+        st = state[c]
+        cur[0] = c
+        if i == 0:
+            oh = ("ohn", "ohy")[w]
+            tt, cl, vb = "tt%d" % c, "cl%d" % c, "vb%d" % c
+            image(c, B("stu", 64 * w + K * c, 64 * w + K * c + K), "stu", W, 2 * W, B(oh, n * c, n * c + n), (oh, c), jk[0], True, B(tt, 0, K), tt)
+            V(K, [tt], [cl], "ts", B(cl, 0, K), B(tt, 0, K), float(A), None, ALU.mult)
+            coefs(c, 0, vb, vb)
+            st["t"], st["tk"] = B(tt, 0, K), tt
+            st["v"], st["vk"] = vb, [(vb, q) for q in range(NH)]
+            st["dead"] = None
+        else:
+            vi, ti, di = "vi%d%d%d" % (w, i - 1, c), "ti%d%d%d" % (w, i - 1, c), "di%d%d" % (w, i - 1)
+            st["t"], st["tk"] = B(ti, 0, K), ti
+            st["v"], st["vk"] = vi, [vi]
+            st["dead"] = (B(di, K * c, K * c + K), (di, c))
+            S(K, [(di, c)], [(dd, 0, c)], B(dd, K * c, K * c + K), B(di, K * c, K * c + K), AF.Copy)
+
+    def lookup(w, i, off, m, c, slots, k):
+        st = state[c]
+        cur[0] = c
+        e, x = slots[k]
+        jl = "jl%d" % c
+        jlist(c, st["t"], st["tk"], w, i, x)
+        if w == 1 and i == 0 and k == 0:
+            oh, ohk = B("ohr", n * c, n * c + n), ("ohr", c)
+        else:
+            oh, ohk = oh_of(off, e, c)
+        hop = k + 1 == len(slots) and i + 1 < len(ST[w])
+        tb = ("to%d%d%d" % (w, i, c)) if hop else ("tt%d" % c)
+        image(c, B(jl, 0, K), jl, 0, W * (2 + e), oh, ohk, ik + jk[e], False, B(tb, 0, K), tb)
+        st["t"], st["tk"] = B(tb, 0, K), tb
+        if hop:
+            ti = "ti%d%d%d" % (w, i, c)
+            send(R + m, "rt%d%d%d" % (w, i, c), 128 * K * 4, [tb], ti, B(ti, 0, K), B(tb, 0, K))
+        st["te"] = gate(c, st["t"], st["tk"], w, i, x)
+
+    def station(w, i, off, m):
+        slots = [(e, e + (1 if w == 1 and i == 0 else 0)) for e in range(m)]
+        if w == 1 and i == 0:
+            slots = [(0, 0)] + slots
+        final = i + 1 == len(ST[w])
+        dst = R - off if final else R + m
+        dd, es = "dd%d%d" % (w, i), "es%d%d" % (w, i)
+        do, di = "do%d%d" % (w, i), "di%d%d" % (w, i)
+        for c in range(NCH):
+            enter(w, i, off, c, dd)
+        for c in range(NCH):
+            lookup(w, i, off, m, c, slots, 0)
+        for k, (e, x) in enumerate(slots):
+            first, last = k == 0, k + 1 == len(slots)
+            nat = last and final
+            for c in range(NCH):
+                st = state[c]
+                cur[0] = c
+                cl, cc, sg, ps, vo, vi = "cl%d" % c, "cc%d" % c, "sg%d" % c, "ps%d" % c, "vo%d%d%d" % (w, i, c), "vi%d%d%d" % (w, i, c)
+                pv = ["pv%d%d" % (q, c) for q in range(NH)]
+                te, tek = st["te"]
+                if first and st["dead"] is None:
+                    V(K, [tek], [cl], "ts", B(cl, 0, K), te, float(A), None, ALU.mult)
+                elif first:
+                    clist(c, te, tek, st["dead"][0], [st["dead"][1]], [])
+                v, vk = st["v"], st["vk"]
+                if not nat:
+                    for q in range(NH):
+                        P(["ID"] + vk, [pv[q]], [(B(pv[q], 0, h), T.ID[:], B(v, h * q, h * q + h), True, False, h)])
+                coefs(c, e, cc, cc)
+                for q in range(NH):
+                    if not nat:
+                        P(["ID", (cc, q)], [pv[q]], [(B(pv[q], 0, h), T.ID[:], B(cc, h * q, h * q + h), False, True, h)])
+                    else:
+                        mm = []
+                        for r in range(16 // NH * q, 16 // NH * (q + 1)):
+                            o = B(pv[q], K * r - h * q, K * r - h * q + K)
+                            mm.append((o, T.ID[:], B(v, r, n, 16), True, False, K))
+                            mm.append((o, T.ID[:], B(cc, r, n, 16), False, True, K))
+                        P(["ID"] + [(cc, y) for y in range(NH)] + vk, [pv[q]], mm)
+                vd = vo if last else "vb%d" % c
+                for q in range(NH):
+                    S(h, [], [pv[q], (sg, q)], B(sg, h * q, h * q + h), B(pv[q], 0, h), AF.Sign, bias=0.5)
+                for q in range(NH):
+                    V(h, [], [pv[q], (vd, q)], "ts", B(vd, h * q, h * q + h), B(pv[q], 0, h), 255.0, -255.0, ALU.min, ALU.max)
+                st["v"], st["vk"] = vd, [(vd, q) for q in range(NH)]
+                if last:
+                    send(dst, "rv%d%d%d" % (w, i, c), 128 * n * 2, st["vk"], vi, B(vi, 0, n), B(vo, 0, n))
+                else:
+                    lookup(w, i, off, m, c, slots, k + 1)
+                ea = 64 * x + K * c
+                pk = ["I4", (es, x)]
+                cnt = B(ps, K, 2 * K)
+                mm = [(cnt, T.I4[:], B(es, ea, ea + K), True, False, K)]
+                if st["dead"] is not None:
+                    mm.append((cnt, T.I8[:], st["dead"][0], False, False, K))
+                    pk += ["I8", st["dead"][1]]
+                for r in range(16):
+                    mm.append((cnt, smat(r), B(sg, K * r, K * r + K) if nat else B(sg, r, n, 16), False, r == 15, K))
+                P(smk + pk + [(sg, q) for q in range(NH)], [ps], mm)
+                a, z = 64 * (x + 1) + K * c, K * c
+                if not last:
+                    te, tek = st["te"]
+                    clist(c, te, tek, cnt, [], [ps])
+                    V(K, [], [ps, (dd, x + 1, c)], "ts", B(dd, a, a + K), cnt, -HIT, STOP, ALU.is_gt, ALU.mult)
+                    st["dead"] = (B(dd, a, a + K), (dd, x + 1, c))
+                else:
+                    V(K, [], [ps, (do, c)], "ts", B(do, z, z + K), cnt, -HIT, STOP, ALU.is_gt, ALU.mult)
+                    send(dst, "rd%d%d%d" % (w, i, c), 128 * K * 2, [(do, c)], (di, c), B(di, z, z + K), B(do, z, z + K))
+                    S(K, [(do, c)], [(dd, x + 1, c)], B(dd, a, a + K), B(do, z, z + K), AF.Copy)
+        cur[0] = None
+        settle(w, i, off, dd, slots)
+
+    def store_yl(s, buf, a, key):
+        for c in range(NCH):
+            D("stores", 16384 // NCH, [key], [("out",)], T.yl[:, NK * s + n * c:NK * s + n * c + n], B(buf, a + K * c, a + K * c + K))
+
+    src1 = {}
+
+    def settle(w, i, off, dd, slots):
+        hi, ls = "hi%d%d" % (w, i), "ls%d%d" % (w, i)
+        for e, x in slots:
+            if w == 1 and i == 0 and x == 0:
+                continue
+            b = 64 * x
+            dk = [(dd, x + 1, c) for c in range(NCH)]
+            if i == 0 and x == 0:
+                hit, hk = B(dd, 64, 128), dk
+            else:
+                V(128, dk + [(dd, x, c) for c in range(NCH)], [(hi, x)], "tt", B(hi, b, b + 64), B(dd, b + 64, b + 128), B(dd, b, b + 64), ALU.subtract)
+                hit, hk = B(hi, b, b + 64), [(hi, x)]
+            src, sk = (slot_letters(off, e), lk[e]) if w == 0 else src1[(i, e)]
+            o = B(ls, 64 * e, 64 * e + 64)
+            V(128, sk + hk, [(ls, e)], "tt", o, src, hit, ALU.max)
+            if w == 1:
+                V(32, [(ls, e)], [("yo", i, e)], "ts", o, o, 16.0, None, ALU.min)
+                if e == 0:
+                    store_yl((R - off) % N, ls, 0, ("yo", i, 0))
+                else:
+                    yr = "yr%d%d" % (i, e)
+                    send(R + e, "ry%d%d" % (i, e), 16384, [("yo", i, e)], yr, B(yr, 0, 64), o)
+                    store_yl((R - e - off) % N, yr, 0, yr)
+        if w == 0:
+            for a, b, lo, hh in MOVES:
+                if a == i:
+                    mv = "mv%d%d" % (a, b)
+                    send(R - off + ST[1][b][0], "rmv%d%d" % (a, b), 16384 * (hh - lo), [(ls, d - off) for d in range(lo, hh)], mv,
+                         B(mv, 0, 64 * (hh - lo)), B(ls, 64 * (lo - off), 64 * (hh - off)))
+
+    for i, (off, m) in enumerate(ST[0]):
+        for e in range(m):
+            gates(0, i, e, e, slot_letters(off, e), lk[e])
+    for e in range(NT):
+        for q in OHS:
+            if q[1] == e:
+                onehots(q[0], e)
+        if e == 0:
+            for c in range(NCH):
+                onehot(B("ohr", n * c, n * c + n), ("ohr", c), B("y0l", K * c, K * c + K), False, yk)
+    for i, (off, m) in enumerate(ST[0]):
+        station(0, i, off, m)
+    hv, hd = "vi0%d" % (len(ST[0]) - 1), "di0%d" % (len(ST[0]) - 1)
+    for c in range(NCH):
+        a = K * c
+        V(K, [(hd, c)], [("es10", 0)], "copy", B("es10", a, a + K), B(hd, a, a + K))
+        S(K, [(hd, c)], [("ej10", 0)], B("ej10", a, a + K), B(hd, a, a + K), AF.Copy, bias=float(W / A), scale=float(-W / A / STOP))
+    for b, (off, m) in enumerate(ST[1]):
+        for e in range(m):
+            d = off + e
+            for a, (o0, m0) in enumerate(ST[0]):
+                if o0 <= d < o0 + m0:
+                    if o0 == off:
+                        ap, key = B("ls0%d" % a, 64 * (d - o0), 64 * (d - o0) + 64), [("ls0%d" % a, d - o0)]
+                    else:
+                        lo = max(o0, off)
+                        ap, key = B("mv%d%d" % (a, b), 64 * (d - lo), 64 * (d - lo) + 64), ["mv%d%d" % (a, b)]
+            src1[(b, e)] = (ap, key)
+            gates(1, b, e + (1 if b == 0 else 0), e, ap, key)
+    for c in range(NCH):
+        vi = hv + str(c)
+        ax, am = "ax%d" % c, "am%d" % c
+        src, sk, wd, pos = vi, vi, n, 0
+        for bi in range(4):
+            hf = wd // 2
+            wb = wbank()
+            mm = []
+            for j in range(2):
+                for k in range(2):
+                    q = 4 * bi + 2 * j + k
+                    mm.append((B(wb, hf * j, hf * j + hf), T.AM[:, 128 * q:128 * q + 128], B(src, pos + hf * k, pos + hf * k + hf), k == 0, k == 1, hf))
+            P([("AM", 4 * bi + y) for y in range(4)] + [sk], [wb], mm)
+            S(hf, [], [wb, ax], B(ax, 0, hf), B(wb, 0, hf), AF.Copy)
+            npos = 0 if bi == 0 else pos + wd
+            V(hf, [ax], [wb, (am, bi)], "tt", B(am, npos, npos + hf), B(ax, 0, hf), B(wb, hf, 2 * hf), ALU.max)
+            src, sk, wd, pos = am, (am, bi), hf, npos
+        wb = rep(B(am, pos, pos + K), True, [(am, 3)])
+        V(n, [vi], [wb, (am, "eq")], "tt", B(am, n, 2 * n), B(vi, 0, n), B(wb, 0, n), ALU.is_equal)
+        w2 = wbank()
+        P(["LTR", (am, "eq")], [w2], [(B(w2, 0, n), T.LTR[:], B(am, n, 2 * n), True, True, n)])
+        V(n, [(am, "eq")], [w2, ("ohy", c)], "tt", B("ohy", n * c, n * c + n), B(am, n, 2 * n), B(w2, 0, n), ALU.is_gt)
+    for i, (off, m) in enumerate(ST[1]):
+        station(1, i, off, m)
+    for c in range(NCH):
+        ax, d1, v1 = "ax%d" % c, "di1%d" % (len(ST[1]) - 1), "vi1%d%d" % (len(ST[1]) - 1, c)
+        a = K * c
+        S(n, [("ohy", c), "ipf"], [ax], B(ax, 0, n), B("ohy", n * c, n * c + n), AF.Copy, scale=T.ipf[:, 0:1])
+        wb = wbank()
+        P(smk + [ax], [wb], [(B(wb, 0, K), smat(r), B(ax, K * r, K * r + K), r == 0, r == 15, K) for r in range(16)])
+        y1, ym = B("y1l", a, a + K), B("yim", a, a + K)
+        V(K, [], [wb, ("y1l", c)], "ts", y1, B(wb, 0, K), float(1.0 / HIT), None, ALU.mult)
+        V(K, [("y0l", c), (hd, c)], [("yim", c)], "tt", ym, B("y0l", a, a + K), B(hd, a, a + K), ALU.max)
+        V(K, [("yim", c), ("dd10", 1, c)], [("yiu", c)], "tt", ym, ym, B("dd10", 64 + a, 64 + a + K), ALU.max)
+        V(K, [("yiu", c)], [("yi0", c)], "ts", B("yit", a, a + K), ym, 16.0, None, ALU.min)
+        V(K, [("y1l", c), (d1, c)], [("y1m", c)], "tt", y1, y1, B(d1, a, a + K), ALU.max)
+        V(K, [("y1m", c)], [("yi1", c)], "ts", B("yit", 64 + a, 64 + a + K), y1, 16.0, None, ALU.min)
+        for t in range(2):
+            D("stores", 16384 // NCH, [("yi%d" % t, c)], [("out",)], T.yi[:, NK * t + n * c:NK * t + n * c + n], B("yit", 64 * t + a, 64 * t + a + K))
+        D("stores", 128 * n * 2, [v1], [("out",)], T.yv[:, n * c:n * c + n], B(v1, 0, n))
+    return ops
+
+
+def depend(ops):
+    writer, readers = {}, {}
+    for k, o in enumerate(ops):
+        d = {}
+        for key in o["r"]:
+            for x in writer.get(key, []):
+                d[x] = True
+        for key in o["w"]:
+            if key == ("out",):
+                continue
+            for x in writer.get(key, []) + readers.get(key, []):
+                d.setdefault(x, False)
+        if "after" in o:
+            d[o["after"]] = True
+        o["d"] = d
+        for key in o["w"]:
+            if key in (("es10", 0), ("ej10", 0)):
+                writer.setdefault(key, []).append(k)
+            else:
+                writer[key] = [k]
+            readers[key] = []
+        for key in o["r"]:
+            readers.setdefault(key, []).append(k)
+
+
+def kind(o):
+    name = o["w"][-1] if o["w"] else (o["r"][0] if o["r"] else "")
+    name = (name if isinstance(name, str) else name[0]).rstrip("0123456789")
+    return name + ("c" if o["q"] == "pe" and any(str(x[0]).startswith("sg") for x in o["r"]) else "")
+
+
+def order(ops):
+    cnt = len(ops)
+    nxt = [[] for _ in range(cnt)]
+    for k, o in enumerate(ops):
+        for x in o["d"]:
+            nxt[x].append(k)
+    prio = [0.0] * cnt
+    for k in range(cnt - 1, -1, -1):
+        o = ops[k]
+        best = 0.0
+        for y in nxt[k]:
+            best = max(best, prio[y] + WAKE)
+        prio[k] = best + o["dur"] + o["lat"] + o["tail"]
+    urge = [prio[k] + o["bonus"] + URGE[o["ch"]].get(kind(o), 0) for k, o in enumerate(ops)]
+    left = [len(o["d"]) for o in ops]
+    ready = [0.0] * cnt
+    cand = {}
+    for k in range(cnt):
+        if left[k] == 0:
+            cand.setdefault(ops[k]["q"], []).append(k)
+    free, lane, out = {}, 0.0, []
+
+    def rank(x):
+        return urge[x]
+    while cand:
+        t, q = None, None
+        for y in cand:
+            f = max(free.get(y, 0.0) if y != "net" else 0.0, min(ready[k] for k in cand[y]))
+            if t is None or f < t:
+                t, q = f, y
+        k = max((x for x in cand[q] if ready[x] <= t + (GAP if q != "net" else 0.0)), key=rank)
+        if ready[k] > t:
+            fit = [x for x in cand[q] if ready[x] <= t and t + ops[x]["dur"] <= ready[k] + 20.0]
+            if fit:
+                k = max(fit, key=rank)
+            else:
+                t = ready[k]
+        cand[q].remove(k)
+        if not cand[q]:
+            del cand[q]
+        o = ops[k]
+        end = t + o["dur"]
+        free[q] = end
+        if o["tail"]:
+            lane = max(end, lane) + o["tail"]
+            end = lane + o["lat"]
+        out.append(k)
+        for y in nxt[k]:
+            left[y] -= 1
+            ready[y] = max(ready[y], end + (WAKE if ops[y]["q"] != q else SELF))
+            if left[y] == 0:
+                cand.setdefault(ops[y]["q"], []).append(y)
+    return out
+
+
+QSEM = {"pe": "kpe", "v": "kv", "s": "ks"}
+
+
+def rank_program(g, core, T, topo):
+    rank = T.rank_of(core)
+    if rank is None:
+        return
+    ops = program(rank, T, topo)
+    depend(ops)
+    seq = order(ops)
+    total = {}
+    for o in ops:
+        if o["dma"]:
+            total[o["sem"]] = total.get(o["sem"], 0) + 16
+    eng = {"pe": g.tensor, "v": g.vector, "s": g.scalar, "g": g, "sync": g.sync}
+    count, sent, arrived, know = {}, 0, {}, {}
+    for k in seq:
+        o = ops[k]
+        q = o["q"]
+        if q == "net":
+            o["done"] = [(o["sem"], o["cnt"])]
+            o["know"] = {o["sem"]: o["cnt"]}
+            arrived[o["sem"]] = o["cnt"]
+            continue
+        mine = know.setdefault(q, {})
+        need, merge = {}, []
+        for x, hard in o["d"].items():
+            p = ops[x]
+            if p["sem"] == "remote" or (not hard and p["q"] == q == "pe"):
+                continue
+            for s, c in p["done"]:
+                if mine.get(s, 0) < c:
+                    need[s] = max(need.get(s, 0), c)
+            merge.append(x)
+        for s in sorted(need):
+            implied = False
+            for x in merge:
+                if ops[x]["know"].get(s, 0) >= need[s] and ops[x]["done"][0][0] != s:
+                    implied = True
+            if not implied:
+                eng[q].wait_ge(T.sem[s], int(need[s]))
+        for x in merge:
+            for s, c in ops[x]["know"].items():
+                mine[s] = max(mine.get(s, 0), c)
+        sem = o["sem"] or QSEM.get(q)
+        for call in o["calls"]:
+            ins = call(g)
+            if sem == "remote":
+                sent += o["cnt"]
+            elif o["dma"]:
+                ins.then_inc(T.sem[sem], 16)
+            else:
+                count[sem] = count.get(sem, 0) + 1
+                ins.then_inc(T.sem[sem], 1)
+        o["know"] = dict(mine)
+        if sem == "remote":
+            o["done"] = []
+            continue
+        c = total[sem] if o["dma"] else count[sem]
+        o["done"] = [(sem, c)]
+        o["know"][sem] = max(o["know"].get(sem, 0), c)
+    for s in ("kpe", "kv", "ks", "kg"):
+        g.wait_ge(T.sem[s], int(count[s]))
+    for s in sorted(total):
+        g.wait_ge(T.sem[s], int(total[s]))
+    for s in sorted(arrived):
+        g.wait_ge(T.sem[s], int(arrived[s]))
+    g.wait_ge(T.sem.ls, int(sent))

@@ -1,531 +1,493 @@
 import math
+from concourse.bass import DstId, RemoteDMATransfer
 from concourse.mybir import AluOpType, ActivationFunctionType
 
 ALU, AF = AluOpType, ActivationFunctionType
 N, W, NK = 8, 4608, 1024
-NCH = 2
-n = NK // NCH
-K = n // 16
-NH = 2
-h = n // NH
-PLAN = [[2, 2, 2, 2], [2, 2, 2, 2]]
-NT = max(max(p) for p in PLAN)
-CWID = W + 32
-PER = 72.0
+BW = W // N
+n, K = 512, 32
+PER = 80.0
+FO = 70
+D = int(PER) * FO
+F = 2.0 ** FO
 SC = math.log(2.0) / PER
 A = PER / math.log(2.0)
-HIT = -22.25
-STOP = 44.5
-JB = 6
-JBW = W // JB
+LOW = 63.8 * PER + 0.35
+WID = D + W
+OFF = [[0, 0, 1, 2, 3, 4, 5, 6, 7], [0, 0, 0, 1, 2, 3, 4, 5, 6, 7]]
+PAIRS = [[(1,), (2, 3), (4, 5), (6, 7), (8,)], [(1, 2), (3, 4), (5, 6), (7, 8), (9,)]]
+CALLS = {"J": [[1, 2, 3, 4], [5, 6, 7]], "C": [[1, 2, 3, 4], [5, 6, 7]]}
 B16, F32, I32, U16 = "bfloat16", "float32", "int32", "uint16"
 
-ST = []
-for _w in range(2):
-    _o, _l = 0, []
-    for _m in PLAN[_w]:
-        _l.append((_o, _m))
-        _o += _m
-    ST.append(_l)
-
-
-def nslots(w, i):
-    return ST[w][i][1] + (1 if w == 1 and i == 0 else 0)
-
-
-SCRATCH, SEMAPHORES = {}, ["kpe", "kv", "ks", "kg", "ls", "lcf", "lst", "llt", "ly", "stores"]
-PLACE = {}
+SCRATCH = {}
+SEMAPHORES = ["kpe", "kv", "ks", "kg", "ls", "xl", "xs", "rl", "rs", "ll", "lst", "jo", "co", "xy", "ry", "ly", "xe", "re", "xv", "rv", "xt", "rt", "stores"]
+SEMAPHORES += ["lj%d" % _b for _b in range(N)]
+for _k in range(len(CALLS["J"])):
+    SEMAPHORES += ["rj%d" % _k, "jr%d" % _k]
+for _k in range(len(CALLS["C"])):
+    SEMAPHORES += ["xc%d" % _k, "rc%d" % _k, "cr%d" % _k]
 
 
 def sb(name, cols, dtype=B16):
     SCRATCH[name] = ("sbuf", [128, cols], dtype)
-    PLACE[name] = (name, 0)
 
 
-def tile(kind, key, cols, dtype=B16):
-    buf = "z" + kind
-    at = SCRATCH[buf][1][1] if buf in SCRATCH else 0
-    SCRATCH[buf] = ("sbuf", [128, at + cols], dtype)
-    PLACE[kind + key] = (buf, at)
-
-
-sb("JW", (1 + NT) * W)
-sb("CW", NT * CWID)
+SCRATCH["ZL"] = ("dram", [15, 128, 64], B16)
+SCRATCH["ZS"] = ("dram", [15, 128, 16], I32)
+SCRATCH["ZJ"] = ("dram", [7, 128, BW], B16)
+SCRATCH["ZC"] = ("dram", [7, 128, BW], B16)
+SCRATCH["XC"] = ("dram", [8, 128, BW], B16)
+SCRATCH["ZY"] = ("dram", [15, 128, 8], B16)
+SCRATCH["ZE"] = ("dram", [15, 128, 64], B16)
+SCRATCH["ZV"] = ("dram", [15, 128, 128], B16)
+SCRATCH["ZT"] = ("dram", [15, 128, 16], B16)
+sb("JW", WID)
+sb("CW", WID)
 sb("jmi", W, I32)
 sb("jmf", W, F32)
-sb("io5", 576, F32)
-for _k in ("ones", "RM", "SM", "AM"):
-    sb(_k, 2048)
-for _k in ("ID", "I4", "I8", "LTa", "LTb", "LTR"):
-    sb(_k, 128)
-sb("b8a", 8)
-sb("b8", 8)
+sb("JS", W)
+for _k, _c in (("ones", 256), ("Z1", 256), ("Z2", 256), ("Z1x", 256), ("IDT", 32), ("BDa", 128), ("BD", 128), ("LTR", 128), ("RM", 2048), ("ROT", 512),
+               ("rta", 512), ("I64", 128), ("I32", 128), ("K16", 32), ("b8a", 8), ("b8", 8), ("LT", 576), ("OH", 9 * NK), ("ohn", NK), ("G1", NK), ("mj", NK),
+               ("A1", 640), ("L1", 512), ("hb", 512), ("YL", 512), ("YI", 128), ("y1l", 64), ("VN", NK)):
+    sb(_k, _c)
 sb("ipi", 2, I32)
 sb("ipj", 2, I32)
 sb("ipf", 2, F32)
+sb("io32", 32, F32)
 sb("sti", 128, I32)
 sb("stu", 128, U16)
-for _k in ("y0l", "y1l", "yim"):
-    sb(_k, 64)
-sb("yit", 128)
-for _k in ("ohn", "ohy", "ohr"):
-    sb(_k, NK)
-SEMAPHORES += ["ljm%d" % _b for _b in range(JB)]
-for _e in range(NT):
-    sb("lt%d" % _e, 512)
-for _c in range(NCH):
-    for _k in ("mj", "sg", "cc", "vb", "ax"):
-        sb("%s%d" % (_k, _c), n)
-    sb("am%d" % _c, 2 * n)
-    sb("tt%d" % _c, K, F32)
-    sb("ta%d" % _c, 3 * K, F32)
-    sb("jl%d" % _c, K, U16)
-    sb("cl%d" % _c, K, U16)
-    for _k in ["ps", "w"] + ["pv%d" % _x for _x in range(NH)]:
+sb("LTf", 576, F32)
+sb("LTu", 576, U16)
+sb("t0", 128, F32)
+sb("l0", 128, U16)
+for _c in range(2):
+    for _k, _w in (("cc", 3 * n), ("sg", 4 * n), ("va", 8 * n), ("vb", 9 * n), ("vf", n), ("xa", 2 * n), ("eq", n), ("oy", n), ("mb", K), ("nc", 2 * K),
+                   ("A0", 9 * K), ("LHa", 8 * K), ("LHb", 9 * K), ("ea", 8 * K), ("eb", 9 * K), ("nf", 9 * K), ("xh", 9 * K), ("ha", 8 * K), ("hc", 9 * K),
+                   ("hit", 8 * K), ("dz", K)):
+        sb("%s%d" % (_k, _c), _w)
+    sb("tt%d" % _c, 2 * K, F32)
+    sb("li%d" % _c, 2 * 10 * 2 * K, U16)
+    sb("lv%d" % _c, 2 * K, U16)
+    for _k in ("pv", "pw", "pj", "pc"):
         SCRATCH["%s%d" % (_k, _c)] = ("psum", [128, 512], F32)
-        PLACE["%s%d" % (_k, _c)] = ("%s%d" % (_k, _c), 0)
-OHS = []
-for _w in range(2):
-    for _o, _m in ST[_w]:
-        for _e in range(_m):
-            if (_o, _e) not in OHS:
-                OHS.append((_o, _e))
-sb("oh", NK * len(OHS))
-MOVES = []
-for _i, (_o, _m) in enumerate(ST[0]):
-    for _k, (_p, _q) in enumerate(ST[1]):
-        _lo, _hi = max(_o, _p), min(_o + _m, _p + _q)
-        if _o != _p and _lo < _hi:
-            MOVES.append((_i, _k, _lo, _hi))
-            tile("mv", "%d%d" % (_i, _k), 64 * (_hi - _lo))
-            SEMAPHORES.append("rmv%d%d" % (_i, _k))
-for _w in range(2):
-    for _i, (_o, _m) in enumerate(ST[_w]):
-        _s = nslots(_w, _i)
-        _x = "%d%d" % (_w, _i)
-        tile("dd", _x, 64 * (_s + 1))
-        tile("es", _x, 64 * _s)
-        tile("ej", _x, 64 * _s, F32)
-        tile("hi", _x, 64 * _s)
-        tile("ls", _x, 64 * _m)
-        tile("do", _x, 64)
-        tile("di", _x, 64)
-        for _c in range(NCH):
-            _y = "%s%d" % (_x, _c)
-            tile("vo", _y, n)
-            tile("vi", _y, n)
-            SEMAPHORES += ["rv" + _y, "rd" + _y]
-            if _i + 1 < len(ST[_w]):
-                tile("to", _y, K, F32)
-                tile("ti", _y, K, F32)
-                SEMAPHORES.append("rt" + _y)
-for _i, (_o, _m) in enumerate(ST[1]):
-    for _e in range(1, _m):
-        tile("yr", "%d%d" % (_i, _e), 64)
-        SEMAPHORES.append("ry%d%d" % (_i, _e))
-for _e in range(1, NT):
-    SEMAPHORES += ["rj%d" % _e, "rc%d" % _e, "rl%d" % _e]
 
-VF, SF, CY, PCY, PF, WAKE, SELF, GAP, HOP, GBW = 5.0, 65.0, 0.95, 0.5, 20.0, 80.0, 40.0, 200.0, 1800.0, 250.0
+VF, SF, CY, PCY, PF, GA, WAKE, SELF, GAP = 45.0, 65.0, 0.95, 0.5, 20.0, 1.5, 90.0, 60.0, 150.0
+HOP, LAT, GBW, CALL = 2000.0, 1800.0, 250.0, 900.0
 FIRST = 1e6
-URGE = {
-    0: {"cc": 600, "cl": 1000, "dd": 1200, "di": -9900, "do": 500, "jl": 3800, "jt": 200, "mj": 1400, "ps": 1400, "psc": -3400, "pv": 900,
-        "sg": 1000, "t": 300, "te": 600, "ti": 100, "to": 1000, "tt": 8900, "vb": -1800, "vi": -14900, "vo": 1700},
-    1: {"dd": 800, "ti": 12400, "mj": 1000, "vi": -5400, "psc": 17000, "te": -200, "t": 700, "jl": -3500, "cl": 3600, "pv": 300, "di": -9700,
-        "ps": 200, "to": 300, "tt": 6600, "sg": 200, "jt": -2400, "vb": 300, "do": 500, "vo": 200},
-    None: {"LTa": -3800, "out": -1500, "ax": -6000, "ipf": 2800, "b8a": -3500, "pad": -1900, "w": -5300, "ohr": 600, "y1l": 22900, "am": -3600,
-           "stu": -1000, "ipi": 15600, "jmf": 5000, "ej": -800, "sti": -6200, "hi": -5000, "ones": -3000, "yo": -26700, "yi": -10000, "yim": -3300,
-           "ID": -21000, "io": 10800, "y0l": 7600, "b": -16500, "ipj": -24300, "LTR": 2100, "jmi": 5800, "RM": 15700, "yiu": -11200, "ls": -8100,
-           "SM": 900, "ohn": -4900, "LTb": -11800, "y1m": 4200, "lt": 9700, "AM": -6200, "ohy": -100, "J": -6200, "I": -1800, "C": -7300, "oh": 300, "es": 600},
-}
+OPT = {"ohv": (8,), "signv": (), "cgv": (), "dupv": 2, "permv": 11, "pace": 5}
+URGE = {}
 
 
 def program(R, T, topo):
     ops = []
-    cur = [None]
+    tag = [None]
     me = T.cores[R]
 
     def B(name, a, z, step=1):
-        buf, at = PLACE[name]
-        return T[buf][:, at + a:at + z:step] if step > 1 else T[buf][:, at + a:at + z]
+        return T[name][:, a:z:step] if step > 1 else T[name][:, a:z]
 
-    def add(q, dur, reads, writes, calls, sem=None, lat=0.0, tail=0.0, dma=False, bonus=0.0):
-        ops.append({"q": q, "dur": dur, "r": list(reads), "w": list(writes), "calls": calls, "sem": sem, "lat": lat, "tail": tail, "dma": dma, "bonus": bonus, "ch": cur[0]})
+    def add(q, dur, reads, writes, calls, sem=None, lat=0.0, tail=0.0, dma=False, bonus=0.0, name=""):
+        ops.append({"q": q, "dur": dur, "r": list(reads), "w": list(writes), "calls": calls, "sem": sem, "lat": lat, "tail": tail, "dma": dma, "bonus": bonus,
+                    "tag": (name, tag[0])})
         return len(ops) - 1
 
-    def V(cyc, reads, writes, name, *a):
+    def V(name, cyc, reads, writes, kind, *a):
         call = {"copy": lambda g: g.vector.tensor_copy(*a), "tt": lambda g: g.vector.tensor_tensor(*a),
-                "ts": lambda g: g.vector.tensor_scalar(*a), "set": lambda g: g.vector.memset(*a)}[name]
-        add("v", VF + CY * max(64, cyc), reads, writes, [call])
+                "ts": lambda g: g.vector.tensor_scalar(*a), "set": lambda g: g.vector.memset(*a)}[kind]
+        add("v", VF + CY * max(32, cyc), reads, writes, [call], name=name)
 
-    def S(cyc, reads, writes, *a, **kw):
-        add("s", SF + CY * max(64, cyc), reads, writes, [lambda g: g.scalar.activation(*a, **kw)])
+    def S(name, cyc, reads, writes, *a, **kw):
+        add("s", SF + CY * max(64, cyc), reads, writes, [lambda g: g.scalar.activation(*a, **kw)], name=name)
 
-    def P(reads, writes, mms):
+    def P(name, reads, writes, mms):
         cost = PF
         for m in mms:
             cost += PCY * max(64, m[5])
-        add("pe", cost, reads, writes, [(lambda g, m=m: g.tensor.matmul(m[0], m[1], m[2], m[3], m[4])) for m in mms])
+        add("pe", cost, reads, writes, [(lambda g, m=m: g.tensor.matmul(m[0], m[1], m[2], m[3], m[4])) for m in mms], name=name)
+
+    def G(key, el, reads, call):
+        add("g", 170 + 1.9 * el, reads, [key], [call], sem="kg", name="const")
 
     def pick(key, out, in_, pat, cmp_, base, cm, el, src):
-        add("g", 170 + 1.9 * el, [src], [key], [lambda g: g.affine_select(out, in_, pat, cmp_, 0.0, base, cm)], sem="kg")
+        G(key, el, [src], lambda g: g.affine_select(out, in_, pat, cmp_, 0.0, base, cm))
 
-    def D(sem, nbytes, reads, writes, out, in_, bonus=0.0):
-        add("sync", 100.0, reads, writes, [lambda g: g.sync.dma_start(out, in_)], sem=sem, lat=1800.0, tail=nbytes / GBW, dma=True, bonus=bonus)
+    def DM(sem, nbytes, reads, writes, out, in_, bonus=0.0):
+        add("sync", 70.0, reads, writes, [lambda g: g.sync.dma_start(out, in_)], sem=sem, lat=LAT, tail=nbytes / GBW, dma=True, bonus=bonus, name=sem)
 
-    def send(dst, sem, nbytes, reads, landing, out, in_, bonus=0.0):
-        core = T.cores[dst % N]
-        rid, pid, _ = topo.addr(core)
-        mk = topo.mask(me, core)
-        k = add("g", 600.0, reads, [], [lambda g: g.remote_dma(out, in_, T.sem[sem], T.sem.ls, pid, rid, mk)], sem="remote", bonus=bonus)
-        j = add("net", 0.0, [], [landing], [], sem=sem, lat=HOP, tail=nbytes / GBW)
+    def send(aheads, sem, nbytes, reads, landing, src, dst, bonus=0.0):
+        far = [x for x in aheads if topo.die(T.cores[(R + x) % N]) != topo.die(me)]
+        near = [x for x in aheads if x not in far]
+        turn = []
+        while far or near:
+            turn += far[:1] + near[:1]
+            far, near = far[1:], near[1:]
+        ways = 1
+        while ways < len(aheads):
+            ways *= 2
+        trs, per = [], 0
+        for i, x in enumerate(turn):
+            core = T.cores[(R + x) % N]
+            rid, pid, _ = topo.addr(core)
+            eng = topo.engines(me, core)[i::ways]
+            per = len(eng)
+            trs.append(RemoteDMATransfer(dst_ids=[DstId(rid=rid, pnc=pid)], dma_engine_mask=sum(1 << e for e in eng), remote_sem=T.sem[sem], src=src(x), dst=dst(x)))
+        k = add("g", CALL, reads, [], [lambda g: g.remote_dma_fused(trs, local_sem=T.sem.ls)], sem="remote", bonus=bonus, name=sem)
+        j = add("net", 0.0, [], [landing], [], sem=sem, lat=HOP, tail=nbytes * len(aheads) / GBW, name=sem)
         ops[j]["after"] = k
-        ops[k]["cnt"] = ops[j]["cnt"] = len(topo.engines(me, core))
+        ops[k]["cnt"] = ops[j]["cnt"] = per * len(aheads)
 
-    for c in range(NCH):
-        D("ly", 16384 // NCH, [], [("y0l", c)], B("y0l", K * c, K * c + K), T.y0[:, n * c:n * c + n], bonus=9 * FIRST)
-    ltk = [("lt0", (R - x) % N, c) for x in range(N) for c in range(NCH)]
-    per = -(-len(ltk) // (JB - 1))
-    for b in range(JB):
-        D("ljm%d" % b, 128 * JBW * 4, [], [("jmi", b)], T.jmi[:, JBW * b:JBW * b + JBW], T.jm[:, JBW * b:JBW * b + JBW], bonus=FIRST * (8.5 - b))
-        for _, s, c in ltk[per * b:per * b + per]:
-            D("llt", 16384 // NCH, [], [("lt0", s, c)], B("lt0", 64 * s + K * c, 64 * s + K * c + K), T.lt[:, NK * s + n * c:NK * s + n * c + n], bonus=FIRST * (8.0 - b))
-        if b == 0:
-            D("lst", 65536, [], ["sti"], T.sti[:], T.st[:], bonus=8 * FIRST)
-    D("lcf", 128 * W * 2, [], [("C", 0)], T.CW[:, 0:W], T.cf[:], bonus=2 * FIRST)
-    yk = [("y0l", c) for c in range(NCH)]
-    V(1024, [], ["ones"], "set", T.ones[:], 1.0)
-    V(1024, [], ["SM0"], "set", T.SM[:], 0.0)
-    for e in range(NT):
-        V(32, [], [("pad", e)], "set", T.CW[:, CWID * e + W:CWID * e + CWID], 0.0)
-    add("g", 1200.0, [], ["io5"], [lambda g: g.iota(T.io5[:], [[1, 576]], 0, 0, allow_small_or_imprecise_dtypes=True)], sem="kg")
-    add("g", 130.0, [], ["ipi"], [lambda g: g.iota(T.ipi[:], [[0, 2]], 0, 1)], sem="kg")
-    V(2, ["ipi"], ["ipj"], "ts", T.ipj[:], T.ipi[:], 15, None, ALU.bitwise_and)
-    V(2, ["ipj"], ["ipf"], "copy", T.ipf[:], T.ipj[:])
-    pick("RM", T.RM[:], T.ones[:], [[-1, 16], [-16, 8], [0, 16]], ALU.is_equal, 0, 1, 2048, "ones")
+    def runs(lo, hi, first):
+        out, i = [], lo
+        while i < hi:
+            at = (first + i) % N
+            z = min(hi, i + N - at)
+            out.append((i, z, at))
+            i = z
+        return out
+
+    ALL = list(range(1, N))
+    xl, xs, xy = [], [], []
+    for i0, i1, g0 in runs(0, N, R):
+        g1 = g0 + i1 - i0
+        for u0, u1, s0 in runs(0, N, R):
+            xl.append(("xl", i0, u0))
+            DM("xl", 2048 * (i1 - i0) * (u1 - u0), [], [xl[-1]], T.ZL[7 + i0:7 + i1, 16 * u0:16 * u1, :], T.lt[g0:g1, NK * s0:NK * (s0 + u1 - u0)], bonus=9 * FIRST)
+        xy.append(("xy", i0))
+        DM("xy", 2048 * (i1 - i0), [], [xy[-1]], T.ZY[7 + i0:7 + i1], T.y0[g0:g1, :], bonus=9 * FIRST)
+        xs.append(("xs", i0))
+        DM("xs", 8192 * (i1 - i0), [], [xs[-1]], T.ZS[7 + i0:7 + i1], T.st[16 * g0:16 * g1, :], bonus=8.5 * FIRST)
+    send(ALL, "rl", 16384, xl, "rl", lambda x: T.ZL[7 + x], lambda x: T.ZL[7 - x], bonus=9 * FIRST)
+    send(ALL, "ry", 2048, xy, "ry", lambda x: T.ZY[7 + x], lambda x: T.ZY[7 - x], bonus=8.5 * FIRST)
+    send(ALL, "rs", 8192, xs, "rs", lambda x: T.ZS[7 + x], lambda x: T.ZS[7 - x], bonus=8 * FIRST)
+    ltk = [("LT", u) for u in range(8)]
+    yk = [("LT", 8)]
+    for u in range(8):
+        DM("ll", 16384, xl + ["rl"], [("LT", u)], B("LT", 64 * u, 64 * u + 64), T.ZL[0:8, 16 * u:16 * u + 16, :], bonus=8 * FIRST)
+    DM("ly", 16384, xy + ["ry"], yk, B("LT", 512, 576), T.ZY[0:8], bonus=8 * FIRST)
+    DM("lst", 65536, xs + ["rs"], ["sti"], T.sti[:], T.ZS[0:8], bonus=7 * FIRST)
+    jorder = [x for c in CALLS["J"] for x in c] + [0]
+    for i, x in enumerate(jorder):
+        g0, a, z = (R + x) % N, BW * x, BW * x + BW
+        DM("lj%d" % x, 128 * BW * 4, [], [("jmi", x)], B("jmi", a, z), T.jm[16 * g0:16 * g0 + 16, :], bonus=FIRST * (8 - 0.1 * i))
+        V("jmf", BW, [("jmi", x)], [("jmf", x)], "copy", B("jmf", a, z), B("jmi", a, z))
+        ops[-1]["bonus"] = FIRST
+        S("JS", BW, [("jmf", x)], [("JS", x)], B("JS", a, z), B("jmf", a, z), AF.Exp, bias=float(-LOW * SC), scale=float(SC))
+        ops[-1]["bonus"] = FIRST
+    jk = ["jo"]
+    for k, c in enumerate(CALLS["J"]):
+        send(c, "rj%d" % k, 128 * BW * 2, [("JS", x) for x in c], "rj%d" % k, lambda x: B("JS", BW * x, BW * x + BW), lambda x: T.ZJ[7 - x], bonus=7 * FIRST)
+        p0, p1 = 7 - max(c), 8 - min(c)
+        DM("jr%d" % k, 128 * BW * 2 * len(c), ["rj%d" % k], ["jr%d" % k], T.JW[16 * p0:16 * p1, 0:W], T.ZJ[p0:p1], bonus=7 * FIRST)
+        jk.append("jr%d" % k)
+    DM("jo", 128 * BW * 2, [("JS", 0)], ["jo"], T.JW[112:128, 0:W], B("JS", 0, BW), bonus=7 * FIRST)
+    ck = ["co", "cz"]
+    pace = [("JS", jorder[OPT["pace"]])]
+    for k, c in enumerate(CALLS["C"]):
+        xk = []
+        for i0, i1, g0 in runs(min(c), max(c) + 1, R):
+            xk.append(("xc", i0))
+            DM("xc%d" % k, 128 * BW * 2 * (i1 - i0), pace, [xk[-1]], T.XC[i0:i1], T.cf[16 * g0:16 * (g0 + i1 - i0), :], bonus=3 * FIRST)
+        send(c, "rc%d" % k, 128 * BW * 2, xk, "rc%d" % k, lambda x: T.XC[x], lambda x: T.ZC[7 - x], bonus=3 * FIRST)
+        p0, p1 = 7 - max(c), 8 - min(c)
+        DM("cr%d" % k, 128 * BW * 2 * len(c), ["rc%d" % k], ["cr%d" % k], T.CW[16 * p0 + 16:16 * p1 + 16, 0:W], T.ZC[p0:p1], bonus=3 * FIRST)
+        ck.append("cr%d" % k)
+    DM("co", 128 * BW * 2, pace, ["co"], T.CW[0:16, 0:W], T.cf[16 * R:16 * R + 16, :], bonus=2 * FIRST)
+    V("c", 128, [], ["ones"], "set", T.ones[:], 1.0)
+    V("c", 128, [], ["Z10"], "set", T.Z1[:], 0.0)
+    V("c", (D - W) // 2, [], ["jz"], "set", B("JW", W, D), 0.0)
+    for i in range(4):
+        V("c", D // 8, [], [("cz", i)], "set", B("CW", W + D // 4 * i, W + D // 4 * (i + 1)), 0.0)
+    ck = [x for x in ck if x != "cz"] + [("cz", i) for i in range(4)]
+    for c in range(2):
+        V("c", 32, [], [("A0", c, 0)], "set", B("A0%d" % c, 0, K), 16.0)
+        V("c", 32, [], [("nf0", c)], "set", B("nf%d" % c, 0, K), float(F))
+    V("c", 32, [], [("A1", 0, 0), ("A1", 1, 0)], "set", B("A1", 0, 64), 16.0)
+    G("ipi", 2, [], lambda g: g.iota(T.ipi[:], [[0, 2]], 0, 1))
+    G("io32", 32, [], lambda g: g.iota(T.io32[:], [[1, 32]], 0, 0, allow_small_or_imprecise_dtypes=True))
+    V("c", 2, ["ipi"], ["ipj"], "ts", T.ipj[:], T.ipi[:], 15, None, ALU.bitwise_and)
+    V("c", 2, ["ipj"], ["ipf"], "copy", T.ipf[:], T.ipj[:])
+    row = T.ipf[:, 0:1]
+    V("c", 32, ["io32", "ipf"], ["IDT"], "ts", T.IDT[:], T.io32[:], row, None, ALU.is_equal)
+    V("c", 32, ["io32"], ["K16"], "ts", T.K16[:], T.io32[:], 16.0, None, ALU.mult)
+    pick("Z2", T.Z2[:], T.ones[:], [[0, 2], [-1, 128]], ALU.is_equal, 0, 1, 256, "ones")
     pick("b8a", T.b8a[:], T.ones[:, 0:8], [[-16, 8]], ALU.is_ge, 0, 1, 8, "ones")
     pick("b8", T.b8[:], T.b8a[:], [[16, 8]], ALU.is_ge, 15, -1, 8, "b8a")
-    pick("ID", T.ID[:], T.ones[:, 0:128], [[-1, 128]], ALU.is_equal, 0, 1, 128, "ones")
-    V(128, ["ID"], ["I4"], "ts", T.I4[:], T.ID[:], 18.0 * HIT / STOP, None, ALU.mult)
-    V(128, ["ID"], ["I8"], "ts", T.I8[:], T.ID[:], -36.0 * HIT / STOP, None, ALU.mult)
-    smk = [("SM", r) for r in range(16)]
+    V("c", 8, ["b8", "Z10"], ["Z1a"], "copy", B("Z1", 0, 128, 16), T.b8[:])
+    V("c", 8, ["b8", "Z10"], ["Z1b"], "copy", B("Z1", 128, 256, 16), T.b8[:])
+    z1 = ["Z1a", "Z1b"]
+    V("c", 128, z1 + ["ipf"], ["Z1x"], "ts", T.Z1x[:], T.Z1[:], row, None, ALU.mult)
+    pick("BDa", T.BDa[:], T.ones[:, 0:128], [[-16, 8], [0, 16]], ALU.is_ge, 0, 1, 128, "ones")
+    pick("BD", T.BD[:], T.BDa[:], [[16, 8], [0, 16]], ALU.is_ge, 15, -1, 128, "BDa")
+    pick("LTR", T.LTR[:], T.BD[:], [[1, 128]], ALU.is_gt, 0, -1, 128, "BD")
+    rmk = [("RM", r) for r in range(16)]
     for r in range(16):
-        V(8, ["b8", "SM0"], [("SM", r)], "ts", T.SM[:, 129 * r:128 * r + 128:16], T.b8[:], HIT, None, ALU.mult)
-    pick("LTa", T.LTa[:], T.ones[:, 0:128], [[-16, 8], [0, 16]], ALU.is_ge, 0, 1, 128, "ones")
-    pick("LTb", T.LTb[:], T.LTa[:], [[16, 8], [0, 16]], ALU.is_ge, 15, -1, 128, "LTa")
-    pick("LTR", T.LTR[:], T.LTb[:], [[1, 128]], ALU.is_gt, 0, -1, 128, "LTb")
-    for bi, be in enumerate((8, 4, 2, 1)):
-        for m, (step, base) in enumerate(((1000, 0), (-1000, 1000), (1000, -be), (-1000, 1000 - be))):
-            j = 4 * bi + m
-            pick(("AM", j), T.AM[:, 128 * j:128 * j + 128], T.ones[:, 0:128], [[-2 * be, 64 // be], [step, 2], [-1, be]], ALU.is_equal, base, 1, 128, "ones")
-    ik = [("I", b) for b in range(8)]
-    for b in range(8):
-        S(576, ["io5"], [("I", b)], T.JW[:, 576 * b:576 * b + 576], T.io5[:], AF.Exp, bias=float(576 * b * SC), scale=float(SC))
-    jk = {0: [("J", 0, b) for b in range(JB)]}
-    lk = {0: ltk}
-    for b in range(JB):
-        a, z = JBW * b, JBW * b + JBW
-        V(JBW, [("jmi", b)], [("jmf", b)], "copy", T.jmf[:, a:z], T.jmi[:, a:z])
-        S(JBW, [("jmf", b)], [("J", 0, b)], T.JW[:, W + a:W + z], T.jmf[:, a:z], AF.Exp, scale=float(SC))
-    for e in range(1, NT):
-        jk[e] = jk[e - 1] + [("J", e)]
-        lk[e] = [("lt", e)]
-        send(R - e, "rl%d" % e, 131072, ltk, ("lt", e), B("lt%d" % e, 0, 512), T.lt0[:], bonus=FIRST)
-    for e in range(1, NT):
-        pace = [("J", e - 1), ("C", e - 1)] if e > 1 else []
-        send(R - e, "rj%d" % e, 128 * W * 2, jk[0] + pace, ("J", e), T.JW[:, W * (1 + e):W * (2 + e)], T.JW[:, W:2 * W], bonus=FIRST if e == 1 else 0.0)
-        send(R - e, "rc%d" % e, 128 * W * 2, [("C", 0)] + pace, ("C", e), T.CW[:, CWID * e:CWID * e + W], T.CW[:, 0:W])
-    wn = [0]
+        V("c", 64, ["BD", "IDT"], [("RM", r)], "ts", B("RM", 128 * r, 128 * r + 128), T.BD[:], T.IDT[:, r:r + 1], None, ALU.mult)
+    for i, be in enumerate((8, 4, 2, 1)):
+        V("c", 256, ["Z2"], [("rta", i)], "tt", B("rta", 128 * i, 128 * i + 128), B("Z2", 128 - be, 256 - be), B("Z2", 16 - be, 144 - be), ALU.add)
+        V("c", 256, [("rta", i), "BD"], [("ROT", i)], "tt", B("ROT", 128 * i, 128 * i + 128), B("rta", 128 * i, 128 * i + 128), T.BD[:], ALU.mult)
+    V("c", 64, ["Z2"], ["I64"], "ts", T.I64[:], B("Z2", 0, 128), 64.0, None, ALU.mult)
+    V("c", 64, ["Z2"], ["I32"], "ts", T.I32[:], B("Z2", 0, 128), 32.0, None, ALU.mult)
 
-    def wbank():
-        wn[0] += 1
-        return "w%d" % (wn[0] % NCH)
+    def sel(r, a, name="Z1"):
+        o = -(16 * a + r) % 128
+        return B(name, o, o + 128)
 
-    def smat(r):
-        return T.SM[:, 128 * r:128 * r + 128]
+    def sh(a):
+        o = -16 * a % 128
+        return B("Z2", o, o + 128)
 
-    def rep(src, natural, reads):
-        wb = wbank()
-        P(["RM"] + reads, [wb], [(B(wb, K * r, K * r + K) if natural else B(wb, r, n, 16), T.RM[:, 128 * r:128 * r + 128], src, True, True, K) for r in range(16)])
-        return wb
-
-    def onehot(out, key, src, natural, reads):
-        wb = rep(src, natural, reads)
-        V(n, ["ipf"], [wb, key], "ts", out, B(wb, 0, n), 15.0, T.ipf[:, 0:1], ALU.min, ALU.is_equal)
-
-    def oh_of(off, e, c):
-        a = NK * OHS.index((off, e)) + n * c
-        return T.oh[:, a:a + n], ("oh", off, e, c)
-
-    def slot_letters(off, e):
-        s = (R - off) % N
-        return B("lt%d" % e, 64 * s, 64 * s + 64)
-
-    def onehots(off, e):
-        s = 64 * ((R - off) % N)
-        for c in range(NCH):
-            out, key = oh_of(off, e, c)
-            onehot(out, key, B("lt%d" % e, s + K * c, s + K * c + K), False, lk[e])
-
-    def gates(w, i, x, e, src, reads):
-        es, ej = "es%d%d" % (w, i), "ej%d%d" % (w, i)
-        a = 64 * x
-        big = W * (1 + e) / A
-        V(32, reads, [(es, x)], "ts", B(es, a, a + 64), src, 15.5, STOP, ALU.is_gt, ALU.mult)
-        S(64, [(es, x)], [(ej, x)], B(ej, a, a + 64), B(es, a, a + 64), AF.Copy, bias=float(big), scale=float(-big / STOP))
-
-    for c in range(NCH):
-        onehot(B("ohn", n * c, n * c + n), ("ohn", c), B("y0l", K * c, K * c + K), True, yk)
-    V(128, ["sti"], ["stu"], "copy", T.stu[:], T.sti[:])
-
-    def image(c, lst, lkey, lo, hi, oh, ohk, tk, natural, out, okey):
-        mj, ps = "mj%d" % c, "ps%d" % c
-        V(1.5 * n, [lkey, ohk] + tk, [mj], "tt", B(mj, 0, n), T.JW[:, lo:hi].indirect(lst), oh, ALU.mult)
-        P(smk + [mj], [ps], [(B(ps, 0, K), smat(r), B(mj, K * r, K * r + K) if natural else B(mj, r, n, 16), r == 0, r == 15, K) for r in range(16)])
-        S(K, [], [ps, okey], out, B(ps, 0, K), AF.Ln, scale=float(1.0 / HIT))
-
-    def jlist(c, t, tkey, w, i, x):
-        ej, jl, ta = "ej%d%d" % (w, i), "jl%d" % c, B("ta%d" % c, 0, K)
-        a = 64 * x + K * c
-        V(K, [tkey, (ej, x)], [("jt", c)], "tt", ta, t, B(ej, a, a + K), ALU.add)
-        V(K, [("jt", c)], [jl], "ts", B(jl, 0, K), ta, float(A), None, ALU.mult)
-
-    def gate(c, t, tkey, w, i, x):
-        es = "es%d%d" % (w, i)
-        a = 64 * x + K * c
-        te = B("ta%d" % c, K, 2 * K)
-        V(2 * K, [tkey, (es, x)], [("te", c)], "tt", te, t, B(es, a, a + K), ALU.max)
-        return te, ("te", c)
-
-    def clist(c, te, tek, stop, skeys, touched):
-        t2, cl = B("ta%d" % c, 2 * K, 3 * K), "cl%d" % c
-        V(2 * K, [tek] + skeys, touched + [("t2", c)], "tt", t2, te, stop, ALU.max)
-        V(K, [("t2", c)], [cl], "ts", B(cl, 0, K), t2, float(A), float(A * STOP), ALU.mult, ALU.min)
-
-    def coefs(c, e, out, okey):
-        cl = "cl%d" % c
-        for q in range(NH):
-            S(1.5 * h, [cl, ("C", e), ("pad", e)], [(okey, q)], B(out, h * q, h * q + h),
-              T.CW[:, CWID * e:CWID * e + CWID].indirect(B(cl, K // NH * q, K // NH * (q + 1))), AF.Copy)
-
-    state = [{} for _ in range(NCH)]
-
-    def enter(w, i, off, c, dd):
-        st = state[c]
-        cur[0] = c
-        if i == 0:
-            oh = ("ohn", "ohy")[w]
-            tt, cl, vb = "tt%d" % c, "cl%d" % c, "vb%d" % c
-            image(c, B("stu", 64 * w + K * c, 64 * w + K * c + K), "stu", W, 2 * W, B(oh, n * c, n * c + n), (oh, c), jk[0], True, B(tt, 0, K), tt)
-            V(K, [tt], [cl], "ts", B(cl, 0, K), B(tt, 0, K), float(A), None, ALU.mult)
-            coefs(c, 0, vb, vb)
-            st["t"], st["tk"] = B(tt, 0, K), tt
-            st["v"], st["vk"] = vb, [(vb, q) for q in range(NH)]
-            st["dead"] = None
+    V("ltf", 576, ltk + yk, ["LTf"], "copy", T.LTf[:], T.LT[:])
+    V("ltf", 576, ["LTf"], ["LTu"], "copy", T.LTu[:], T.LTf[:])
+    V("stu", 128, ["sti"], ["stu"], "copy", T.stu[:], T.sti[:])
+    for d in range(9):
+        u = 8 if d == 8 else -d % N
+        src, out = T.IDT[:].indirect(B("LTu", 64 * u, 64 * u + 64)), B("OH", NK * d, NK * d + NK)
+        if d in OPT["ohv"]:
+            V("oh", GA * NK, ["LTu", "IDT"], [("OH", d)], "copy", out, src)
         else:
-            vi, ti, di = "vi%d%d%d" % (w, i - 1, c), "ti%d%d%d" % (w, i - 1, c), "di%d%d" % (w, i - 1)
-            st["t"], st["tk"] = B(ti, 0, K), ti
-            st["v"], st["vk"] = vi, [vi]
-            st["dead"] = (B(di, K * c, K * c + K), (di, c))
-            S(K, [(di, c)], [(dd, 0, c)], B(dd, K * c, K * c + K), B(di, K * c, K * c + K), AF.Copy)
-
-    def lookup(w, i, off, m, c, slots, k):
-        st = state[c]
-        cur[0] = c
-        e, x = slots[k]
-        jl = "jl%d" % c
-        jlist(c, st["t"], st["tk"], w, i, x)
-        if w == 1 and i == 0 and k == 0:
-            oh, ohk = B("ohr", n * c, n * c + n), ("ohr", c)
+            S("oh", GA * NK, ["LTu", "IDT"], [("OH", d)], out, src, AF.Copy)
+    for c in range(2):
+        pw = "pw%d" % c
+        P("ohn", rmk + yk, [pw], [(B(pw, 64 * r, 64 * r + 64), B("RM", 128 * (8 * c + r), 128 * (8 * c + r + 1)), B("LT", 512, 576), True, True, 64) for r in range(8)])
+        V("ohn", n, ["ipf"], [pw, ("ohn", c)], "ts", B("ohn", n * c, n * c + n), B(pw, 0, n), row, None, ALU.is_equal)
+    dupk = ["jz"]
+    for i in range(8):
+        a, z = BW * i, BW * i + BW
+        dupk.append(("dup", i))
+        if i < OPT["dupv"]:
+            V("dup", BW // 2, jk, [("dup", i)], "copy", B("JW", D + a, D + z), B("JW", a, z))
         else:
-            oh, ohk = oh_of(off, e, c)
-        hop = k + 1 == len(slots) and i + 1 < len(ST[w])
-        tb = ("to%d%d%d" % (w, i, c)) if hop else ("tt%d" % c)
-        image(c, B(jl, 0, K), jl, 0, W * (2 + e), oh, ohk, ik + jk[e], False, B(tb, 0, K), tb)
-        st["t"], st["tk"] = B(tb, 0, K), tb
-        if hop:
-            ti = "ti%d%d%d" % (w, i, c)
-            send(R + m, "rt%d%d%d" % (w, i, c), 128 * K * 4, [tb], ti, B(ti, 0, K), B(tb, 0, K))
-        st["te"] = gate(c, st["t"], st["tk"], w, i, x)
+            S("dup", BW, jk, [("dup", i)], B("JW", D + a, D + z), B("JW", a, z), AF.Copy)
+    S("G1", GA * NK, jk + ["stu"], ["G1"], T.G1[:], B("JW", 0, W).indirect(B("stu", 64, 128)), AF.Copy)
 
-    def station(w, i, off, m):
-        slots = [(e, e + (1 if w == 1 and i == 0 else 0)) for e in range(m)]
-        if w == 1 and i == 0:
-            slots = [(0, 0)] + slots
-        final = i + 1 == len(ST[w])
-        dst = R - off if final else R + m
-        dd, es = "dd%d%d" % (w, i), "es%d%d" % (w, i)
-        do, di = "do%d%d" % (w, i), "di%d%d" % (w, i)
-        for c in range(NCH):
-            enter(w, i, off, c, dd)
-        for c in range(NCH):
-            lookup(w, i, off, m, c, slots, 0)
-        for k, (e, x) in enumerate(slots):
-            first, last = k == 0, k + 1 == len(slots)
-            nat = last and final
-            for c in range(NCH):
-                st = state[c]
-                cur[0] = c
-                cl, cc, sg, ps, vo, vi = "cl%d" % c, "cc%d" % c, "sg%d" % c, "ps%d" % c, "vo%d%d%d" % (w, i, c), "vi%d%d%d" % (w, i, c)
-                pv = ["pv%d%d" % (q, c) for q in range(NH)]
-                te, tek = st["te"]
-                if first and st["dead"] is None:
-                    V(K, [tek], [cl], "ts", B(cl, 0, K), te, float(A), None, ALU.mult)
-                elif first:
-                    clist(c, te, tek, st["dead"][0], [st["dead"][1]], [])
-                v, vk = st["v"], st["vk"]
-                if not nat:
-                    for q in range(NH):
-                        P(["ID"] + vk, [pv[q]], [(B(pv[q], 0, h), T.ID[:], B(v, h * q, h * q + h), True, False, h)])
-                coefs(c, e, cc, cc)
-                for q in range(NH):
-                    if not nat:
-                        P(["ID", (cc, q)], [pv[q]], [(B(pv[q], 0, h), T.ID[:], B(cc, h * q, h * q + h), False, True, h)])
-                    else:
-                        mm = []
-                        for r in range(16 // NH * q, 16 // NH * (q + 1)):
-                            o = B(pv[q], K * r - h * q, K * r - h * q + K)
-                            mm.append((o, T.ID[:], B(v, r, n, 16), True, False, K))
-                            mm.append((o, T.ID[:], B(cc, r, n, 16), False, True, K))
-                        P(["ID"] + [(cc, y) for y in range(NH)] + vk, [pv[q]], mm)
-                vd = vo if last else "vb%d" % c
-                for q in range(NH):
-                    S(h, [], [pv[q], (sg, q)], B(sg, h * q, h * q + h), B(pv[q], 0, h), AF.Sign, bias=0.5)
-                for q in range(NH):
-                    V(h, [], [pv[q], (vd, q)], "ts", B(vd, h * q, h * q + h), B(pv[q], 0, h), 255.0, -255.0, ALU.min, ALU.max)
-                st["v"], st["vk"] = vd, [(vd, q) for q in range(NH)]
-                if last:
-                    send(dst, "rv%d%d%d" % (w, i, c), 128 * n * 2, st["vk"], vi, B(vi, 0, n), B(vo, 0, n))
-                else:
-                    lookup(w, i, off, m, c, slots, k + 1)
-                ea = 64 * x + K * c
-                pk = ["I4", (es, x)]
-                cnt = B(ps, K, 2 * K)
-                mm = [(cnt, T.I4[:], B(es, ea, ea + K), True, False, K)]
-                if st["dead"] is not None:
-                    mm.append((cnt, T.I8[:], st["dead"][0], False, False, K))
-                    pk += ["I8", st["dead"][1]]
-                for r in range(16):
-                    mm.append((cnt, smat(r), B(sg, K * r, K * r + K) if nat else B(sg, r, n, 16), False, r == 15, K))
-                P(smk + pk + [(sg, q) for q in range(NH)], [ps], mm)
-                a, z = 64 * (x + 1) + K * c, K * c
-                if not last:
-                    te, tek = st["te"]
-                    clist(c, te, tek, cnt, [], [ps])
-                    V(K, [], [ps, (dd, x + 1, c)], "ts", B(dd, a, a + K), cnt, -HIT, STOP, ALU.is_gt, ALU.mult)
-                    st["dead"] = (B(dd, a, a + K), (dd, x + 1, c))
-                else:
-                    V(K, [], [ps, (do, c)], "ts", B(do, z, z + K), cnt, -HIT, STOP, ALU.is_gt, ALU.mult)
-                    send(dst, "rd%d%d%d" % (w, i, c), 128 * K * 2, [(do, c)], (di, c), B(di, z, z + K), B(do, z, z + K))
-                    S(K, [(do, c)], [(dd, x + 1, c)], B(dd, a, a + K), B(do, z, z + K), AF.Copy)
-        cur[0] = None
-        settle(w, i, off, dd, slots)
+    def gates(w, c):
+        Tn = len(OFF[w]) - 1
+        lh, e, h = ("LHa", "LHb")[w] + str(c), ("ea", "eb")[w] + str(c), ("ha", "hc")[w] + str(c)
+        nf, xh, pw = "nf%d" % c, "xh%d" % c, "pw%d" % c
+        lk = [(lh, 0), (lh, 1)] if w else [lh]
+        V("e", Tn * K // 2, lk, [e], "ts", B(e, 0, Tn * K), B(lh, 0, Tn * K), 15.5, None, ALU.is_gt)
+        V("nf", Tn * K // 2, lk, [nf], "ts", B(nf, K, Tn * K), B(lh, 0, Tn * K - K), 15.5, float(F), ALU.is_lt, ALU.mult)
+        V("xh", Tn * K, [e, nf, ("nf0", c)], [xh], "tt", B(xh, 0, Tn * K), B(e, 0, Tn * K), B(nf, 0, Tn * K), ALU.mult)
+        mm = []
+        for t in range(1, Tn + 1):
+            a = K * (t - 1)
+            mm.append((B(pw, a, a + K), sh(OFF[w][t - 1] + 1), B(xh, a, a + K), True, False, K))
+            mm.append((B(pw, a, a + K), sh(OFF[w][t - 1] + 1), B(e, a, a + K), False, True, K))
+        P("h", ["Z2", xh, e], [pw], mm)
+        S("h", Tn * K, [], [pw, h], B(h, 0, Tn * K), B(pw, 0, Tn * K), AF.Copy)
 
-    def store_yl(s, buf, a, key):
-        for c in range(NCH):
-            D("stores", 16384 // NCH, [key], [("out",)], T.yl[:, NK * s + n * c:NK * s + n * c + n], B(buf, a + K * c, a + K * c + K))
+    for c in range(2):
+        tag[0] = (0, c, 0)
+        pw = "pw%d" % c
+        P("lh", ["Z2"] + ltk, [pw], [(B(pw, K * d, K * d + K), sh(-d), B("LT", 64 * (-d % N) + K * c, 64 * (-d % N) + K * c + K), True, True, K) for d in range(8)])
+        S("lh", 8 * K, [], [pw, "LHa%d" % c], B("LHa%d" % c, 0, 8 * K), B(pw, 0, 8 * K), AF.Copy)
+        gates(0, c)
 
-    src1 = {}
+    lists = {}
 
-    def settle(w, i, off, dd, slots):
-        hi, ls = "hi%d%d" % (w, i), "ls%d%d" % (w, i)
-        for e, x in slots:
-            if w == 1 and i == 0 and x == 0:
-                continue
-            b = 64 * x
-            dk = [(dd, x + 1, c) for c in range(NCH)]
-            if i == 0 and x == 0:
-                hit, hk = B(dd, 64, 128), dk
+    def mark(w, c, t, bank, at):
+        h = ("ha", "hc")[w] + str(c)
+        V("mb", K, [h], [bank, "mb%d" % c], "tt", B("mb%d" % c, 0, K), B(bank, at, at + K), B(h, K * t, K * t + K), ALU.mult)
+
+    def decode(w, c, t, two):
+        pj, tt, li = "pj%d" % c, "tt%d" % c, "li%d" % c
+        m, a = K * (1 + two), 2 * K * (10 * w + t)
+        S("ln", m, [], [pj, tt], B(tt, 0, m), B(pj, 0, m), AF.Ln)
+        V("li", m, [tt], [(li, w, t)], "ts", B(li, a, a + m), B(tt, 0, m), float(A), float(LOW), ALU.mult, ALU.add)
+        lists[w, c, t] = (B(li, a, a + K), B(li, a + K * two, a + K * two + K), (li, w, t))
+        if t + 1 < len(OFF[w]):
+            mark(w, c, t, pj, 0)
+
+    def series(w, c, t):
+        pj, mb, o = "pj%d" % c, "mb%d" % c, OFF[w]
+        two = int(t + 1 < len(o) and o[t + 1] == o[t])
+        mm = []
+        for y in range(1 + two):
+            out = B(pj, K * y, K * y + K)
+            if t:
+                mm.append((out, sh(o[t] - o[t - 1] - y), B(mb, 0, K), True, False, K))
+            for r in range(16):
+                mm.append((out, sel(r, 1 - y), B("mj", n * c + r, n * c + n, 16), r == 0 and not t, r == 15, K))
+        P("js", z1 + ["Z2", ("mj", c)] + ([mb] if t else []), [pj], mm)
+        decode(w, c, t, two)
+
+    def image(w, c, t):
+        _, lj, key = lists[w, c, t - 1]
+        d = 8 if (w, t) == (1, 1) else OFF[w][t]
+        hi, tk = (W, jk) if t == 1 else (WID, jk + dupk)
+        V("jg", GA * n, [key, ("OH", d)] + tk, [("mj", c)], "tt", B("mj", n * c, n * c + n), B("JW", 0, hi).indirect(lj), B("OH", NK * d + n * c, NK * d + n * c + n), ALU.mult)
+        series(w, c, t)
+
+    def coefs(w, c, t):
+        lc, _, key = lists[w, c, t]
+        y = 2 if t == 0 else t % 2
+        out, src = B("cc%d" % c, n * y, n * y + n), B("CW", 0, WID).indirect(lc)
+        if (w, c, t) in OPT["cgv"]:
+            V("cg", GA * n, [key] + ck, [("cc", c, y)], "copy", out, src)
+        else:
+            S("cg", GA * n, [key] + ck, [("cc", c, y)], out, src, AF.Copy)
+
+    def akey(w, c, t):
+        return (B("A0%d" % c, K * t, K * t + K), ("A0", c, t)) if w == 0 else (B("A1", 64 * t + K * c, 64 * t + K * c + K), ("A1", c, t))
+
+    def sums(w, c, t):
+        va, pv, cc, o = ("va", "vb")[w] + str(c), "pv%d" % c, "cc%d" % c, OFF[w]
+        y = t % 2
+        mm = [(B(pv, 0, n), sh(-o[t] - 1), B(cc, n * y, n * y + n), True, False, n)]
+        if t == 1:
+            mm.append((B(pv, 0, n), sh(-1), B(cc, 2 * n, 3 * n), False, True, n))
+            rk = [("cc", c, 2)]
+        else:
+            mm.append((B(pv, 0, n), sh(0), B(va, n * (t - 2), n * (t - 1)), False, True, n))
+            rk = [(va, t - 1)]
+        P("add", ["Z2", ("cc", c, y)] + rk, [pv], mm)
+        v = B(va, n * (t - 1), n * t)
+        V("clip", n, [], [pv, (va, t)], "ts", v, B(pv, 0, n), 255.0, -255.0, ALU.min, ALU.max)
+        j = [i for i, p in enumerate(PAIRS[w]) if t in p][0]
+        pair = PAIRS[w][j]
+        sg, a = "sg%d" % c, 2 * n * (j % 2)
+        b = a + n * pair.index(t)
+        if (w, c, t) in OPT["signv"]:
+            V("sg", n // 2, [(va, t)], [(sg, j % 2, pair.index(t))], "ts", B(sg, b, b + n), v, 0.0, 0.5, ALU.is_ge, ALU.subtract)
+        else:
+            S("sg", n, [(va, t)], [(sg, j % 2, pair.index(t))], B(sg, b, b + n), v, AF.Sign, bias=0.5)
+        if t != pair[-1]:
+            return
+        e, pc, nc, m = ("ea", "eb")[w] + str(c), "pc%d" % c, "nc%d" % c, K * len(pair)
+        mm = [(B(pc, 0, m), T.I64[:], B(e, K * (pair[0] - 1), K * pair[-1]), True, False, m)]
+        for r in range(16):
+            mm.append((B(pc, 0, m), sel(r, 0), B(sg, a + r, a + n * len(pair), 16), False, r == 15, m))
+        P("cnt", z1 + ["I64", e] + [(sg, j % 2, i) for i in range(len(pair))], [pc], mm)
+        if pair == (1,):
+            V("nc", m, [], [pc, akey(w, c, 1)[1]], "ts", akey(w, c, 1)[0], B(pc, 0, m), -0.75, 16.0, ALU.is_gt, ALU.mult)
+        else:
+            V("nc", m, [], [pc, nc], "ts", B(nc, 0, m), B(pc, 0, m), -0.75, 16.0, ALU.is_gt, ALU.mult)
+            for i, x in enumerate(pair):
+                (p, pk), (q, qk) = akey(w, c, x - 1), akey(w, c, x)
+                V("al", 2 * K, [nc, pk], [qk], "tt", q, p, B(nc, K * i, K * i + K), ALU.min)
+        if t == len(o) - 2:
+            ended(w, c)
+
+    def ended(w, c):
+        Tn = len(OFF[w]) - 1
+        pc, lv = "pc%d" % c, "lv%d" % c
+        mm = [(B(pc, 64, 64 + K), sh(0), T.K16[:], True, False, K)]
+        for t in range(1, Tn):
+            mm.append((B(pc, 64, 64 + K), T.I32[:], akey(w, c, t)[0], False, t == Tn - 1, K))
+        P("pick", ["Z2", "K16", "I32"] + [akey(w, c, t)[1] for t in range(1, Tn)], [pc], mm)
+        V("lv", K, ["ipf"], [pc, (lv, w)], "ts", B(lv, K * w, K * w + K), B(pc, 64, 64 + K), row, None, ALU.add)
+
+    def final(w, c):
+        Tn = len(OFF[w]) - 1
+        va, lv, vf = ("va", "vb")[w] + str(c), "lv%d" % c, "vf%d" % c
+        S("vf", GA * n, [(lv, w)] + [(va, t) for t in range(1, Tn + 1)], [vf], B(vf, 0, n), B(va, 0, n * Tn).indirect(B(lv, K * w, K * w + K)), AF.Copy)
+
+    def walk(w, c):
+        for t in range(len(OFF[w])):
+            tag[0] = (w, c, t)
+            if t:
+                image(w, c, t)
+            coefs(w, c, t)
+            if t:
+                sums(w, c, t)
+            if t == len(OFF[w]) - 1:
+                final(w, c)
+
+    tag[0] = (0, 0, 0)
+    V("jg", GA * NK, ["stu", ("ohn", 0), ("ohn", 1)] + jk, [("mj", 0), ("mj", 1)], "tt", T.mj[:], B("JW", 0, W).indirect(B("stu", 0, 64)), T.ohn[:], ALU.mult)
+    mm = []
+    for y in range(2):
+        for r in range(16):
+            mm.append((B("pj0", 64 * y, 64 * y + 64), sel(r, 1 - y), B("mj", 64 * r, 64 * r + 64), r == 0, r == 15, 64))
+    P("js", z1 + [("mj", 0), ("mj", 1)], ["pj0"], mm)
+    S("ln", 128, [], ["pj0", "t0"], T.t0[:], B("pj0", 0, 128), AF.Ln)
+    V("li", 128, ["t0"], ["l0"], "ts", T.l0[:], T.t0[:], float(A), float(LOW), ALU.mult, ALU.add)
+    for c in range(2):
+        lists[0, c, 0] = (B("l0", K * c, K * c + K), B("l0", 64 + K * c, 64 + K * c + K), "l0")
+        mark(0, c, 0, "pj0", K * c)
+    for c in range(2):
+        walk(0, c)
+    for c in range(2):
+        tag[0] = (1, c, -1)
+        a0, lha, lhb, hit, dz = "A0%d" % c, "LHa%d" % c, "LHb%d" % c, "hit%d" % c, "dz%d" % c
+        V("hit", 16 * K, [("A0", c, t) for t in range(9)], [hit], "tt", B(hit, 0, 8 * K), B(a0, 0, 8 * K), B(a0, K, 9 * K), ALU.subtract)
+        V("lhb", 16 * K, [hit, lha], [(lhb, 1)], "tt", B(lhb, K, 9 * K), B(lha, 0, 8 * K), B(hit, 0, 8 * K), ALU.max)
+        V("dz", K, [("A0", c, 8)], [dz], "ts", B(dz, 0, K), B(a0, 8 * K, 9 * K), -1.0, 16.0, ALU.mult, ALU.add)
+        V("lhb", 2 * K, [dz] + yk, [(lhb, 0)], "tt", B(lhb, 0, K), B("LT", 512 + K * c, 512 + K * c + K), B(dz, 0, K), ALU.max)
+        gates(1, c)
+        vf, xa, eq, oy, pv, pj, pc = "vf%d" % c, "xa%d" % c, "eq%d" % c, "oy%d" % c, "pv%d" % c, "pj%d" % c, "pc%d" % c
+        P("g1", ["Z2", "G1"], [pj], [(B(pj, r, n, 16), sh(0), B("G1", 64 * r + K * c, 64 * r + K * c + K), True, True, K) for r in range(16)])
+        src, sk = B(vf, 0, n), vf
+        for i in range(4):
+            P("mx", [("ROT", i), sk], [pv], [(B(pv, 0, n), B("ROT", 128 * i, 128 * i + 128), src, True, True, n)])
+            if i < 3:
+                out = B(xa, n * (i % 2), n * (i % 2) + n)
+                V("mx", n, [sk], [pv, (xa, i % 2)], "tt", out, src, B(pv, 0, n), ALU.max)
+                src, sk = out, (xa, i % 2)
+        V("mx", n, [sk], [pv], "tt", B(pv, 0, n), src, B(pv, 0, n), ALU.max)
+        V("eq", n, [vf], [pv, eq], "tt", B(eq, 0, n), B(vf, 0, n), B(pv, 0, n), ALU.is_equal)
+        P("ltr", ["LTR", eq], [pv], [(B(pv, 0, n), T.LTR[:], B(eq, 0, n), True, True, n)])
+        V("oy", n, [eq], [pv, oy], "tt", B(oy, 0, n), B(eq, 0, n), B(pv, 0, n), ALU.is_gt)
+        V("jg", n, [oy], [pj, ("mj", c)], "tt", B("mj", n * c, n * c + n), B(oy, 0, n), B(pj, 0, n), ALU.mult)
+        tag[0] = (1, c, 0)
+        series(1, c, 0)
+        pw = "pw%d" % c
+        P("y1", ["Z1x", oy], [pw], [(B(pw, 0, K), sel(r, 0, "Z1x"), B(oy, r, n, 16), r == 0, r == 15, K) for r in range(16)])
+        S("y1", K, [], [pw, ("y1l", c)], B("y1l", K * c, K * c + K), B(pw, 0, K), AF.Copy)
+    tag[0] = (1, 1, -1)
+    P("l1", ["Z2", ("LHb0", 1), ("LHb1", 1)], ["pw1"],
+      [(B("pw1", 64 * d + K * c, 64 * d + K * c + K), sh(0), B("LHb%d" % c, K * (d + 1), K * (d + 2)), True, True, K) for d in range(8) for c in range(2)])
+    S("l1", 512, [], ["pw1", "L1"], T.L1[:], B("pw1", 0, 512), AF.Copy)
+    for c in range(2):
+        walk(1, c)
+    tag[0] = (1, 1, 10)
+    xo = {"xe": [], "xv": [], "xt": []}
+
+    def stage(sem, nbytes, reads, out, in_):
+        xo[sem].append((sem, len(xo[sem])))
+        DM(sem, nbytes, reads, [xo[sem][-1]], out, in_)
+
+    for pair in PAIRS[1]:
+        ts_ = [t for t in pair if t > 1]
+        a, z = 64 * (ts_[0] - 2), 64 * (ts_[-1] - 1)
+        ak = [("A1", c, t) for c in range(2) for t in range(ts_[0] - 1, ts_[-1] + 1)]
+        V("yl", 2 * (z - a), ak, [("hb", a)], "tt", B("hb", a, z), B("A1", a + 64, z + 64), B("A1", a + 128, z + 128), ALU.subtract)
+        V("yl", 2 * (z - a), [("hb", a), "L1"], [("YL", a)], "tt", B("YL", a, z), B("hb", a, z), B("L1", a, z), ALU.max)
+        for t in ts_:
+            d = t - 2
+            for i0, i1, p0 in runs(0, N, d):
+                out = T.ZE[p0:p0 + i1 - i0, 16 * (7 - d):16 * (8 - d), :] if d < 7 else T.ZT[p0:p0 + i1 - i0, 0:64, :]
+                stage("xe" if d < 7 else "xt", 2048 * (i1 - i0), [("YL", a)], out, T.YL[16 * i0:16 * i1, 64 * d:64 * d + 64])
+    for c in range(2):
+        a, dz, hit = K * c, "dz%d" % c, "hit%d" % c
+        V("yi", K, [("A1", c, 1)], [dz], "ts", B(dz, 0, K), akey(1, c, 1)[0], -1.0, 16.0, ALU.mult, ALU.add)
+        V("yi", 2 * K, [dz, ("LHb%d" % c, 0)], [("YI", 0, c)], "tt", B("YI", a, a + K), B("LHb%d" % c, 0, K), B(dz, 0, K), ALU.max)
+    stage("xe", 16384, [("YI", 0, 0), ("YI", 0, 1)], T.ZE[0:8, 0:16, :], B("YI", 0, 64))
+    V("yi", 64, [("A1", 0, 9), ("A1", 1, 9)], [("hit0", 1), "hit0"], "ts", B("hit0", 0, 64), B("A1", 576, 640), -1.0, 16.0, ALU.mult, ALU.add)
+    V("yi", 128, [("hit0", 1), ("y1l", 0), ("y1l", 1)], [("YI", 1)], "tt", B("YI", 64, 128), T.y1l[:], B("hit0", 0, 64), ALU.max)
+    stage("xt", 16384, [("YI", 1)], T.ZT[0:8, 64:128, :], B("YI", 64, 128))
+    vn = []
+    for c in range(2):
+        vf = "vf%d" % c
+        for r in range(16):
+            out, src = B("VN", 64 * r + K * c, 64 * r + K * c + K), B(vf, r, n, 16)
+            vn.append(("VN", c, r))
+            if r < OPT["permv"]:
+                V("vn", K, [vf], [vn[-1]], "copy", out, src)
             else:
-                V(128, dk + [(dd, x, c) for c in range(NCH)], [(hi, x)], "tt", B(hi, b, b + 64), B(dd, b + 64, b + 128), B(dd, b, b + 64), ALU.subtract)
-                hit, hk = B(hi, b, b + 64), [(hi, x)]
-            src, sk = (slot_letters(off, e), lk[e]) if w == 0 else src1[(i, e)]
-            o = B(ls, 64 * e, 64 * e + 64)
-            V(128, sk + hk, [(ls, e)], "tt", o, src, hit, ALU.max)
-            if w == 1:
-                V(32, [(ls, e)], [("yo", i, e)], "ts", o, o, 16.0, None, ALU.min)
-                if e == 0:
-                    store_yl((R - off) % N, ls, 0, ("yo", i, 0))
-                else:
-                    yr = "yr%d%d" % (i, e)
-                    send(R + e, "ry%d%d" % (i, e), 16384, [("yo", i, e)], yr, B(yr, 0, 64), o)
-                    store_yl((R - e - off) % N, yr, 0, yr)
-        if w == 0:
-            for a, b, lo, hh in MOVES:
-                if a == i:
-                    mv = "mv%d%d" % (a, b)
-                    send(R - off + ST[1][b][0], "rmv%d%d" % (a, b), 16384 * (hh - lo), [(ls, d - off) for d in range(lo, hh)], mv,
-                         B(mv, 0, 64 * (hh - lo)), B(ls, 64 * (lo - off), 64 * (hh - off)))
-
-    for i, (off, m) in enumerate(ST[0]):
-        for e in range(m):
-            gates(0, i, e, e, slot_letters(off, e), lk[e])
-    for e in range(NT):
-        for q in OHS:
-            if q[1] == e:
-                onehots(q[0], e)
-        if e == 0:
-            for c in range(NCH):
-                onehot(B("ohr", n * c, n * c + n), ("ohr", c), B("y0l", K * c, K * c + K), False, yk)
-    for i, (off, m) in enumerate(ST[0]):
-        station(0, i, off, m)
-    hv, hd = "vi0%d" % (len(ST[0]) - 1), "di0%d" % (len(ST[0]) - 1)
-    for c in range(NCH):
-        a = K * c
-        V(K, [(hd, c)], [("es10", 0)], "copy", B("es10", a, a + K), B(hd, a, a + K))
-        S(K, [(hd, c)], [("ej10", 0)], B("ej10", a, a + K), B(hd, a, a + K), AF.Copy, bias=float(W / A), scale=float(-W / A / STOP))
-    for b, (off, m) in enumerate(ST[1]):
-        for e in range(m):
-            d = off + e
-            for a, (o0, m0) in enumerate(ST[0]):
-                if o0 <= d < o0 + m0:
-                    if o0 == off:
-                        ap, key = B("ls0%d" % a, 64 * (d - o0), 64 * (d - o0) + 64), [("ls0%d" % a, d - o0)]
-                    else:
-                        lo = max(o0, off)
-                        ap, key = B("mv%d%d" % (a, b), 64 * (d - lo), 64 * (d - lo) + 64), ["mv%d%d" % (a, b)]
-            src1[(b, e)] = (ap, key)
-            gates(1, b, e + (1 if b == 0 else 0), e, ap, key)
-    for c in range(NCH):
-        vi = hv + str(c)
-        ax, am = "ax%d" % c, "am%d" % c
-        src, sk, wd, pos = vi, vi, n, 0
-        for bi in range(4):
-            hf = wd // 2
-            wb = wbank()
-            mm = []
-            for j in range(2):
-                for k in range(2):
-                    q = 4 * bi + 2 * j + k
-                    mm.append((B(wb, hf * j, hf * j + hf), T.AM[:, 128 * q:128 * q + 128], B(src, pos + hf * k, pos + hf * k + hf), k == 0, k == 1, hf))
-            P([("AM", 4 * bi + y) for y in range(4)] + [sk], [wb], mm)
-            S(hf, [], [wb, ax], B(ax, 0, hf), B(wb, 0, hf), AF.Copy)
-            npos = 0 if bi == 0 else pos + wd
-            V(hf, [ax], [wb, (am, bi)], "tt", B(am, npos, npos + hf), B(ax, 0, hf), B(wb, hf, 2 * hf), ALU.max)
-            src, sk, wd, pos = am, (am, bi), hf, npos
-        wb = rep(B(am, pos, pos + K), True, [(am, 3)])
-        V(n, [vi], [wb, (am, "eq")], "tt", B(am, n, 2 * n), B(vi, 0, n), B(wb, 0, n), ALU.is_equal)
-        w2 = wbank()
-        P(["LTR", (am, "eq")], [w2], [(B(w2, 0, n), T.LTR[:], B(am, n, 2 * n), True, True, n)])
-        V(n, [(am, "eq")], [w2, ("ohy", c)], "tt", B("ohy", n * c, n * c + n), B(am, n, 2 * n), B(w2, 0, n), ALU.is_gt)
-    for i, (off, m) in enumerate(ST[1]):
-        station(1, i, off, m)
-    for c in range(NCH):
-        ax, d1, v1 = "ax%d" % c, "di1%d" % (len(ST[1]) - 1), "vi1%d%d" % (len(ST[1]) - 1, c)
-        a = K * c
-        S(n, [("ohy", c), "ipf"], [ax], B(ax, 0, n), B("ohy", n * c, n * c + n), AF.Copy, scale=T.ipf[:, 0:1])
-        wb = wbank()
-        P(smk + [ax], [wb], [(B(wb, 0, K), smat(r), B(ax, K * r, K * r + K), r == 0, r == 15, K) for r in range(16)])
-        y1, ym = B("y1l", a, a + K), B("yim", a, a + K)
-        V(K, [], [wb, ("y1l", c)], "ts", y1, B(wb, 0, K), float(1.0 / HIT), None, ALU.mult)
-        V(K, [("y0l", c), (hd, c)], [("yim", c)], "tt", ym, B("y0l", a, a + K), B(hd, a, a + K), ALU.max)
-        V(K, [("yim", c), ("dd10", 1, c)], [("yiu", c)], "tt", ym, ym, B("dd10", 64 + a, 64 + a + K), ALU.max)
-        V(K, [("yiu", c)], [("yi0", c)], "ts", B("yit", a, a + K), ym, 16.0, None, ALU.min)
-        V(K, [("y1l", c), (d1, c)], [("y1m", c)], "tt", y1, y1, B(d1, a, a + K), ALU.max)
-        V(K, [("y1m", c)], [("yi1", c)], "ts", B("yit", 64 + a, 64 + a + K), y1, 16.0, None, ALU.min)
-        for t in range(2):
-            D("stores", 16384 // NCH, [("yi%d" % t, c)], [("out",)], T.yi[:, NK * t + n * c:NK * t + n * c + n], B("yit", 64 * t + a, 64 * t + a + K))
-        D("stores", 128 * n * 2, [v1], [("out",)], T.yv[:, n * c:n * c + n], B(v1, 0, n))
+                S("vn", K, [vf], [vn[-1]], out, src, AF.Copy)
+    stage("xv", 262144, vn, T.ZV[0:8], T.VN[:])
+    send(ALL, "re", 16384, xo["xe"], "re", lambda x: T.ZE[x - 1], lambda x: T.ZE[15 - x])
+    send(ALL, "rv", 32768, xo["xv"], "rv", lambda x: T.ZV[x - 1], lambda x: T.ZV[15 - x])
+    send(ALL, "rt", 4096, xo["xt"], "rt", lambda x: T.ZT[x - 1], lambda x: T.ZT[15 - x])
+    for i0, i1, g0 in runs(0, N, R):
+        g1, a, z, m, s1 = g0 + i1 - i0, 7 + i0, 7 + i1, 2048 * (i1 - i0), (R + 1) % N
+        for u0, u1, s0 in runs(1, N, R + 1):
+            DM("stores", m * (u1 - u0), xo["xe"] + ["re"], [("out",)], T.yl[g0:g1, NK * s0:NK * (s0 + u1 - u0)], T.ZE[a:z, 16 * u0:16 * u1, :])
+        DM("stores", m, xo["xe"] + ["re"], [("out",)], T.yi[g0:g1, 0:NK], T.ZE[a:z, 0:16, :])
+        DM("stores", 16 * m, xo["xv"] + ["rv"], [("out",)], T.yv[16 * g0:16 * g1, :], T.ZV[a:z])
+        DM("stores", m, xo["xt"] + ["rt"], [("out",)], T.yl[g0:g1, NK * s1:NK * s1 + NK], T.ZT[a:z, 0:64, :])
+        DM("stores", m, xo["xt"] + ["rt"], [("out",)], T.yi[g0:g1, NK:2 * NK], T.ZT[a:z, 64:128, :])
     return ops
 
 
@@ -534,30 +496,20 @@ def depend(ops):
     for k, o in enumerate(ops):
         d = {}
         for key in o["r"]:
-            for x in writer.get(key, []):
-                d[x] = True
+            d[writer[key]] = True
         for key in o["w"]:
             if key == ("out",):
                 continue
-            for x in writer.get(key, []) + readers.get(key, []):
+            for x in ([writer[key]] if key in writer else []) + readers.get(key, []):
                 d.setdefault(x, False)
         if "after" in o:
             d[o["after"]] = True
         o["d"] = d
         for key in o["w"]:
-            if key in (("es10", 0), ("ej10", 0)):
-                writer.setdefault(key, []).append(k)
-            else:
-                writer[key] = [k]
+            writer[key] = k
             readers[key] = []
         for key in o["r"]:
             readers.setdefault(key, []).append(k)
-
-
-def kind(o):
-    name = o["w"][-1] if o["w"] else (o["r"][0] if o["r"] else "")
-    name = (name if isinstance(name, str) else name[0]).rstrip("0123456789")
-    return name + ("c" if o["q"] == "pe" and any(str(x[0]).startswith("sg") for x in o["r"]) else "")
 
 
 def order(ops):
@@ -573,7 +525,10 @@ def order(ops):
         for y in nxt[k]:
             best = max(best, prio[y] + WAKE)
         prio[k] = best + o["dur"] + o["lat"] + o["tail"]
-    urge = [prio[k] + o["bonus"] + URGE[o["ch"]].get(kind(o), 0) for k, o in enumerate(ops)]
+    urge = []
+    for k, o in enumerate(ops):
+        name, tg = o["tag"]
+        urge.append(prio[k] + o["bonus"] + URGE.get((name,) + tg[:2] if tg else name, 0))
     left = [len(o["d"]) for o in ops]
     ready = [0.0] * cnt
     cand = {}
@@ -606,6 +561,7 @@ def order(ops):
         if o["tail"]:
             lane = max(end, lane) + o["tail"]
             end = lane + o["lat"]
+        o["at"] = (t, end)
         out.append(k)
         for y in nxt[k]:
             left[y] -= 1
@@ -660,7 +616,7 @@ def rank_program(g, core, T, topo):
             for s, c in ops[x]["know"].items():
                 mine[s] = max(mine.get(s, 0), c)
         sem = o["sem"] or QSEM.get(q)
-        for call in o["calls"]:
+        for i, call in enumerate(o["calls"]):
             ins = call(g)
             if sem == "remote":
                 sent += o["cnt"]

@@ -16,11 +16,12 @@ LOW = 63.8 * PER + 0.35
 WID = D + W
 OFF = [[0, 0, 1, 2, 3, 4, 5, 6, 7], [0, 0, 0, 1, 2, 3, 4, 5, 6, 7]]
 PAIRS = [[(1,), (2, 3), (4, 5), (6, 7), (8,)], [(1, 2), (3, 4), (5, 6), (7, 8), (9,)]]
-CALLS = {"J": [[1, 2, 3, 4], [5, 6, 7]], "C": [[1, 2, 3, 4], [5, 6, 7]]}
+CALLS = {"J": [[1, 2], [3, 4], [5, 6, 7]], "C": [[1, 2, 3, 4], [5, 6, 7]]}
+NCC = 3
 B16, F32, I32, U16 = "bfloat16", "float32", "int32", "uint16"
 
 SCRATCH = {}
-SEMAPHORES = ["kpe", "kv", "ks", "kg", "ls", "xl", "xs", "rl", "rs", "ll", "lst", "jo", "co", "xy", "ry", "ly", "xe", "re", "xv", "rv", "xt", "rt", "stores"]
+SEMAPHORES = ["kpe", "kv", "ks", "kg", "ls", "xl", "xs", "rl", "rs", "ll", "lst", "ls0", "jo", "co", "xy", "ry", "ly", "xe", "re", "xv", "rv", "xt", "rt", "stores"]
 SEMAPHORES += ["lj%d" % _b for _b in range(N)]
 for _k in range(len(CALLS["J"])):
     SEMAPHORES += ["rj%d" % _k, "jr%d" % _k]
@@ -33,7 +34,7 @@ def sb(name, cols, dtype=B16):
 
 
 SCRATCH["ZL"] = ("dram", [15, 128, 64], B16)
-SCRATCH["ZS"] = ("dram", [15, 128, 16], I32)
+SCRATCH["ZS"] = ("dram", [15, 128, 16], B16)
 SCRATCH["ZJ"] = ("dram", [7, 128, BW], B16)
 SCRATCH["ZC"] = ("dram", [7, 128, BW], B16)
 SCRATCH["XC"] = ("dram", [8, 128, BW], B16)
@@ -46,10 +47,13 @@ sb("CW", WID)
 sb("jmi", W, I32)
 sb("jmf", W, F32)
 sb("JS", W)
-for _k, _c in (("ones", 256), ("Z1", 256), ("Z2", 256), ("Z1x", 256), ("IDT", 32), ("BDa", 128), ("BD", 128), ("LTR", 128), ("RM", 2048), ("ROT", 512),
-               ("rta", 512), ("I64", 128), ("I32", 128), ("K16", 32), ("b8a", 8), ("b8", 8), ("LT", 576), ("OH", 9 * NK), ("ohn", NK), ("G1", NK), ("mj", NK),
-               ("A1", 640), ("L1", 512), ("hb", 512), ("YL", 512), ("YI", 128), ("y1l", 64), ("VN", NK)):
+SCALED = {"I64": (64.0, 1), "I32": (32.0, -1), "I16": (16.0, 0), "I8": (8.0, 0), "In": (-1.0, 0), "Ib": (-1.0, -1), "Ip": (1.0 / 16, -1), "Im": (-1.0 / 16, -1)}
+for _k, _c in (("ones", n), ("Z1", 256), ("Z2", 256), ("ZF", 256), ("ZN", 256), ("Z1x", 256), ("IDT", 32), ("BDa", 128), ("BD", 128), ("LTR", 128), ("M1", 128),
+               ("RM", 2048), ("AM", 2048), ("IS", 128 * len(SCALED)), ("K16", 32), ("b8a", 8), ("b8", 8), ("LT", 576), ("eR", 512), ("OH", 9 * NK), ("ohn", NK),
+               ("G1", NK), ("Gp", NK), ("mj", NK), ("L1", 640), ("YL", 640), ("VN", NK), ("stc", 128), ("std", 128)):
     sb(_k, _c)
+sb("stf", 128, F32)
+sb("stg", 128, F32)
 sb("ipi", 2, I32)
 sb("ipj", 2, I32)
 sb("ipf", 2, F32)
@@ -61,9 +65,8 @@ sb("LTu", 576, U16)
 sb("t0", 128, F32)
 sb("l0", 128, U16)
 for _c in range(2):
-    for _k, _w in (("cc", 3 * n), ("sg", 4 * n), ("va", 8 * n), ("vb", 9 * n), ("vf", n), ("xa", 2 * n), ("eq", n), ("oy", n), ("mb", K), ("nc", 2 * K),
-                   ("A0", 9 * K), ("LHa", 8 * K), ("LHb", 9 * K), ("ea", 8 * K), ("eb", 9 * K), ("nf", 9 * K), ("xh", 9 * K), ("ha", 8 * K), ("hc", 9 * K),
-                   ("hit", 8 * K), ("dz", K)):
+    for _k, _w in (("cc", NCC * n), ("X", 5 * n), ("va", 8 * n), ("vb", 9 * n), ("vf", n), ("ax", n // 2), ("am", n), ("eq", n), ("oy", n), ("mb", K),
+                   ("Aa", 9 * K), ("Ab", 10 * K), ("ea", 8 * K), ("eb", 9 * K), ("ha", 8 * K), ("hc", 9 * K)):
         sb("%s%d" % (_k, _c), _w)
     sb("tt%d" % _c, 2 * K, F32)
     sb("li%d" % _c, 2 * 10 * 2 * K, U16)
@@ -74,8 +77,10 @@ for _c in range(2):
 VF, SF, CY, PCY, PF, GA, WAKE, SELF, GAP = 45.0, 65.0, 0.95, 0.5, 20.0, 1.5, 90.0, 60.0, 150.0
 HOP, LAT, GBW, CALL = 2000.0, 1800.0, 250.0, 900.0
 FIRST = 1e6
-OPT = {"ohv": (8,), "signv": (), "cgv": (), "dupv": 2, "permv": 11, "pace": 5}
-URGE = {}
+OPT = {"ohv": (8,), "signv": (), "cgv": (), "dupv": 2, "dupg": 0, "permv": 11, "pace": [("JS", 0), "rj1", "jr0"], "deep": 3, "eqv": True, "mjv": True, "oyv": False, "vfv": (),
+       "merge": [[(7, 4), (9, 3)], [(4, 3), (4, 3)]]}
+OPT = {'ohv': (3, 4, 5, 7, 8), 'signv': ((0, 0, 2), (0, 0, 7), (0, 1, 7), (0, 1, 8), (1, 0, 6), (1, 1, 7), (1, 1, 9)), 'cgv': ((0, 0, 0), (0, 0, 2), (0, 0, 8), (1, 0, 0)), 'dupv': 5, 'dupg': 1, 'permv': 10, 'pace': ['rj1', 'rj2', 'jr1'], 'deep': 3, 'eqv': True, 'mjv': True, 'oyv': False, 'vfv': ((0, 1),), 'merge': [[(9, 4), (7, 3)], [(4, 3), (4, 3)]]}
+URGE = {'oh': -20000, 'G1': -15000, 'Gp': -15000, ('l1', 1, 1): -10000, ('oy', 1, 0): -10000, ('oy', 1, 1): -10000, ('y1', 1, 0): -10000, ('y1', 1, 1): -10000, ('cg', 0, 0): 3000, ('add', 0, 0): 3000, ('clip', 0, 0): 3000, ('sg', 0, 0): 3000, ('cnt', 0, 0): 3000, ('nc', 0, 0): 3000, ('al', 0, 0): 3000, ('vf', 0, 0): 4000, ('pick', 0, 0): 4000, ('lv', 0, 0): 4000, ('jg', 0, 0): 6000, ('js', 0, 0): 6000, ('ln', 0, 0): 6000, ('li', 0, 0): 6000, ('mb', 0, 0): 6000, ('eb', 1, 0): 4000, ('eb', 1, 1): 4000, ('h', 1, 0): 4000, ('h', 1, 1): 4000, ('m1', 1, 0): 4000, ('m1', 1, 1): 4000, ('mx', 1, 0): 4000, ('mx', 1, 1): 4000, ('rep', 1, 0): 4000, ('rep', 1, 1): 4000, ('eq', 1, 0): 4000, ('eq', 1, 1): 4000, ('ltr', 1, 0): 4000, ('ltr', 1, 1): 4000, ('m0', 1, 0): 4000, ('m0', 1, 1): 4000, ('jg', 1, 0): 6000, ('jg', 1, 1): 6000, ('js', 1, 0): 6000, ('js', 1, 1): 6000, ('ln', 1, 0): 6000, ('ln', 1, 1): 6000, ('li', 1, 0): 6000, ('li', 1, 1): 6000, ('mb', 1, 0): 6000, ('mb', 1, 1): 6000, ('jg', 1, 1, 2): -4000, 'JS': 200, ('li', 0, 0, 8): -8000, ('clip', 0, 1, 2): -200, ('li', 0, 1, 1): 200, ('mb', 1, 0, 0): 500, ('pick', 0, 1): -8000, 'rs': -1500, ('js', 1, 0, 3): 1000, ('lv', 0, 1): 500, ('mb', 1, 0, 8): -2000, 'stu': -12000, ('cg', 0, 1): -500, ('cg', 1, 1): -1000, ('add', 1, 1): -1000, ('clip', 1, 1): -1000, ('sg', 1, 1): -1000, ('cnt', 1, 1): -1000, ('nc', 1, 1): -1000, ('al', 1, 1): -1000, ('jg', 0, 0, 4): 4000, ('nc', 0, 1, 3): 2000, ('sg', 1, 1, 4): 8000, ('al', 1, 0): -200, ('cnt', 0, 0, 5): 2000, ('mb', 1, 1, 4): -4000, ('li', 1, 1, 8): -8000, ('sg', 1, 1, 7): -200}
 
 
 def program(R, T, topo):
@@ -154,21 +159,25 @@ def program(R, T, topo):
             DM("xl", 2048 * (i1 - i0) * (u1 - u0), [], [xl[-1]], T.ZL[7 + i0:7 + i1, 16 * u0:16 * u1, :], T.lt[g0:g1, NK * s0:NK * (s0 + u1 - u0)], bonus=9 * FIRST)
         xy.append(("xy", i0))
         DM("xy", 2048 * (i1 - i0), [], [xy[-1]], T.ZY[7 + i0:7 + i1], T.y0[g0:g1, :], bonus=9 * FIRST)
+    DM("ls0", 65536, [], ["sti"], T.sti[:], T.st[:], bonus=8.5 * FIRST)
+    V("st", 128, ["sti"], ["stf"], "copy", T.stf[:], T.sti[:])
+    S("st", 128, ["stf"], ["stc"], T.stc[:], T.stf[:], AF.Exp, bias=float(-LOW * SC), scale=float(SC))
+    for i0, i1, g0 in runs(0, N, R):
         xs.append(("xs", i0))
-        DM("xs", 8192 * (i1 - i0), [], [xs[-1]], T.ZS[7 + i0:7 + i1], T.st[16 * g0:16 * g1, :], bonus=8.5 * FIRST)
+        DM("xs", 4096 * (i1 - i0), ["stc"], [xs[-1]], T.ZS[7 + i0:7 + i1], T.stc[16 * g0:16 * (g0 + i1 - i0), :], bonus=8.5 * FIRST)
     send(ALL, "rl", 16384, xl, "rl", lambda x: T.ZL[7 + x], lambda x: T.ZL[7 - x], bonus=9 * FIRST)
     send(ALL, "ry", 2048, xy, "ry", lambda x: T.ZY[7 + x], lambda x: T.ZY[7 - x], bonus=8.5 * FIRST)
-    send(ALL, "rs", 8192, xs, "rs", lambda x: T.ZS[7 + x], lambda x: T.ZS[7 - x], bonus=8 * FIRST)
+    send(ALL, "rs", 4096, xs, "rs", lambda x: T.ZS[7 + x], lambda x: T.ZS[7 - x], bonus=6 * FIRST)
     ltk = [("LT", u) for u in range(8)]
     yk = [("LT", 8)]
     for u in range(8):
         DM("ll", 16384, xl + ["rl"], [("LT", u)], B("LT", 64 * u, 64 * u + 64), T.ZL[0:8, 16 * u:16 * u + 16, :], bonus=8 * FIRST)
     DM("ly", 16384, xy + ["ry"], yk, B("LT", 512, 576), T.ZY[0:8], bonus=8 * FIRST)
-    DM("lst", 65536, xs + ["rs"], ["sti"], T.sti[:], T.ZS[0:8], bonus=7 * FIRST)
+    DM("lst", 32768, xs + ["rs"], ["std"], T.std[:], T.ZS[0:8], bonus=7 * FIRST)
     jorder = [x for c in CALLS["J"] for x in c] + [0]
     for i, x in enumerate(jorder):
         g0, a, z = (R + x) % N, BW * x, BW * x + BW
-        DM("lj%d" % x, 128 * BW * 4, [], [("jmi", x)], B("jmi", a, z), T.jm[16 * g0:16 * g0 + 16, :], bonus=FIRST * (8 - 0.1 * i))
+        DM("lj%d" % x, 128 * BW * 4, [("jmi", jorder[i - OPT["deep"]])] if i >= OPT["deep"] else [], [("jmi", x)], B("jmi", a, z), T.jm[16 * g0:16 * g0 + 16, :], bonus=FIRST * (8 - 0.1 * i))
         V("jmf", BW, [("jmi", x)], [("jmf", x)], "copy", B("jmf", a, z), B("jmi", a, z))
         ops[-1]["bonus"] = FIRST
         S("JS", BW, [("jmf", x)], [("JS", x)], B("JS", a, z), B("jmf", a, z), AF.Exp, bias=float(-LOW * SC), scale=float(SC))
@@ -181,9 +190,8 @@ def program(R, T, topo):
         jk.append("jr%d" % k)
     DM("jo", 128 * BW * 2, [("JS", 0)], ["jo"], T.JW[112:128, 0:W], B("JS", 0, BW), bonus=7 * FIRST)
     ck = ["co", "cz"]
-    pace = [("JS", jorder[OPT["pace"]])]
     for k, c in enumerate(CALLS["C"]):
-        xk = []
+        xk, pace = [], [OPT["pace"][k]]
         for i0, i1, g0 in runs(min(c), max(c) + 1, R):
             xk.append(("xc", i0))
             DM("xc%d" % k, 128 * BW * 2 * (i1 - i0), pace, [xk[-1]], T.XC[i0:i1], T.cf[16 * g0:16 * (g0 + i1 - i0), :], bonus=3 * FIRST)
@@ -191,17 +199,16 @@ def program(R, T, topo):
         p0, p1 = 7 - max(c), 8 - min(c)
         DM("cr%d" % k, 128 * BW * 2 * len(c), ["rc%d" % k], ["cr%d" % k], T.CW[16 * p0 + 16:16 * p1 + 16, 0:W], T.ZC[p0:p1], bonus=3 * FIRST)
         ck.append("cr%d" % k)
-    DM("co", 128 * BW * 2, pace, ["co"], T.CW[0:16, 0:W], T.cf[16 * R:16 * R + 16, :], bonus=2 * FIRST)
-    V("c", 128, [], ["ones"], "set", T.ones[:], 1.0)
+    DM("co", 128 * BW * 2, [OPT["pace"][-1]], ["co"], T.CW[0:16, 0:W], T.cf[16 * R:16 * R + 16, :], bonus=2 * FIRST)
+    V("c", 256, [], ["ones"], "set", T.ones[:], 1.0)
     V("c", 128, [], ["Z10"], "set", T.Z1[:], 0.0)
     V("c", (D - W) // 2, [], ["jz"], "set", B("JW", W, D), 0.0)
     for i in range(4):
         V("c", D // 8, [], [("cz", i)], "set", B("CW", W + D // 4 * i, W + D // 4 * (i + 1)), 0.0)
     ck = [x for x in ck if x != "cz"] + [("cz", i) for i in range(4)]
     for c in range(2):
-        V("c", 32, [], [("A0", c, 0)], "set", B("A0%d" % c, 0, K), 16.0)
-        V("c", 32, [], [("nf0", c)], "set", B("nf%d" % c, 0, K), float(F))
-    V("c", 32, [], [("A1", 0, 0), ("A1", 1, 0)], "set", B("A1", 0, 64), 16.0)
+        for a in ("Aa%d" % c, "Ab%d" % c):
+            V("c", 32, [], [(a, 0)], "set", B(a, 0, K), 16.0)
     G("ipi", 2, [], lambda g: g.iota(T.ipi[:], [[0, 2]], 0, 1))
     G("io32", 32, [], lambda g: g.iota(T.io32[:], [[1, 32]], 0, 0, allow_small_or_imprecise_dtypes=True))
     V("c", 2, ["ipi"], ["ipj"], "ts", T.ipj[:], T.ipi[:], 15, None, ALU.bitwise_and)
@@ -209,7 +216,7 @@ def program(R, T, topo):
     row = T.ipf[:, 0:1]
     V("c", 32, ["io32", "ipf"], ["IDT"], "ts", T.IDT[:], T.io32[:], row, None, ALU.is_equal)
     V("c", 32, ["io32"], ["K16"], "ts", T.K16[:], T.io32[:], 16.0, None, ALU.mult)
-    pick("Z2", T.Z2[:], T.ones[:], [[0, 2], [-1, 128]], ALU.is_equal, 0, 1, 256, "ones")
+    pick("Z2", T.Z2[:], T.ones[:, 0:256], [[0, 2], [-1, 128]], ALU.is_equal, 0, 1, 256, "ones")
     pick("b8a", T.b8a[:], T.ones[:, 0:8], [[-16, 8]], ALU.is_ge, 0, 1, 8, "ones")
     pick("b8", T.b8[:], T.b8a[:], [[16, 8]], ALU.is_ge, 15, -1, 8, "b8a")
     V("c", 8, ["b8", "Z10"], ["Z1a"], "copy", B("Z1", 0, 128, 16), T.b8[:])
@@ -222,23 +229,39 @@ def program(R, T, topo):
     rmk = [("RM", r) for r in range(16)]
     for r in range(16):
         V("c", 64, ["BD", "IDT"], [("RM", r)], "ts", B("RM", 128 * r, 128 * r + 128), T.BD[:], T.IDT[:, r:r + 1], None, ALU.mult)
-    for i, be in enumerate((8, 4, 2, 1)):
-        V("c", 256, ["Z2"], [("rta", i)], "tt", B("rta", 128 * i, 128 * i + 128), B("Z2", 128 - be, 256 - be), B("Z2", 16 - be, 144 - be), ALU.add)
-        V("c", 256, [("rta", i), "BD"], [("ROT", i)], "tt", B("ROT", 128 * i, 128 * i + 128), B("rta", 128 * i, 128 * i + 128), T.BD[:], ALU.mult)
-    V("c", 64, ["Z2"], ["I64"], "ts", T.I64[:], B("Z2", 0, 128), 64.0, None, ALU.mult)
-    V("c", 64, ["Z2"], ["I32"], "ts", T.I32[:], B("Z2", 0, 128), 32.0, None, ALU.mult)
+    for bi, be in enumerate((8, 4, 2, 1)):
+        for m, (step, base) in enumerate(((1000, 0), (-1000, 1000), (1000, -be), (-1000, 1000 - be))):
+            j = 4 * bi + m
+            G(("AM", j), 128, ["ones", "rc%d" % (len(CALLS["C"]) - 1)], lambda g, j=j, be=be, step=step, base=base: g.affine_select(
+                B("AM", 128 * j, 128 * j + 128), T.ones[:, 0:128], [[-2 * be, 64 // be], [step, 2], [-1, be]], ALU.is_equal, 0.0, base, 1))
+    I = {}
+    for i, k in enumerate(sorted(SCALED)):
+        I[k] = B("IS", 128 * i, 128 * i + 128)
+        o = -16 * SCALED[k][1] % 128
+        V("c", 64, ["Z2"], [k], "ts", I[k], B("Z2", o, o + 128), SCALED[k][0], None, ALU.mult)
+    V("c", 128, ["Z2"], ["ZF"], "ts", T.ZF[:], T.Z2[:], float(F), None, ALU.mult)
+    V("c", 128, ["Z2"], ["ZN"], "ts", T.ZN[:], T.Z2[:], float(-F), None, ALU.mult)
+    V("c", 256, ["Z2", "LTR"], ["M1"], "tt", T.M1[:], B("Z2", 0, 128), T.LTR[:], ALU.subtract)
 
     def sel(r, a, name="Z1"):
         o = -(16 * a + r) % 128
         return B(name, o, o + 128)
 
-    def sh(a):
+    def sh(a, name="Z2"):
         o = -16 * a % 128
-        return B("Z2", o, o + 128)
+        return B(name, o, o + 128)
+
+    def relu(name, on_v, cyc, reads, writes, out, src):
+        if on_v:
+            V(name, cyc, reads, writes, "ts", out, src, 0.0, None, ALU.max)
+        else:
+            S(name, cyc, reads, writes, out, src, AF.Relu)
 
     V("ltf", 576, ltk + yk, ["LTf"], "copy", T.LTf[:], T.LT[:])
     V("ltf", 576, ["LTf"], ["LTu"], "copy", T.LTu[:], T.LTf[:])
-    V("stu", 128, ["sti"], ["stu"], "copy", T.stu[:], T.sti[:])
+    S("stu", 128 + 1500, ["std"] + [("JS", x) for x in range(N)], ["stg"], T.stg[:], T.std[:], AF.Ln)
+    V("stu", 128, ["stg"], ["stu"], "ts", T.stu[:], T.stg[:], float(A), float(LOW), ALU.mult, ALU.add)
+    V("eR", 256, ltk, ["eR"], "ts", T.eR[:], B("LT", 0, 512), 15.5, None, ALU.is_gt)
     for d in range(9):
         u = 8 if d == 8 else -d % N
         src, out = T.IDT[:].indirect(B("LTu", 64 * u, 64 * u + 64)), B("OH", NK * d, NK * d + NK)
@@ -256,32 +279,36 @@ def program(R, T, topo):
         dupk.append(("dup", i))
         if i < OPT["dupv"]:
             V("dup", BW // 2, jk, [("dup", i)], "copy", B("JW", D + a, D + z), B("JW", a, z))
+        elif i < OPT["dupv"] + OPT["dupg"]:
+            G(("dup", i), BW, jk, lambda g, a=a, z=z: g.affine_select(B("JW", D + a, D + z), B("JW", a, z), [[0, BW]], ALU.is_equal, 0.0, 0, 0))
         else:
             S("dup", BW, jk, [("dup", i)], B("JW", D + a, D + z), B("JW", a, z), AF.Copy)
-    S("G1", GA * NK, jk + ["stu"], ["G1"], T.G1[:], B("JW", 0, W).indirect(B("stu", 64, 128)), AF.Copy)
 
     def gates(w, c):
         Tn = len(OFF[w]) - 1
-        lh, e, h = ("LHa", "LHb")[w] + str(c), ("ea", "eb")[w] + str(c), ("ha", "hc")[w] + str(c)
-        nf, xh, pw = "nf%d" % c, "xh%d" % c, "pw%d" % c
-        lk = [(lh, 0), (lh, 1)] if w else [lh]
-        V("e", Tn * K // 2, lk, [e], "ts", B(e, 0, Tn * K), B(lh, 0, Tn * K), 15.5, None, ALU.is_gt)
-        V("nf", Tn * K // 2, lk, [nf], "ts", B(nf, K, Tn * K), B(lh, 0, Tn * K - K), 15.5, float(F), ALU.is_lt, ALU.mult)
-        V("xh", Tn * K, [e, nf, ("nf0", c)], [xh], "tt", B(xh, 0, Tn * K), B(e, 0, Tn * K), B(nf, 0, Tn * K), ALU.mult)
+        e, h, pw = ("ea", "eb")[w] + str(c), ("ha", "hc")[w] + str(c), "pw%d" % c
         mm = []
         for t in range(1, Tn + 1):
-            a = K * (t - 1)
-            mm.append((B(pw, a, a + K), sh(OFF[w][t - 1] + 1), B(xh, a, a + K), True, False, K))
-            mm.append((B(pw, a, a + K), sh(OFF[w][t - 1] + 1), B(e, a, a + K), False, True, K))
-        P("h", ["Z2", xh, e], [pw], mm)
-        S("h", Tn * K, [], [pw, h], B(h, 0, Tn * K), B(pw, 0, Tn * K), AF.Copy)
+            a, s = K * (t - 1), OFF[w][t - 1] + 1
+            mm.append((B(pw, a, a + K), sh(s, "ZF"), B(e, a, a + K), True, t == 1, K))
+            if t > 1:
+                mm.append((B(pw, a, a + K), sh(s, "ZN"), B(e, a - K, a), False, False, K))
+                mm.append((B(pw, a, a + K), sh(s), B(e, a, a + K), False, True, K))
+        P("h", ["Z2", "ZF", "ZN", e], [pw], mm)
+        S("h", Tn * K, [], [pw, h], B(h, 0, Tn * K), B(pw, 0, Tn * K), AF.Relu)
 
     for c in range(2):
         tag[0] = (0, c, 0)
         pw = "pw%d" % c
-        P("lh", ["Z2"] + ltk, [pw], [(B(pw, K * d, K * d + K), sh(-d), B("LT", 64 * (-d % N) + K * c, 64 * (-d % N) + K * c + K), True, True, K) for d in range(8)])
-        S("lh", 8 * K, [], [pw, "LHa%d" % c], B("LHa%d" % c, 0, 8 * K), B(pw, 0, 8 * K), AF.Copy)
+        P("ea", ["Z2", "eR"], [pw], [(B(pw, K * d, K * d + K), sh(-d), B("eR", 64 * (-d % N) + K * c, 64 * (-d % N) + K * c + K), True, True, K) for d in range(8)])
+        S("ea", 8 * K, [], [pw, "ea%d" % c], B("ea%d" % c, 0, 8 * K), B(pw, 0, 8 * K), AF.Copy)
         gates(0, c)
+    tag[0] = None
+    S("G1", GA * NK, jk + ["stu"], ["G1"], T.G1[:], B("JW", 0, W).indirect(B("stu", 64, 128)), AF.Copy)
+    for c in range(2):
+        pw = "pw%d" % c
+        P("Gp", ["Z2", "G1"], [pw], [(B(pw, r, n, 16), sh(0), B("G1", 64 * r + K * c, 64 * r + K * c + K), True, True, K) for r in range(16)])
+        S("Gp", n, [], [pw, ("Gp", c)], B("Gp", n * c, n * c + n), B(pw, 0, n), AF.Copy)
 
     lists = {}
 
@@ -289,117 +316,157 @@ def program(R, T, topo):
         h = ("ha", "hc")[w] + str(c)
         V("mb", K, [h], [bank, "mb%d" % c], "tt", B("mb%d" % c, 0, K), B(bank, at, at + K), B(h, K * t, K * t + K), ALU.mult)
 
-    def decode(w, c, t, two):
-        pj, tt, li = "pj%d" % c, "tt%d" % c, "li%d" % c
-        m, a = K * (1 + two), 2 * K * (10 * w + t)
-        S("ln", m, [], [pj, tt], B(tt, 0, m), B(pj, 0, m), AF.Ln)
-        V("li", m, [tt], [(li, w, t)], "ts", B(li, a, a + m), B(tt, 0, m), float(A), float(LOW), ALU.mult, ALU.add)
-        lists[w, c, t] = (B(li, a, a + K), B(li, a + K * two, a + K * two + K), (li, w, t))
-        if t + 1 < len(OFF[w]):
-            mark(w, c, t, pj, 0)
+    jobs, along = {}, {}
+    for w in range(2):
+        for c in range(2):
+            Tn = len(OFF[w]) - 1
+            first, lag = OPT["merge"][w][c]
+            rest = []
+            for t in range(1, Tn + 2):
+                if t <= Tn and not first <= t + lag <= Tn:
+                    rest.append(t)
+                    if t < Tn - 1:
+                        continue
+                for i in range(len(rest) % 2 - 2, len(rest) - 1, 2):
+                    job = tuple(rest[max(i, 0):i + 2])
+                    for y, x in enumerate(job):
+                        jobs[w, c, x] = (job, 3 + y if len(job) == 2 else 3 + x % 2)
+                if t <= Tn and t not in rest:
+                    jobs[w, c, t] = (None, 2 * (t % 2))
+                    along[w, c, t + lag] = t
+                rest = []
+
+    def akey(w, c, t):
+        a = ("Aa", "Ab")[w] + str(c)
+        return B(a, K * t, K * t + K), (a, t)
+
+    def alive(w, c, job, bank, at):
+        al, m = ("Aa", "Ab")[w] + str(c), K * len(job)
+        V("nc", m, [], [bank] + [(al, x) for x in job], "ts", B(al, K * job[0], K * job[0] + m), B(bank, at, at + m), 127.25, 16.0, ALU.is_gt, ALU.mult)
+        if len(job) == 2:
+            (p, pk), (q, qk) = akey(w, c, job[0]), akey(w, c, job[1])
+            V("al", 2 * K, [pk, qk], [qk], "tt", q, p, q, ALU.min)
+        if job[-1] == len(OFF[w]) - 2:
+            ended(w, c)
+
+    def marks(w, c, job, bank, at):
+        e = ("ea", "eb")[w] + str(c)
+        p, pk = akey(w, c, job[0] - 1)
+        mm = [(B(bank, at + K * i, at + K * i + K), I["I8"], p, False, False, K) for i in range(len(job))]
+        mm.append((B(bank, at, at + K * len(job)), I["I64"], B(e, K * (job[0] - 1), K * job[-1]), False, True, K * len(job)))
+        return mm, ["I64", "I8", e, pk]
 
     def series(w, c, t):
-        pj, mb, o = "pj%d" % c, "mb%d" % c, OFF[w]
+        pj, mb, x, o = "pj%d" % c, "mb%d" % c, "X%d" % c, OFF[w]
         two = int(t + 1 < len(o) and o[t + 1] == o[t])
-        mm = []
-        for y in range(1 + two):
+        reads = z1 + ["Z2", (x, 1)] + ([mb] if t else [])
+        u, at, mm = along.get((w, c, t)), 0, []
+        if u:
+            y = jobs[w, c, u][1]
+            at, a = (0, n) if y else (K, 0)
+            mm = [(B(pj, 0, 2 * K), sel(r, 1), B(x, a + r, a + 2 * n, 16), r == 0, False, 2 * K) for r in range(16)]
+            mm.append((B(pj, at, at + K), sh(1), B(mb, 0, K), False, False, K))
+            more, mk = marks(w, c, (u,), pj, K - at)
+            mm += more
+            reads += mk + [(x, y)]
+        for y in range(0 if u else 1 + two):
             out = B(pj, K * y, K * y + K)
             if t:
                 mm.append((out, sh(o[t] - o[t - 1] - y), B(mb, 0, K), True, False, K))
             for r in range(16):
-                mm.append((out, sel(r, 1 - y), B("mj", n * c + r, n * c + n, 16), r == 0 and not t, r == 15, K))
-        P("js", z1 + ["Z2", ("mj", c)] + ([mb] if t else []), [pj], mm)
-        decode(w, c, t, two)
+                mm.append((out, sel(r, 1 - y), B(x, n + r, 2 * n, 16), r == 0 and not t, r == 15, K))
+        P("js", reads, [pj], mm)
+        tt, li = "tt%d" % c, "li%d" % c
+        m, a = K * (1 + two), 2 * K * (10 * w + t)
+        S("ln", m, [], [pj, tt], B(tt, 0, m), B(pj, at, at + m), AF.Ln)
+        V("li", m, [tt], [(li, w, t)], "ts", B(li, a, a + m), B(tt, 0, m), float(A), float(LOW), ALU.mult, ALU.add)
+        lists[w, c, t] = (B(li, a, a + K), B(li, a + K * two, a + K * two + K), (li, w, t))
+        if t + 1 < len(o):
+            mark(w, c, t, pj, at)
+        if u:
+            alive(w, c, (u,), pj, K - at)
 
     def image(w, c, t):
         _, lj, key = lists[w, c, t - 1]
         d = 8 if (w, t) == (1, 1) else OFF[w][t]
         hi, tk = (W, jk) if t == 1 else (WID, jk + dupk)
-        V("jg", GA * n, [key, ("OH", d)] + tk, [("mj", c)], "tt", B("mj", n * c, n * c + n), B("JW", 0, hi).indirect(lj), B("OH", NK * d + n * c, NK * d + n * c + n), ALU.mult)
+        V("jg", GA * n, [key, ("OH", d)] + tk, [("X%d" % c, 1)], "tt", B("X%d" % c, n, 2 * n), B("JW", 0, hi).indirect(lj), B("OH", NK * d + n * c, NK * d + n * c + n), ALU.mult)
         series(w, c, t)
 
     def coefs(w, c, t):
         lc, _, key = lists[w, c, t]
-        y = 2 if t == 0 else t % 2
+        y = t % NCC
         out, src = B("cc%d" % c, n * y, n * y + n), B("CW", 0, WID).indirect(lc)
         if (w, c, t) in OPT["cgv"]:
             V("cg", GA * n, [key] + ck, [("cc", c, y)], "copy", out, src)
         else:
             S("cg", GA * n, [key] + ck, [("cc", c, y)], out, src, AF.Copy)
 
-    def akey(w, c, t):
-        return (B("A0%d" % c, K * t, K * t + K), ("A0", c, t)) if w == 0 else (B("A1", 64 * t + K * c, 64 * t + K * c + K), ("A1", c, t))
-
     def sums(w, c, t):
         va, pv, cc, o = ("va", "vb")[w] + str(c), "pv%d" % c, "cc%d" % c, OFF[w]
-        y = t % 2
+        y = t % NCC
         mm = [(B(pv, 0, n), sh(-o[t] - 1), B(cc, n * y, n * y + n), True, False, n)]
         if t == 1:
-            mm.append((B(pv, 0, n), sh(-1), B(cc, 2 * n, 3 * n), False, True, n))
-            rk = [("cc", c, 2)]
+            mm.append((B(pv, 0, n), sh(-1), B(cc, 0, n), False, True, n))
+            rk = [("cc", c, 0)]
         else:
             mm.append((B(pv, 0, n), sh(0), B(va, n * (t - 2), n * (t - 1)), False, True, n))
             rk = [(va, t - 1)]
         P("add", ["Z2", ("cc", c, y)] + rk, [pv], mm)
         v = B(va, n * (t - 1), n * t)
         V("clip", n, [], [pv, (va, t)], "ts", v, B(pv, 0, n), 255.0, -255.0, ALU.min, ALU.max)
-        j = [i for i, p in enumerate(PAIRS[w]) if t in p][0]
-        pair = PAIRS[w][j]
-        sg, a = "sg%d" % c, 2 * n * (j % 2)
-        b = a + n * pair.index(t)
+        job, y = jobs[w, c, t]
+        x = "X%d" % c
         if (w, c, t) in OPT["signv"]:
-            V("sg", n // 2, [(va, t)], [(sg, j % 2, pair.index(t))], "ts", B(sg, b, b + n), v, 0.0, 0.5, ALU.is_ge, ALU.subtract)
+            V("sg", n // 2, [(va, t)], [(x, y)], "ts", B(x, n * y, n * y + n), v, 0.0, 0.5, ALU.is_ge, ALU.subtract)
         else:
-            S("sg", n, [(va, t)], [(sg, j % 2, pair.index(t))], B(sg, b, b + n), v, AF.Sign, bias=0.5)
-        if t != pair[-1]:
-            return
-        e, pc, nc, m = ("ea", "eb")[w] + str(c), "pc%d" % c, "nc%d" % c, K * len(pair)
-        mm = [(B(pc, 0, m), T.I64[:], B(e, K * (pair[0] - 1), K * pair[-1]), True, False, m)]
-        for r in range(16):
-            mm.append((B(pc, 0, m), sel(r, 0), B(sg, a + r, a + n * len(pair), 16), False, r == 15, m))
-        P("cnt", z1 + ["I64", e] + [(sg, j % 2, i) for i in range(len(pair))], [pc], mm)
-        if pair == (1,):
-            V("nc", m, [], [pc, akey(w, c, 1)[1]], "ts", akey(w, c, 1)[0], B(pc, 0, m), -0.75, 16.0, ALU.is_gt, ALU.mult)
-        else:
-            V("nc", m, [], [pc, nc], "ts", B(nc, 0, m), B(pc, 0, m), -0.75, 16.0, ALU.is_gt, ALU.mult)
-            for i, x in enumerate(pair):
-                (p, pk), (q, qk) = akey(w, c, x - 1), akey(w, c, x)
-                V("al", 2 * K, [nc, pk], [qk], "tt", q, p, B(nc, K * i, K * i + K), ALU.min)
-        if t == len(o) - 2:
-            ended(w, c)
+            S("sg", n, [(va, t)], [(x, y)], B(x, n * y, n * y + n), v, AF.Sign, bias=0.5)
+        if job and t == job[-1]:
+            pc, m, a = "pc%d" % c, K * len(job), n * jobs[w, c, job[0]][1]
+            mm = [(B(pc, 0, m), sel(r, 1), B(x, a + r, a + n * len(job), 16), r == 0, False, m) for r in range(16)]
+            more, mk = marks(w, c, job, pc, 0)
+            P("cnt", z1 + mk + [(x, jobs[w, c, i][1]) for i in job], [pc], mm + more)
+            alive(w, c, job, pc, 0)
 
     def ended(w, c):
         Tn = len(OFF[w]) - 1
         pc, lv = "pc%d" % c, "lv%d" % c
         mm = [(B(pc, 64, 64 + K), sh(0), T.K16[:], True, False, K)]
         for t in range(1, Tn):
-            mm.append((B(pc, 64, 64 + K), T.I32[:], akey(w, c, t)[0], False, t == Tn - 1, K))
+            mm.append((B(pc, 64, 64 + K), I["I32"], akey(w, c, t)[0], False, t == Tn - 1, K))
         P("pick", ["Z2", "K16", "I32"] + [akey(w, c, t)[1] for t in range(1, Tn)], [pc], mm)
         V("lv", K, ["ipf"], [pc, (lv, w)], "ts", B(lv, K * w, K * w + K), B(pc, 64, 64 + K), row, None, ALU.add)
 
     def final(w, c):
         Tn = len(OFF[w]) - 1
         va, lv, vf = ("va", "vb")[w] + str(c), "lv%d" % c, "vf%d" % c
-        S("vf", GA * n, [(lv, w)] + [(va, t) for t in range(1, Tn + 1)], [vf], B(vf, 0, n), B(va, 0, n * Tn).indirect(B(lv, K * w, K * w + K)), AF.Copy)
+        reads, src = [(lv, w)] + [(va, t) for t in range(1, Tn + 1)], B(va, 0, n * Tn).indirect(B(lv, K * w, K * w + K))
+        if (w, c) in OPT["vfv"]:
+            V("vf", GA * n, reads, [vf], "copy", B(vf, 0, n), src)
+        else:
+            S("vf", GA * n, reads, [vf], B(vf, 0, n), src, AF.Copy)
 
     def walk(w, c):
-        for t in range(len(OFF[w])):
+        late = OPT["merge"][w][c][1] - 1
+        for u in range(len(OFF[w]) + late):
+            if 0 < u < len(OFF[w]):
+                tag[0] = (w, c, u)
+                image(w, c, u)
+            t = u - late
             tag[0] = (w, c, t)
-            if t:
-                image(w, c, t)
-            coefs(w, c, t)
-            if t:
+            if t >= 0:
+                coefs(w, c, t)
+            if t > 0:
                 sums(w, c, t)
-            if t == len(OFF[w]) - 1:
-                final(w, c)
+        final(w, c)
 
     tag[0] = (0, 0, 0)
-    V("jg", GA * NK, ["stu", ("ohn", 0), ("ohn", 1)] + jk, [("mj", 0), ("mj", 1)], "tt", T.mj[:], B("JW", 0, W).indirect(B("stu", 0, 64)), T.ohn[:], ALU.mult)
+    V("jg", GA * NK, ["stu", ("ohn", 0), ("ohn", 1)] + jk, ["mj"], "tt", T.mj[:], B("JW", 0, W).indirect(B("stu", 0, 64)), T.ohn[:], ALU.mult)
     mm = []
     for y in range(2):
         for r in range(16):
             mm.append((B("pj0", 64 * y, 64 * y + 64), sel(r, 1 - y), B("mj", 64 * r, 64 * r + 64), r == 0, r == 15, 64))
-    P("js", z1 + [("mj", 0), ("mj", 1)], ["pj0"], mm)
+    P("js", z1 + ["mj"], ["pj0"], mm)
     S("ln", 128, [], ["pj0", "t0"], T.t0[:], B("pj0", 0, 128), AF.Ln)
     V("li", 128, ["t0"], ["l0"], "ts", T.l0[:], T.t0[:], float(A), float(LOW), ALU.mult, ALU.add)
     for c in range(2):
@@ -409,35 +476,55 @@ def program(R, T, topo):
         walk(0, c)
     for c in range(2):
         tag[0] = (1, c, -1)
-        a0, lha, lhb, hit, dz = "A0%d" % c, "LHa%d" % c, "LHb%d" % c, "hit%d" % c, "dz%d" % c
-        V("hit", 16 * K, [("A0", c, t) for t in range(9)], [hit], "tt", B(hit, 0, 8 * K), B(a0, 0, 8 * K), B(a0, K, 9 * K), ALU.subtract)
-        V("lhb", 16 * K, [hit, lha], [(lhb, 1)], "tt", B(lhb, K, 9 * K), B(lha, 0, 8 * K), B(hit, 0, 8 * K), ALU.max)
-        V("dz", K, [("A0", c, 8)], [dz], "ts", B(dz, 0, K), B(a0, 8 * K, 9 * K), -1.0, 16.0, ALU.mult, ALU.add)
-        V("lhb", 2 * K, [dz] + yk, [(lhb, 0)], "tt", B(lhb, 0, K), B("LT", 512 + K * c, 512 + K * c + K), B(dz, 0, K), ALU.max)
+        aa, ea, eb, pw = "Aa%d" % c, "ea%d" % c, "eb%d" % c, "pw%d" % c
+        P("eb", ["Z2", "ones", "Ip", "Im", ea] + [(aa, t) for t in range(9)], [pw],
+          [(B(pw, 0, K), sh(0), B("ones", 0, K), True, False, K), (B(pw, 0, K), I["Im"], B(aa, 8 * K, 9 * K), False, True, K),
+           (B(pw, K, 9 * K), sh(0), B(ea, 0, 8 * K), True, False, 8 * K), (B(pw, K, 9 * K), I["Ip"], B(aa, 0, 8 * K), False, False, 8 * K),
+           (B(pw, K, 9 * K), I["Im"], B(aa, K, 9 * K), False, True, 8 * K)])
+        S("eb", 9 * K, [], [pw, eb], B(eb, 0, 9 * K), B(pw, 0, 9 * K), AF.Copy)
         gates(1, c)
-        vf, xa, eq, oy, pv, pj, pc = "vf%d" % c, "xa%d" % c, "eq%d" % c, "oy%d" % c, "pv%d" % c, "pj%d" % c, "pc%d" % c
-        P("g1", ["Z2", "G1"], [pj], [(B(pj, r, n, 16), sh(0), B("G1", 64 * r + K * c, 64 * r + K * c + K), True, True, K) for r in range(16)])
-        src, sk = B(vf, 0, n), vf
-        for i in range(4):
-            P("mx", [("ROT", i), sk], [pv], [(B(pv, 0, n), B("ROT", 128 * i, 128 * i + 128), src, True, True, n)])
-            if i < 3:
-                out = B(xa, n * (i % 2), n * (i % 2) + n)
-                V("mx", n, [sk], [pv, (xa, i % 2)], "tt", out, src, B(pv, 0, n), ALU.max)
-                src, sk = out, (xa, i % 2)
-        V("mx", n, [sk], [pv], "tt", B(pv, 0, n), src, B(pv, 0, n), ALU.max)
-        V("eq", n, [vf], [pv, eq], "tt", B(eq, 0, n), B(vf, 0, n), B(pv, 0, n), ALU.is_equal)
-        P("ltr", ["LTR", eq], [pv], [(B(pv, 0, n), T.LTR[:], B(eq, 0, n), True, True, n)])
-        V("oy", n, [eq], [pv, oy], "tt", B(oy, 0, n), B(eq, 0, n), B(pv, 0, n), ALU.is_gt)
-        V("jg", n, [oy], [pj, ("mj", c)], "tt", B("mj", n * c, n * c + n), B(oy, 0, n), B(pj, 0, n), ALU.mult)
+        vf, ax, am, eq, oy, pv, pj = "vf%d" % c, "ax%d" % c, "am%d" % c, "eq%d" % c, "oy%d" % c, "pv%d" % c, "pj%d" % c
+        P("m1", ["In", "ones"], [pj], [(B(pj, 0, n), I["In"], T.ones[:], True, False, n)])
+        src, sk, wd, pos = vf, vf, n, 0
+        for bi in range(4):
+            hf = wd // 2
+            mm = []
+            for j in range(2):
+                for k in range(2):
+                    q = 4 * bi + 2 * j + k
+                    mm.append((B(pv, hf * j, hf * j + hf), B("AM", 128 * q, 128 * q + 128), B(src, pos + hf * k, pos + hf * k + hf), k == 0, k == 1, hf))
+            P("mx", [("AM", 4 * bi + y) for y in range(4)] + [sk], [pv], mm)
+            S("mx", hf, [], [pv, ax], B(ax, 0, hf), B(pv, 0, hf), AF.Copy)
+            npos = 0 if bi == 0 else pos + wd
+            V("mx", hf, [ax], [pv, (am, bi)], "tt", B(am, npos, npos + hf), B(ax, 0, hf), B(pv, hf, 2 * hf), ALU.max)
+            src, sk, wd, pos = am, (am, bi), hf, npos
+        alone = OPT["eqv"]
+        mm = [] if alone else [(B(pv, 0, n), I["In"], B(vf, 0, n), True, False, n)]
+        mm += [(B(pv, K * r, K * r + K), B("RM", 128 * r, 128 * r + 128), B(am, pos, pos + K), alone, alone or r == 15, K) for r in range(16)]
+        P("rep", rmk + ["In", vf, sk], [pv], mm)
+        if alone:
+            V("eq", n, [vf], [pv, eq], "tt", B(eq, 0, n), B(vf, 0, n), B(pv, 0, n), ALU.is_equal)
+        else:
+            S("eq", n, [], [pv, eq], B(eq, 0, n), B(pv, 0, n), AF.Relu, bias=1.0, scale=-1.0)
+        P("ltr", ["M1", "Z2", eq, ("Gp", c)], [pj], [(B(pj, 0, n), T.M1[:], B(eq, 0, n), False, False, n), (B(pj, 0, n), sh(0), B("Gp", n * c, n * c + n), False, True, n)])
+        relu("m0", OPT["mjv"], n, [], [pj, ("X%d" % c, 1)], B("X%d" % c, n, 2 * n), B(pj, 0, n))
         tag[0] = (1, c, 0)
         series(1, c, 0)
-        pw = "pw%d" % c
+        P("oy", ["M1", eq], [pv], [(B(pv, 0, n), T.M1[:], B(eq, 0, n), True, True, n)])
+        relu("oy", OPT["oyv"], n, [], [pv, oy], B(oy, 0, n), B(pv, 0, n))
         P("y1", ["Z1x", oy], [pw], [(B(pw, 0, K), sel(r, 0, "Z1x"), B(oy, r, n, 16), r == 0, r == 15, K) for r in range(16)])
-        S("y1", K, [], [pw, ("y1l", c)], B("y1l", K * c, K * c + K), B(pw, 0, K), AF.Copy)
+        S("y1", K, [], [pw, ("y1l", c)], B("L1", 576 + K * c, 576 + K * c + K), B(pw, 0, K), AF.Copy)
     tag[0] = (1, 1, -1)
-    P("l1", ["Z2", ("LHb0", 1), ("LHb1", 1)], ["pw1"],
-      [(B("pw1", 64 * d + K * c, 64 * d + K * c + K), sh(0), B("LHb%d" % c, K * (d + 1), K * (d + 2)), True, True, K) for d in range(8) for c in range(2)])
-    S("l1", 512, [], ["pw1", "L1"], T.L1[:], B("pw1", 0, 512), AF.Copy)
+    for pw, blocks in (("pw0", [0]), ("pw1", range(1, 9))):
+        mm = []
+        for i, b in enumerate(blocks):
+            u = -(b - 1) % N if b else 8
+            mm.append((B(pw, 64 * i, 64 * i + 64), sh(1 - b if b else 0), B("LT", 64 * u, 64 * u + 64), True, False, 64))
+            for c in range(2):
+                mm.append((B(pw, 64 * i + K * c, 64 * i + K * c + K), I["I16"], B("eb%d" % c, K * b, K * b + K), False, c == 1, K))
+        P("l1", ["Z2", "I16", "eb0", "eb1"] + ltk + yk, [pw], mm)
+        m = 64 * len(blocks)
+        S("l1", m, [], [pw, ("L1", pw)], B("L1", 64 * blocks[0], 64 * blocks[0] + m), B(pw, 0, m), AF.Copy)
     for c in range(2):
         walk(1, c)
     tag[0] = (1, 1, 10)
@@ -447,25 +534,31 @@ def program(R, T, topo):
         xo[sem].append((sem, len(xo[sem])))
         DM(sem, nbytes, reads, [xo[sem][-1]], out, in_)
 
-    for pair in PAIRS[1]:
-        ts_ = [t for t in pair if t > 1]
-        a, z = 64 * (ts_[0] - 2), 64 * (ts_[-1] - 1)
-        ak = [("A1", c, t) for c in range(2) for t in range(ts_[0] - 1, ts_[-1] + 1)]
-        V("yl", 2 * (z - a), ak, [("hb", a)], "tt", B("hb", a, z), B("A1", a + 64, z + 64), B("A1", a + 128, z + 128), ALU.subtract)
-        V("yl", 2 * (z - a), [("hb", a), "L1"], [("YL", a)], "tt", B("YL", a, z), B("hb", a, z), B("L1", a, z), ALU.max)
-        for t in ts_:
-            d = t - 2
+    for j, pair in enumerate(PAIRS[1]):
+        pw, a = "pw%d" % (j % 2), 64 * (pair[0] - 1)
+        last = pair[-1] == 9
+        terms = [(t - 1, t) for t in pair] + ([(0, 9)] if last else [])
+        mm = [(B(pw, 0, 64 * len(terms)), sh(0), B("L1", a, a + 64 * len(terms)), True, False, 64 * len(terms))]
+        reads = ["Z2", "Ib", ("L1", "pw0"), ("L1", "pw1")] + ([("y1l", 0), ("y1l", 1)] if last else [])
+        for i, (x, y) in enumerate(terms):
+            for c in range(2):
+                out = B(pw, 64 * i + K * c, 64 * i + K * c + K)
+                mm.append((out, sh(-1), akey(1, c, x)[0], False, False, K))
+                mm.append((out, I["Ib"], akey(1, c, y)[0], False, i + 1 == len(terms) and c == 1, K))
+                reads += [akey(1, c, x)[1], akey(1, c, y)[1]]
+        P("yl", reads, [pw], mm)
+        m = 64 * len(terms)
+        V("yl", m, [], [pw, ("YL", a)], "ts", B("YL", a, a + m), B(pw, 0, m), 16.0, None, ALU.min)
+        for t in pair:
+            d, b = t - 2, 64 * (t - 1)
+            if t == 1:
+                stage("xe", 16384, [("YL", a)], T.ZE[0:8, 0:16, :], B("YL", 0, 64))
+                continue
             for i0, i1, p0 in runs(0, N, d):
                 out = T.ZE[p0:p0 + i1 - i0, 16 * (7 - d):16 * (8 - d), :] if d < 7 else T.ZT[p0:p0 + i1 - i0, 0:64, :]
-                stage("xe" if d < 7 else "xt", 2048 * (i1 - i0), [("YL", a)], out, T.YL[16 * i0:16 * i1, 64 * d:64 * d + 64])
-    for c in range(2):
-        a, dz, hit = K * c, "dz%d" % c, "hit%d" % c
-        V("yi", K, [("A1", c, 1)], [dz], "ts", B(dz, 0, K), akey(1, c, 1)[0], -1.0, 16.0, ALU.mult, ALU.add)
-        V("yi", 2 * K, [dz, ("LHb%d" % c, 0)], [("YI", 0, c)], "tt", B("YI", a, a + K), B("LHb%d" % c, 0, K), B(dz, 0, K), ALU.max)
-    stage("xe", 16384, [("YI", 0, 0), ("YI", 0, 1)], T.ZE[0:8, 0:16, :], B("YI", 0, 64))
-    V("yi", 64, [("A1", 0, 9), ("A1", 1, 9)], [("hit0", 1), "hit0"], "ts", B("hit0", 0, 64), B("A1", 576, 640), -1.0, 16.0, ALU.mult, ALU.add)
-    V("yi", 128, [("hit0", 1), ("y1l", 0), ("y1l", 1)], [("YI", 1)], "tt", B("YI", 64, 128), T.y1l[:], B("hit0", 0, 64), ALU.max)
-    stage("xt", 16384, [("YI", 1)], T.ZT[0:8, 64:128, :], B("YI", 64, 128))
+                stage("xe" if d < 7 else "xt", 2048 * (i1 - i0), [("YL", a)], out, T.YL[16 * i0:16 * i1, b:b + 64])
+        if last:
+            stage("xt", 16384, [("YL", a)], T.ZT[0:8, 64:128, :], B("YL", 576, 640))
     vn = []
     for c in range(2):
         vf = "vf%d" % c
@@ -528,7 +621,7 @@ def order(ops):
     urge = []
     for k, o in enumerate(ops):
         name, tg = o["tag"]
-        urge.append(prio[k] + o["bonus"] + URGE.get((name,) + tg[:2] if tg else name, 0))
+        urge.append(prio[k] + o["bonus"] + URGE.get((name,) + tg[:2] if tg else name, 0) + (URGE.get((name,) + tg, 0) if tg else 0))
     left = [len(o["d"]) for o in ops]
     ready = [0.0] * cnt
     cand = {}

@@ -5,7 +5,7 @@ from concourse.mybir import AluOpType, ActivationFunctionType
 ALU, AF = AluOpType, ActivationFunctionType
 N, W, NK = 8, 4608, 1024
 BW = W // N
-n, K = 512, 32
+n, K, L = 512, 32, 64
 PER = 80.0
 FO = 70
 D = int(PER) * FO
@@ -15,76 +15,62 @@ A = PER / math.log(2.0)
 LOW = 63.8 * PER + 0.35
 WID = D + W
 OFF = [[0, 0, 1, 2, 3, 4, 5, 6, 7], [0, 0, 0, 1, 2, 3, 4, 5, 6, 7]]
-PAIRS = [[(1,), (2, 3), (4, 5), (6, 7), (8,)], [(1, 2), (3, 4), (5, 6), (7, 8), (9,)]]
-CALLS = {"J": [[1, 2], [3, 4], [5, 6, 7]], "C": [[1, 2, 3, 4], [5, 6, 7]]}
 NCC = 3
 B16, F32, I32, U16 = "bfloat16", "float32", "int32", "uint16"
 
 SCRATCH = {}
 SEMAPHORES = ["kpe", "kv", "ks", "kg", "ls", "xl", "xs", "rl", "rs", "ll", "lst", "ls0", "jo", "co", "xy", "ry", "ly", "xe", "re", "xv", "rv", "xt", "rt", "stores"]
 SEMAPHORES += ["lj%d" % _b for _b in range(N)]
-for _k in range(len(CALLS["J"])):
-    SEMAPHORES += ["rj%d" % _k, "jr%d" % _k]
-for _k in range(len(CALLS["C"])):
-    SEMAPHORES += ["xc%d" % _k, "rc%d" % _k, "cr%d" % _k]
+SEMAPHORES += ["%s%d" % (_x, _k) for _x in ("rj", "jr", "xc", "rc", "cr") for _k in range(4)]
 
 
 def sb(name, cols, dtype=B16):
     SCRATCH[name] = ("sbuf", [128, cols], dtype)
 
 
-SCRATCH["ZL"] = ("dram", [15, 128, 64], B16)
-SCRATCH["ZS"] = ("dram", [15, 128, 16], B16)
-SCRATCH["ZJ"] = ("dram", [7, 128, BW], B16)
-SCRATCH["ZC"] = ("dram", [7, 128, BW], B16)
-SCRATCH["XC"] = ("dram", [8, 128, BW], B16)
-SCRATCH["ZY"] = ("dram", [15, 128, 8], B16)
-SCRATCH["ZE"] = ("dram", [15, 128, 64], B16)
-SCRATCH["ZV"] = ("dram", [15, 128, 128], B16)
-SCRATCH["ZT"] = ("dram", [15, 128, 16], B16)
-sb("JW", WID)
-sb("CW", WID)
-sb("jmi", W, I32)
-sb("jmf", W, F32)
-sb("JS", W)
-SCALED = {"I64": (64.0, 1), "I32": (32.0, -1), "I16": (16.0, 0), "I8": (8.0, 0), "In": (-1.0, 0), "Ib": (-1.0, -1), "Ip": (1.0 / 16, -1), "Im": (-1.0 / 16, -1)}
-for _k, _c in (("ones", n), ("Z1", 256), ("Z2", 256), ("ZF", 256), ("ZN", 256), ("Z1x", 256), ("IDT", 32), ("BDa", 128), ("BD", 128), ("LTR", 128), ("M1", 128),
-               ("RM", 2048), ("AM", 2048), ("IS", 128 * len(SCALED)), ("K16", 32), ("b8a", 8), ("b8", 8), ("LT", 576), ("eR", 512), ("OH", 9 * NK), ("ohn", NK),
-               ("G1", NK), ("Gp", NK), ("mj", NK), ("L1", 640), ("YL", 640), ("VN", NK), ("stc", 128), ("std", 128)):
+for _k, _s, _c in (("ZL", 15, 64), ("ZS", 15, 16), ("ZY", 15, 8), ("ZJ", 7, BW), ("ZC", 7, BW), ("XC", 8, BW), ("ZE", 15, 64), ("ZV", 15, 128), ("ZT", 15, 16)):
+    SCRATCH[_k] = ("dram", [_s, 128, _c], B16)
+SCALED = {"I64": 64.0, "I16": 16.0, "In": -1.0, "I8": 8.0, "J8": -8.0, "I512": 512.0, "Ip": 0.5, "Im": -0.5}
+for _k, _c in (("JW", WID), ("CW", WID), ("JS", W), ("ones", n), ("Z1", 256), ("Z2", 256), ("ZF", 256), ("ZN", 256), ("Z1x", 256), ("IDT", 32), ("BDa", 128),
+               ("BD", 128), ("LTR", 128), ("M1", 128), ("RM", 2048), ("AM", 2048), ("ROT", 512), ("rta", 512), ("IS", 128 * len(SCALED)), ("K16", L), ("b8a", 8),
+               ("b8", 8), ("LT", 9 * L), ("LR", 512), ("LM", 1088), ("eR", 512), ("OH", 9 * NK), ("ohn", NK), ("G1", NK), ("Gp", NK), ("mj", NK), ("L1", 10 * L),
+               ("YL", 10 * L), ("VN", NK), ("stc", 128), ("std", 128), ("cc", NCC * NK), ("sg", 2 * NK), ("va", 8 * NK), ("vb", 9 * NK), ("vf", NK), ("eq", NK),
+               ("oy", NK), ("mb", L), ("cb", L), ("Aa", 9 * L), ("Ab", 10 * L), ("ea", 8 * L), ("eb", 9 * L), ("ha", 8 * L), ("hc", 9 * L)):
     sb(_k, _c)
-sb("stf", 128, F32)
-sb("stg", 128, F32)
-sb("ipi", 2, I32)
-sb("ipj", 2, I32)
-sb("ipf", 2, F32)
-sb("io32", 32, F32)
-sb("sti", 128, I32)
-sb("stu", 128, U16)
-sb("LTf", 576, F32)
-sb("LTu", 576, U16)
-sb("t0", 128, F32)
-sb("l0", 128, U16)
+for _k, _c, _d in (("jmi", W, I32), ("jmf", W, F32), ("stf", 128, F32), ("stg", 128, F32), ("ipi", 2, I32), ("ipj", 2, I32), ("ipf", 2, F32), ("io", L, F32),
+                   ("sti", 128, I32), ("stu", 128, U16), ("LTu", 9 * L, U16), ("tt", 2 * L, F32), ("li", 20 * 2 * L, U16), ("lv", 2 * L, U16)):
+    sb(_k, _c, _d)
 for _c in range(2):
-    for _k, _w in (("cc", NCC * n), ("X", 5 * n), ("va", 8 * n), ("vb", 9 * n), ("vf", n), ("ax", n // 2), ("am", n), ("eq", n), ("oy", n), ("mb", K),
-                   ("Aa", 9 * K), ("Ab", 10 * K), ("ea", 8 * K), ("eb", 9 * K), ("ha", 8 * K), ("hc", 9 * K)):
-        sb("%s%d" % (_k, _c), _w)
-    sb("tt%d" % _c, 2 * K, F32)
-    sb("li%d" % _c, 2 * 10 * 2 * K, U16)
-    sb("lv%d" % _c, 2 * K, U16)
+    sb("ax%d" % _c, n // 2)
+    sb("am%d" % _c, n)
     for _k in ("pv", "pw", "pj", "pc"):
         SCRATCH["%s%d" % (_k, _c)] = ("psum", [128, 512], F32)
 
-VF, SF, CY, PCY, PF, GA, WAKE, SELF, GAP = 45.0, 65.0, 0.95, 0.5, 20.0, 1.5, 90.0, 60.0, 150.0
-HOP, LAT, GBW, CALL = 2000.0, 1800.0, 250.0, 900.0
+VF, SF, CY, PCY, PF, GA, WAKE, SELF, GAP = 45.0, 65.0, 0.88, 0.46, 20.0, 1.45, 90.0, 60.0, 150.0
+HOP, LAT, GBW, CALL, ROW = 2000.0, 1800.0, 295.0, 900.0, 17.0
+ROWS = {"ll": 1024, "ly": 128, "ls": 256, "xs": 256, "lj": 4 * BW, "jo": 2 * BW, "xe": 128, "xt": 128, "xv": 2048, "rj": 2 * BW}
 FIRST = 1e6
-OPT = {"ohv": (8,), "signv": (), "cgv": (), "dupv": 2, "dupg": 0, "permv": 11, "pace": [("JS", 0), "rj1", "jr0"], "deep": 3, "eqv": True, "mjv": True, "oyv": False, "vfv": (),
-       "merge": [[(7, 4), (9, 3)], [(4, 3), (4, 3)]]}
-OPT = {'ohv': (3, 4, 5, 7, 8), 'signv': ((0, 0, 2), (0, 0, 7), (0, 1, 7), (0, 1, 8), (1, 0, 6), (1, 1, 7), (1, 1, 9)), 'cgv': ((0, 0, 0), (0, 0, 2), (0, 0, 8), (1, 0, 0)), 'dupv': 5, 'dupg': 1, 'permv': 10, 'pace': ['rj1', 'rj2', 'jr1'], 'deep': 3, 'eqv': True, 'mjv': True, 'oyv': False, 'vfv': ((0, 1),), 'merge': [[(9, 4), (7, 3)], [(4, 3), (4, 3)]]}
-URGE = {'oh': -20000, 'G1': -15000, 'Gp': -15000, ('l1', 1, 1): -10000, ('oy', 1, 0): -10000, ('oy', 1, 1): -10000, ('y1', 1, 0): -10000, ('y1', 1, 1): -10000, ('cg', 0, 0): 3000, ('add', 0, 0): 3000, ('clip', 0, 0): 3000, ('sg', 0, 0): 3000, ('cnt', 0, 0): 3000, ('nc', 0, 0): 3000, ('al', 0, 0): 3000, ('vf', 0, 0): 4000, ('pick', 0, 0): 4000, ('lv', 0, 0): 4000, ('jg', 0, 0): 6000, ('js', 0, 0): 6000, ('ln', 0, 0): 6000, ('li', 0, 0): 6000, ('mb', 0, 0): 6000, ('eb', 1, 0): 4000, ('eb', 1, 1): 4000, ('h', 1, 0): 4000, ('h', 1, 1): 4000, ('m1', 1, 0): 4000, ('m1', 1, 1): 4000, ('mx', 1, 0): 4000, ('mx', 1, 1): 4000, ('rep', 1, 0): 4000, ('rep', 1, 1): 4000, ('eq', 1, 0): 4000, ('eq', 1, 1): 4000, ('ltr', 1, 0): 4000, ('ltr', 1, 1): 4000, ('m0', 1, 0): 4000, ('m0', 1, 1): 4000, ('jg', 1, 0): 6000, ('jg', 1, 1): 6000, ('js', 1, 0): 6000, ('js', 1, 1): 6000, ('ln', 1, 0): 6000, ('ln', 1, 1): 6000, ('li', 1, 0): 6000, ('li', 1, 1): 6000, ('mb', 1, 0): 6000, ('mb', 1, 1): 6000, ('jg', 1, 1, 2): -4000, 'JS': 200, ('li', 0, 0, 8): -8000, ('clip', 0, 1, 2): -200, ('li', 0, 1, 1): 200, ('mb', 1, 0, 0): 500, ('pick', 0, 1): -8000, 'rs': -1500, ('js', 1, 0, 3): 1000, ('lv', 0, 1): 500, ('mb', 1, 0, 8): -2000, 'stu': -12000, ('cg', 0, 1): -500, ('cg', 1, 1): -1000, ('add', 1, 1): -1000, ('clip', 1, 1): -1000, ('sg', 1, 1): -1000, ('cnt', 1, 1): -1000, ('nc', 1, 1): -1000, ('al', 1, 1): -1000, ('jg', 0, 0, 4): 4000, ('nc', 0, 1, 3): 2000, ('sg', 1, 1, 4): 8000, ('al', 1, 0): -200, ('cnt', 0, 0, 5): 2000, ('mb', 1, 1, 4): -4000, ('li', 1, 1, 8): -8000, ('sg', 1, 1, 7): -200}
+PASSES = 2
+HOLD = {}
+OPT = {"J": ((0, 1), (2, 3)), "C": ((0,), (1,), (2, 3)), "pace": ["rj1"] * 4, "deep": 3, "old": (), "fly": (0, 1), "one": (), "ohv": ((0, 0), (1, 0), (0, 1), (1, 1), (0, 2), (1, 2)),
+       "dupv": 4, "permv": 9, "eqv": (0, 1), "mjv": (0,), "oyv": (), "split": ((0, 1), (0, 2), (0, 3), (0, 4), (0, 5)), "cg": {}, "sg": {}, "vf": ("h", "h")}
+URGE = {}
+OPT = {'J': ((0, 1), (2, 3)), 'C': ((0,), (1,), (2, 3)), 'pace': ['rj1', 'rj1', 'rj1', 'rj1'], 'deep': 3, 'old': (), 'fly': (0, 1), 'one': ((0, 0), (1, 0), (1, 1)), 'ohv': ((0, 0), (0, 2), (0, 3), (1, 0), (1, 2)), 'dupv': 4, 'permv': 10, 'eqv': (0, 1), 'mjv': (0, 1), 'oyv': (0,), 'split': ((0, 1), (0, 2), (0, 3), (0, 4), (0, 5), (0, 6), (1, 2), (1, 6)), 'cg': {(0, 0): 'h', (0, 1): 'h', (0, 4): 'ss', (0, 5): 'ss', (0, 6): 'ss', (0, 7): 'ss', (0, 8): 'ss', (1, 9): 'h', (1, 0): 'h', (1, 1): 'h', (1, 6): 'ss', (1, 7): 'ss'}, 'sg': {(0, 2): 'h', (0, 3): 'v', (0, 6): 'vv', (0, 7): 'h', (0, 8): 'h', (1, 8): 'h', (1, 9): 'h', (0, 4): 'h', (1, 5): 'ss', (1, 3): 'ss', (1, 7): 'ss', (0, 1): 'ss', (0, 5): 'vv'}, 'vf': ('h', 'h')}
+URGE = {'ltf': 29500, ('li', 0, 2): 2700, ('mb', 0, 2): 2700, ('sg', 0, 2): 200, ('jg', 0, 1): 13000, ('ln', 0, 1): 12000, ('li', 0, 1): 12000, ('ln', 0, 0): 1200, ('mb', 1, 2): 2000, ('cg', 1, 2): -2000, ('sg', 1, 2): -2000, ('pick', 1, 2): -2000, ('clip', 0, 0, 5): 4000, ('oh', 2, 0, 0): 8000, ('jg', 0, 0): 400, ('li', 0, 0): 200, ('clip', 1, 1): -3500, ('sg', 1, 2, 6): -500, ('clip', 1, 0): -8000, ('mb', 0, 1): 8000, ('add', 1, 1): 4500, ('mb', 1, 0): -500, ('jg', 0, 2): 500, ('ln', 0, 2): 500}
+HOLD = {'lj2': 4000}
+OPT["G1"] = "ss"
+OPT = {'J': ((0, 1), (2, 3)), 'C': ((0,), (1,), (2, 3)), 'pace': ['rj1', 'rj1', 'rj1', 'rj1'], 'deep': 3, 'old': (), 'fly': (1,), 'one': ((0, 0), (1, 0), (1, 1)), 'ohv': ((0, 0), (0, 3), (0, 4), (1, 0), (1, 3)), 'dupv': 2, 'permv': 10, 'eqv': (0,), 'mjv': (0, 1), 'oyv': (0,), 'split': ((0, 1), (0, 2), (0, 3), (0, 4), (0, 5), (1, 0), (1, 1), (1, 2), (1, 3), (1, 6)), 'cg': {(0, 0): 'h', (0, 1): 'h', (0, 4): 'ss', (0, 7): 'ss', (0, 8): 'ss', (1, 9): 'h', (1, 0): 'ss', (1, 1): 'h', (1, 6): 'ss', (1, 7): 'ss'}, 'sg': {(0, 2): 'v', (0, 3): 'h', (0, 6): 'vv', (0, 7): 'h', (0, 8): 'vv', (1, 8): 'h', (1, 9): 'h', (1, 5): 'ss', (1, 3): 'ss', (1, 7): 'ss', (0, 5): 'vv'}, 'vf': ('h', 'h'), 'G1': 'ss'}
+URGE = {'ltf': 2000000, ('li', 0, 2): 2700, ('mb', 0, 2): 2700, ('ln', 0, 1): 11200, ('ln', 0, 0): 1200, ('mb', 1, 2): 4000, ('cg', 1, 2): -1000, ('sg', 1, 2): -1000, ('clip', 0, 0, 5): 8000, ('clip', 1, 0): -8000, ('add', 1, 1): 4500, ('jg', 0, 2): 500, ('ln', 0, 2): 2500, 'eR': 30000, ('sg', 0, 2, 1): 500, ('jg', 1, 0): -500, ('jg', 0, 1): -800, ('li', 0, 1, 4): -1000, ('ln', 0, 2, 8): -8000, ('li', 1, 1): 4000, ('add', 1, 0, 5): -4000, ('li', 1, 0): 4000, ('sg', 0, 2): -200, ('li', 1, 2, 7): 2000, ('mb', 0, 0, 5): 4000, ('cg', 0, 2, 4): -1000, ('js', 1, 2): 2000, ('ln', 1, 2): 2000, ('li', 1, 2): 2000, ('clip', 1, 2): 2000, ('cnt', 1, 2): 2000, ('nc', 1, 2): 2000, ('vf', 1, 2): 2000, ('js', 0, 1): -1000, ('li', 0, 1): -1000, ('mb', 0, 1): -1000, ('sg', 1, 2, 4): 4000, ('mb', 0, 2, 6): 4000}
+HOLD = {}
 
 
 def program(R, T, topo):
     ops = []
+    dies = [topo.die(c) for c in T.cores]
+    pairs = [[x, y] for x in range(1, N) for y in range(x + 1, N) if all(dies[(r + x) % N] != dies[(r + y) % N] for r in range(N))]
+    alone = [x for x in range(1, N) if not any(x in p for p in pairs)]
+    parts = pairs + [alone]
+    CALLS = {k: [[x for i in c for x in parts[i]] for c in OPT[k]] for k in "JC"}
     tag = [None]
     me = T.cores[R]
 
@@ -114,13 +100,16 @@ def program(R, T, topo):
         add("g", 170 + 1.9 * el, reads, [key], [call], sem="kg", name="const")
 
     def pick(key, out, in_, pat, cmp_, base, cm, el, src):
-        G(key, el, [src], lambda g: g.affine_select(out, in_, pat, cmp_, 0.0, base, cm))
+        G(key, el, src, lambda g: g.affine_select(out, in_, pat, cmp_, 0.0, base, cm))
+
+    def lane(sem, nbytes):
+        return nbytes / GBW + ROW * max(1.0, nbytes / ROWS.get(sem[:2], 8192) / 16)
 
     def DM(sem, nbytes, reads, writes, out, in_, bonus=0.0):
-        add("sync", 70.0, reads, writes, [lambda g: g.sync.dma_start(out, in_)], sem=sem, lat=LAT, tail=nbytes / GBW, dma=True, bonus=bonus, name=sem)
+        add("sync", 70.0, reads, writes, [lambda g: g.sync.dma_start(out, in_)], sem=sem, lat=LAT, tail=lane(sem, nbytes), dma=True, bonus=bonus, name=sem)
 
-    def send(aheads, sem, nbytes, reads, landing, src, dst, bonus=0.0):
-        far = [x for x in aheads if topo.die(T.cores[(R + x) % N]) != topo.die(me)]
+    def send(aheads, sem, nbytes, reads, src, dst, bonus=0.0):
+        far = [x for x in aheads if dies[(R + x) % N] != dies[R]]
         near = [x for x in aheads if x not in far]
         turn = []
         while far or near:
@@ -134,12 +123,14 @@ def program(R, T, topo):
             core = T.cores[(R + x) % N]
             rid, pid, _ = topo.addr(core)
             eng = topo.engines(me, core)[i::ways]
-            per = len(eng)
+            if len(turn) < ways and x in alone:
+                eng = eng + topo.engines(me, core)[ways - 1::ways]
+            per += len(eng)
             trs.append(RemoteDMATransfer(dst_ids=[DstId(rid=rid, pnc=pid)], dma_engine_mask=sum(1 << e for e in eng), remote_sem=T.sem[sem], src=src(x), dst=dst(x)))
         k = add("g", CALL, reads, [], [lambda g: g.remote_dma_fused(trs, local_sem=T.sem.ls)], sem="remote", bonus=bonus, name=sem)
-        j = add("net", 0.0, [], [landing], [], sem=sem, lat=HOP, tail=nbytes * len(aheads) / GBW, name=sem)
+        j = add("net", 0.0, [], [sem], [], sem=sem, lat=HOP, tail=lane(sem, nbytes * len(aheads)), name=sem)
         ops[j]["after"] = k
-        ops[k]["cnt"] = ops[j]["cnt"] = per * len(aheads)
+        ops[k]["cnt"] = ops[j]["cnt"] = per
 
     def runs(lo, hi, first):
         out, i = [], lo
@@ -149,6 +140,18 @@ def program(R, T, topo):
             out.append((i, z, at))
             i = z
         return out
+
+    def spans(c):
+        out = []
+        for x in sorted(c):
+            if out and out[-1][1] == x:
+                out[-1] = (out[-1][0], x + 1)
+            else:
+                out.append((x, x + 1))
+        return out
+
+    def both(*key):
+        return [key + (0,), key + (1,)]
 
     ALL = list(range(1, N))
     xl, xs, xy = [], [], []
@@ -165,80 +168,80 @@ def program(R, T, topo):
     for i0, i1, g0 in runs(0, N, R):
         xs.append(("xs", i0))
         DM("xs", 4096 * (i1 - i0), ["stc"], [xs[-1]], T.ZS[7 + i0:7 + i1], T.stc[16 * g0:16 * (g0 + i1 - i0), :], bonus=8.5 * FIRST)
-    send(ALL, "rl", 16384, xl, "rl", lambda x: T.ZL[7 + x], lambda x: T.ZL[7 - x], bonus=9 * FIRST)
-    send(ALL, "ry", 2048, xy, "ry", lambda x: T.ZY[7 + x], lambda x: T.ZY[7 - x], bonus=8.5 * FIRST)
-    send(ALL, "rs", 4096, xs, "rs", lambda x: T.ZS[7 + x], lambda x: T.ZS[7 - x], bonus=6 * FIRST)
-    ltk = [("LT", u) for u in range(8)]
-    yk = [("LT", 8)]
-    for u in range(8):
-        DM("ll", 16384, xl + ["rl"], [("LT", u)], B("LT", 64 * u, 64 * u + 64), T.ZL[0:8, 16 * u:16 * u + 16, :], bonus=8 * FIRST)
-    DM("ly", 16384, xy + ["ry"], yk, B("LT", 512, 576), T.ZY[0:8], bonus=8 * FIRST)
+    send(ALL, "rl", 16384, xl, lambda x: T.ZL[7 + x], lambda x: T.ZL[7 - x], bonus=9 * FIRST)
+    send(ALL, "ry", 2048, xy, lambda x: T.ZY[7 + x], lambda x: T.ZY[7 - x], bonus=8.5 * FIRST)
+    send(ALL, "rs", 4096, xs, lambda x: T.ZS[7 + x], lambda x: T.ZS[7 - x], bonus=6 * FIRST)
+    DM("ll", 131072, xl + ["rl"], ["LR"], T.LR[:], T.ZL[0:8], bonus=8 * FIRST)
+    DM("ly", 16384, xy + ["ry"], ["LY"], B("LT", 8 * L, 9 * L), T.ZY[0:8], bonus=8 * FIRST)
     DM("lst", 32768, xs + ["rs"], ["std"], T.std[:], T.ZS[0:8], bonus=7 * FIRST)
     jorder = [x for c in CALLS["J"] for x in c] + [0]
     for i, x in enumerate(jorder):
         g0, a, z = (R + x) % N, BW * x, BW * x + BW
-        DM("lj%d" % x, 128 * BW * 4, [("jmi", jorder[i - OPT["deep"]])] if i >= OPT["deep"] else [], [("jmi", x)], B("jmi", a, z), T.jm[16 * g0:16 * g0 + 16, :], bonus=FIRST * (8 - 0.1 * i))
+        DM("lj%d" % x, 128 * BW * 4, [("jmi", y) for y in jorder[i - OPT["deep"]:i - OPT["deep"] + 1] if i >= OPT["deep"]], [("jmi", x)], B("jmi", a, z),
+           T.jm[16 * g0:16 * g0 + 16, :], bonus=FIRST * (8 - 0.1 * i))
         V("jmf", BW, [("jmi", x)], [("jmf", x)], "copy", B("jmf", a, z), B("jmi", a, z))
         ops[-1]["bonus"] = FIRST
         S("JS", BW, [("jmf", x)], [("JS", x)], B("JS", a, z), B("jmf", a, z), AF.Exp, bias=float(-LOW * SC), scale=float(SC))
         ops[-1]["bonus"] = FIRST
     jk = ["jo"]
     for k, c in enumerate(CALLS["J"]):
-        send(c, "rj%d" % k, 128 * BW * 2, [("JS", x) for x in c], "rj%d" % k, lambda x: B("JS", BW * x, BW * x + BW), lambda x: T.ZJ[7 - x], bonus=7 * FIRST)
-        p0, p1 = 7 - max(c), 8 - min(c)
-        DM("jr%d" % k, 128 * BW * 2 * len(c), ["rj%d" % k], ["jr%d" % k], T.JW[16 * p0:16 * p1, 0:W], T.ZJ[p0:p1], bonus=7 * FIRST)
-        jk.append("jr%d" % k)
+        send(c, "rj%d" % k, 128 * BW * 2, [("JS", x) for x in c], lambda x: B("JS", BW * x, BW * x + BW), lambda x: T.ZJ[7 - x], bonus=(7 - 0.1 * k) * FIRST)
+        for lo, hi in spans(c):
+            jk.append(("jr", lo))
+            DM("jr%d" % k, 128 * BW * 2 * (hi - lo), ["rj%d" % k], [jk[-1]], T.JW[16 * (8 - hi):16 * (8 - lo), 0:W], T.ZJ[8 - hi:8 - lo], bonus=(7 - 0.1 * k) * FIRST)
     DM("jo", 128 * BW * 2, [("JS", 0)], ["jo"], T.JW[112:128, 0:W], B("JS", 0, BW), bonus=7 * FIRST)
-    ck = ["co", "cz"]
+    ck = ["co"]
     for k, c in enumerate(CALLS["C"]):
-        xk, pace = [], [OPT["pace"][k]]
-        for i0, i1, g0 in runs(min(c), max(c) + 1, R):
-            xk.append(("xc", i0))
-            DM("xc%d" % k, 128 * BW * 2 * (i1 - i0), pace, [xk[-1]], T.XC[i0:i1], T.cf[16 * g0:16 * (g0 + i1 - i0), :], bonus=3 * FIRST)
-        send(c, "rc%d" % k, 128 * BW * 2, xk, "rc%d" % k, lambda x: T.XC[x], lambda x: T.ZC[7 - x], bonus=3 * FIRST)
-        p0, p1 = 7 - max(c), 8 - min(c)
-        DM("cr%d" % k, 128 * BW * 2 * len(c), ["rc%d" % k], ["cr%d" % k], T.CW[16 * p0 + 16:16 * p1 + 16, 0:W], T.ZC[p0:p1], bonus=3 * FIRST)
-        ck.append("cr%d" % k)
+        xk, bonus = [], (3 - 0.1 * k) * FIRST
+        for lo, hi in spans(c):
+            for i0, i1, g0 in runs(lo, hi, R):
+                xk.append(("xc", i0))
+                DM("xc%d" % k, 128 * BW * 2 * (i1 - i0), [OPT["pace"][k]], [xk[-1]], T.XC[i0:i1], T.cf[16 * g0:16 * (g0 + i1 - i0), :], bonus=bonus)
+        send(c, "rc%d" % k, 128 * BW * 2, xk, lambda x: T.XC[x], lambda x: T.ZC[7 - x], bonus=bonus)
+        for lo, hi in spans(c):
+            ck.append(("cr", lo))
+            DM("cr%d" % k, 128 * BW * 2 * (hi - lo), ["rc%d" % k], [ck[-1]], T.CW[16 * (9 - hi):16 * (9 - lo), 0:W], T.ZC[8 - hi:8 - lo], bonus=bonus)
     DM("co", 128 * BW * 2, [OPT["pace"][-1]], ["co"], T.CW[0:16, 0:W], T.cf[16 * R:16 * R + 16, :], bonus=2 * FIRST)
     V("c", 256, [], ["ones"], "set", T.ones[:], 1.0)
     V("c", 128, [], ["Z10"], "set", T.Z1[:], 0.0)
     V("c", (D - W) // 2, [], ["jz"], "set", B("JW", W, D), 0.0)
     for i in range(4):
+        ck.append(("cz", i))
         V("c", D // 8, [], [("cz", i)], "set", B("CW", W + D // 4 * i, W + D // 4 * (i + 1)), 0.0)
-    ck = [x for x in ck if x != "cz"] + [("cz", i) for i in range(4)]
-    for c in range(2):
-        for a in ("Aa%d" % c, "Ab%d" % c):
-            V("c", 32, [], [(a, 0)], "set", B(a, 0, K), 16.0)
+    for a in ("Aa", "Ab"):
+        V("c", 32, [], [(a, 0)], "set", B(a, 0, L), 1.0)
     G("ipi", 2, [], lambda g: g.iota(T.ipi[:], [[0, 2]], 0, 1))
-    G("io32", 32, [], lambda g: g.iota(T.io32[:], [[1, 32]], 0, 0, allow_small_or_imprecise_dtypes=True))
+    G("io", L, [], lambda g: g.iota(T["io"][:], [[1, L]], 0, 0, allow_small_or_imprecise_dtypes=True))
     V("c", 2, ["ipi"], ["ipj"], "ts", T.ipj[:], T.ipi[:], 15, None, ALU.bitwise_and)
     V("c", 2, ["ipj"], ["ipf"], "copy", T.ipf[:], T.ipj[:])
     row = T.ipf[:, 0:1]
-    V("c", 32, ["io32", "ipf"], ["IDT"], "ts", T.IDT[:], T.io32[:], row, None, ALU.is_equal)
-    V("c", 32, ["io32"], ["K16"], "ts", T.K16[:], T.io32[:], 16.0, None, ALU.mult)
-    pick("Z2", T.Z2[:], T.ones[:, 0:256], [[0, 2], [-1, 128]], ALU.is_equal, 0, 1, 256, "ones")
-    pick("b8a", T.b8a[:], T.ones[:, 0:8], [[-16, 8]], ALU.is_ge, 0, 1, 8, "ones")
-    pick("b8", T.b8[:], T.b8a[:], [[16, 8]], ALU.is_ge, 15, -1, 8, "b8a")
+    V("c", 32, ["io", "ipf"], ["IDT"], "ts", T.IDT[:], B("io", 0, 32), row, None, ALU.is_equal)
+    V("c", L, ["io"], ["K16"], "ts", T.K16[:], B("io", 0, L), 16.0, None, ALU.mult)
+    pick("Z2", T.Z2[:], T.ones[:, 0:256], [[0, 2], [-1, 128]], ALU.is_equal, 0, 1, 256, ["ones"])
+    pick("b8a", T.b8a[:], T.ones[:, 0:8], [[-16, 8]], ALU.is_ge, 0, 1, 8, ["ones"])
+    pick("b8", T.b8[:], T.b8a[:], [[16, 8]], ALU.is_ge, 15, -1, 8, ["b8a"])
     V("c", 8, ["b8", "Z10"], ["Z1a"], "copy", B("Z1", 0, 128, 16), T.b8[:])
     V("c", 8, ["b8", "Z10"], ["Z1b"], "copy", B("Z1", 128, 256, 16), T.b8[:])
     z1 = ["Z1a", "Z1b"]
     V("c", 128, z1 + ["ipf"], ["Z1x"], "ts", T.Z1x[:], T.Z1[:], row, None, ALU.mult)
-    pick("BDa", T.BDa[:], T.ones[:, 0:128], [[-16, 8], [0, 16]], ALU.is_ge, 0, 1, 128, "ones")
-    pick("BD", T.BD[:], T.BDa[:], [[16, 8], [0, 16]], ALU.is_ge, 15, -1, 128, "BDa")
-    pick("LTR", T.LTR[:], T.BD[:], [[1, 128]], ALU.is_gt, 0, -1, 128, "BD")
+    pick("BDa", T.BDa[:], T.ones[:, 0:128], [[-16, 8], [0, 16]], ALU.is_ge, 0, 1, 128, ["ones"])
+    pick("BD", T.BD[:], T.BDa[:], [[16, 8], [0, 16]], ALU.is_ge, 15, -1, 128, ["BDa"])
+    pick("LTR", T.LTR[:], T.BD[:], [[1, 128]], ALU.is_gt, 0, -1, 128, ["BD"])
     rmk = [("RM", r) for r in range(16)]
     for r in range(16):
         V("c", 64, ["BD", "IDT"], [("RM", r)], "ts", B("RM", 128 * r, 128 * r + 128), T.BD[:], T.IDT[:, r:r + 1], None, ALU.mult)
-    for bi, be in enumerate((8, 4, 2, 1)):
+    for i, be in enumerate((8, 4, 2, 1) if OPT["fly"] else ()):
+        V("c", 256, ["Z2"], [("rta", i)], "tt", B("rta", 128 * i, 128 * i + 128), B("Z2", 128 - be, 256 - be), B("Z2", 16 - be, 144 - be), ALU.add)
+        V("c", 256, [("rta", i), "BD"], [("ROT", i)], "tt", B("ROT", 128 * i, 128 * i + 128), B("rta", 128 * i, 128 * i + 128), T.BD[:], ALU.mult)
+    for bi, be in enumerate((8, 4, 2, 1) if len(OPT["fly"]) < 2 else ()):
         for m, (step, base) in enumerate(((1000, 0), (-1000, 1000), (1000, -be), (-1000, 1000 - be))):
             j = 4 * bi + m
-            G(("AM", j), 128, ["ones", "rc%d" % (len(CALLS["C"]) - 1)], lambda g, j=j, be=be, step=step, base=base: g.affine_select(
-                B("AM", 128 * j, 128 * j + 128), T.ones[:, 0:128], [[-2 * be, 64 // be], [step, 2], [-1, be]], ALU.is_equal, 0.0, base, 1))
+            pick(("AM", j), B("AM", 128 * j, 128 * j + 128), T.ones[:, 0:128], [[-2 * be, 64 // be], [step, 2], [-1, be]], ALU.is_equal, base, 1, 128,
+                 ["ones", "rc%d" % (len(CALLS["C"]) - 1)])
     I = {}
     for i, k in enumerate(sorted(SCALED)):
         I[k] = B("IS", 128 * i, 128 * i + 128)
-        o = -16 * SCALED[k][1] % 128
-        V("c", 64, ["Z2"], [k], "ts", I[k], B("Z2", o, o + 128), SCALED[k][0], None, ALU.mult)
+        V("c", 64, ["Z2"], [k], "ts", I[k], B("Z2", 0, 128), SCALED[k], None, ALU.mult)
     V("c", 128, ["Z2"], ["ZF"], "ts", T.ZF[:], T.Z2[:], float(F), None, ALU.mult)
     V("c", 128, ["Z2"], ["ZN"], "ts", T.ZN[:], T.Z2[:], float(-F), None, ALU.mult)
     V("c", 256, ["Z2", "LTR"], ["M1"], "tt", T.M1[:], B("Z2", 0, 128), T.LTR[:], ALU.subtract)
@@ -257,21 +260,41 @@ def program(R, T, topo):
         else:
             S(name, cyc, reads, writes, out, src, AF.Relu)
 
-    V("ltf", 576, ltk + yk, ["LTf"], "copy", T.LTf[:], T.LT[:])
-    V("ltf", 576, ["LTf"], ["LTu"], "copy", T.LTu[:], T.LTf[:])
+    def gather(name, mode, reads, key, out, at, win, lst, la):
+        for c, q in enumerate({"h": "sv", "ss": "ss", "vv": "vv"}.get(mode, mode)):
+            m = NK if mode in "sv" else n
+            src, dst = win.indirect(B(lst, la + K * c, la + K * c + m // 16)), B(out, at + n * c, at + n * c + m)
+            cs = range(2) if mode in "sv" else [c]
+            rk, wk = [y for x in cs for y in reads(x)], [key + (x,) for x in cs]
+            if q == "v":
+                V(name, GA * m, rk, wk, "copy", dst, src)
+            else:
+                S(name, GA * m, rk, wk, dst, src, AF.Copy)
+
+    V("c", 544, [], ["LM0"], "set", T.LM[:], 0.0)
+    for j in range(16):
+        a = 136 * (j // 2) + 8 + 8 * (j % 2)
+        V("c", 8, ["b8", "IDT", "LM0"], [("LM", j)], "ts", B("LM", a, 136 * (j // 2 + 1), 16), T.b8[:], T.IDT[:, j:j + 1], None, ALU.mult)
+    P("lt", ["LR"] + [("LM", j) for j in range(16)], ["pc0"],
+      [(B("pc0", L * u, L * u + L), B("LM", 136 * u + 8 - r, 136 * u + 136 - r), B("LR", L * r, L * r + L), r == 0, r == 7, L) for u in range(8) for r in range(8)])
+    S("lt", n, [], ["pc0", "LT"], B("LT", 0, n), B("pc0", 0, n), AF.Copy)
+    V("ltf", 288, ["LT", "LY"], ["LTu"], "ts", T.LTu[:], T.LT[:], 1.0, None, ALU.mult)
     S("stu", 128 + 1500, ["std"] + [("JS", x) for x in range(N)], ["stg"], T.stg[:], T.std[:], AF.Ln)
     V("stu", 128, ["stg"], ["stu"], "ts", T.stu[:], T.stg[:], float(A), float(LOW), ALU.mult, ALU.add)
-    V("eR", 256, ltk, ["eR"], "ts", T.eR[:], B("LT", 0, 512), 15.5, None, ALU.is_gt)
+    V("eR", 256, ["LT"], ["eR"], "ts", T.eR[:], B("LT", 0, 512), 15.5, None, ALU.is_gt)
     for d in range(9):
         u = 8 if d == 8 else -d % N
-        src, out = T.IDT[:].indirect(B("LTu", 64 * u, 64 * u + 64)), B("OH", NK * d, NK * d + NK)
-        if d in OPT["ohv"]:
-            V("oh", GA * NK, ["LTu", "IDT"], [("OH", d)], "copy", out, src)
-        else:
-            S("oh", GA * NK, ["LTu", "IDT"], [("OH", d)], out, src, AF.Copy)
+        for c in range(2):
+            tag[0] = (2, c, d)
+            src, out = T.IDT[:].indirect(B("LTu", L * u + K * c, L * u + K * c + K)), B("OH", NK * d + n * c, NK * d + n * c + n)
+            if (c, d) in OPT["ohv"]:
+                V("oh", GA * n, ["LTu", "IDT"], [("OH", d, c)], "copy", out, src)
+            else:
+                S("oh", GA * n, ["LTu", "IDT"], [("OH", d, c)], out, src, AF.Copy)
+    tag[0] = None
     for c in range(2):
         pw = "pw%d" % c
-        P("ohn", rmk + yk, [pw], [(B(pw, 64 * r, 64 * r + 64), B("RM", 128 * (8 * c + r), 128 * (8 * c + r + 1)), B("LT", 512, 576), True, True, 64) for r in range(8)])
+        P("ohn", rmk + ["LY"], [pw], [(B(pw, L * r, L * r + L), B("RM", 128 * (8 * c + r), 128 * (8 * c + r + 1)), B("LT", 8 * L, 9 * L), True, True, L) for r in range(8)])
         V("ohn", n, ["ipf"], [pw, ("ohn", c)], "ts", B("ohn", n * c, n * c + n), B(pw, 0, n), row, None, ALU.is_equal)
     dupk = ["jz"]
     for i in range(8):
@@ -279,300 +302,235 @@ def program(R, T, topo):
         dupk.append(("dup", i))
         if i < OPT["dupv"]:
             V("dup", BW // 2, jk, [("dup", i)], "copy", B("JW", D + a, D + z), B("JW", a, z))
-        elif i < OPT["dupv"] + OPT["dupg"]:
-            G(("dup", i), BW, jk, lambda g, a=a, z=z: g.affine_select(B("JW", D + a, D + z), B("JW", a, z), [[0, BW]], ALU.is_equal, 0.0, 0, 0))
         else:
             S("dup", BW, jk, [("dup", i)], B("JW", D + a, D + z), B("JW", a, z), AF.Copy)
 
-    def gates(w, c):
-        Tn = len(OFF[w]) - 1
-        e, h, pw = ("ea", "eb")[w] + str(c), ("ha", "hc")[w] + str(c), "pw%d" % c
-        mm = []
-        for t in range(1, Tn + 1):
-            a, s = K * (t - 1), OFF[w][t - 1] + 1
-            mm.append((B(pw, a, a + K), sh(s, "ZF"), B(e, a, a + K), True, t == 1, K))
+    def gates(w, t0, t1, pw):
+        e, h, mm = ("ea", "eb")[w], ("ha", "hc")[w], []
+        for t in range(t0, t1):
+            a, s, out = L * (t - 1), OFF[w][t - 1] + 1, B(pw, L * (t - t0), L * (t - t0 + 1))
+            mm.append((out, sh(s, "ZF"), B(e, a, a + L), True, t == 1, L))
             if t > 1:
-                mm.append((B(pw, a, a + K), sh(s, "ZN"), B(e, a - K, a), False, False, K))
-                mm.append((B(pw, a, a + K), sh(s), B(e, a, a + K), False, True, K))
-        P("h", ["Z2", "ZF", "ZN", e], [pw], mm)
-        S("h", Tn * K, [], [pw, h], B(h, 0, Tn * K), B(pw, 0, Tn * K), AF.Relu)
+                mm.append((out, sh(s, "ZN"), B(e, a - L, a), False, False, L))
+                mm.append((out, sh(s), B(e, a, a + L), False, True, L))
+        P("h", ["Z2", "ZF", "ZN"] + both(e), [pw], mm)
+        S("h", L * (t1 - t0), [], [pw] + [(h, t) for t in range(t0, t1)], B(h, L * (t0 - 1), L * (t1 - 1)), B(pw, 0, L * (t1 - t0)), AF.Relu)
 
-    for c in range(2):
-        tag[0] = (0, c, 0)
-        pw = "pw%d" % c
-        P("ea", ["Z2", "eR"], [pw], [(B(pw, K * d, K * d + K), sh(-d), B("eR", 64 * (-d % N) + K * c, 64 * (-d % N) + K * c + K), True, True, K) for d in range(8)])
-        S("ea", 8 * K, [], [pw, "ea%d" % c], B("ea%d" % c, 0, 8 * K), B(pw, 0, 8 * K), AF.Copy)
-        gates(0, c)
-    tag[0] = None
-    S("G1", GA * NK, jk + ["stu"], ["G1"], T.G1[:], B("JW", 0, W).indirect(B("stu", 64, 128)), AF.Copy)
+    P("ea", ["Z2", "eR"], ["pw0"], [(B("pw0", L * d, L * d + L), sh(-d), B("eR", L * (-d % N), L * (-d % N) + L), True, True, L) for d in range(8)])
+    S("ea", n, [], ["pw0"] + both("ea"), T.ea[:], B("pw0", 0, n), AF.Copy)
+    gates(0, 1, 9, "pw1")
+    gather("G1", OPT["G1"], lambda c: jk + ["stu"], ("G1",), "G1", 0, B("JW", 0, W), "stu", L)
     for c in range(2):
         pw = "pw%d" % c
-        P("Gp", ["Z2", "G1"], [pw], [(B(pw, r, n, 16), sh(0), B("G1", 64 * r + K * c, 64 * r + K * c + K), True, True, K) for r in range(16)])
+        P("Gp", ["Z2"] + both("G1"), [pw], [(B(pw, r, n, 16), sh(0), B("G1", L * r + K * c, L * r + K * c + K), True, True, K) for r in range(16)])
         S("Gp", n, [], [pw, ("Gp", c)], B("Gp", n * c, n * c + n), B(pw, 0, n), AF.Copy)
 
-    lists = {}
+    def at(w, t, y):
+        o = OFF[w]
+        return 2 * L * (10 * w + t) + (L if y and o[t + 1] == o[t] else 0)
 
-    def mark(w, c, t, bank, at):
-        h = ("ha", "hc")[w] + str(c)
-        V("mb", K, [h], [bank, "mb%d" % c], "tt", B("mb%d" % c, 0, K), B(bank, at, at + K), B(h, K * t, K * t + K), ALU.mult)
+    def decode(w, t, cs, pj, a, m, y):
+        b, c0 = at(w, t, 0) + a + K * cs[0], a + K * cs[0]
+        S("ln", m, [], [pj] + [("tt", x, c) for x in y for c in cs], B("tt", c0, c0 + m), B(pj, a, a + m), AF.Ln)
+        V("li", m, [("tt", x, c) for x in y for c in cs], [("li", w, t, x, c) for x in y for c in cs], "ts", B("li", b, b + m), B("tt", c0, c0 + m),
+          float(A), float(LOW), ALU.mult, ALU.add)
 
-    jobs, along = {}, {}
-    for w in range(2):
-        for c in range(2):
-            Tn = len(OFF[w]) - 1
-            first, lag = OPT["merge"][w][c]
-            rest = []
-            for t in range(1, Tn + 2):
-                if t <= Tn and not first <= t + lag <= Tn:
-                    rest.append(t)
-                    if t < Tn - 1:
-                        continue
-                for i in range(len(rest) % 2 - 2, len(rest) - 1, 2):
-                    job = tuple(rest[max(i, 0):i + 2])
-                    for y, x in enumerate(job):
-                        jobs[w, c, x] = (job, 3 + y if len(job) == 2 else 3 + x % 2)
-                if t <= Tn and t not in rest:
-                    jobs[w, c, t] = (None, 2 * (t % 2))
-                    along[w, c, t + lag] = t
-                rest = []
+    def mark(w, t, cs, pj):
+        h, a, m = ("ha", "hc")[w], K * cs[0], K * len(cs)
+        if t + 1 < len(OFF[w]):
+            V("mb", m, [(h, t + 1)], [pj] + [("mb", c) for c in cs], "tt", B("mb", a, a + m), B(pj, 0, m), B(h, L * t + a, L * t + a + m), ALU.mult)
 
-    def akey(w, c, t):
-        a = ("Aa", "Ab")[w] + str(c)
-        return B(a, K * t, K * t + K), (a, t)
+    def series(w, t, cs):
+        o, pj, m = OFF[w], "pj%d" % cs[0], K * len(cs)
+        two = t + 1 < len(o) and o[t + 1] == o[t]
+        reads = z1 + ["Z2"] + [("mj", c) for c in cs] + ([("mb", c) for c in cs] if t else [])
 
-    def alive(w, c, job, bank, at):
-        al, m = ("Aa", "Ab")[w] + str(c), K * len(job)
-        V("nc", m, [], [bank] + [(al, x) for x in job], "ts", B(al, K * job[0], K * job[0] + m), B(bank, at, at + m), 127.25, 16.0, ALU.is_gt, ALU.mult)
-        if len(job) == 2:
-            (p, pk), (q, qk) = akey(w, c, job[0]), akey(w, c, job[1])
-            V("al", 2 * K, [pk, qk], [qk], "tt", q, p, q, ALU.min)
-        if job[-1] == len(OFF[w]) - 2:
-            ended(w, c)
-
-    def marks(w, c, job, bank, at):
-        e = ("ea", "eb")[w] + str(c)
-        p, pk = akey(w, c, job[0] - 1)
-        mm = [(B(bank, at + K * i, at + K * i + K), I["I8"], p, False, False, K) for i in range(len(job))]
-        mm.append((B(bank, at, at + K * len(job)), I["I64"], B(e, K * (job[0] - 1), K * job[-1]), False, True, K * len(job)))
-        return mm, ["I64", "I8", e, pk]
-
-    def series(w, c, t):
-        pj, mb, x, o = "pj%d" % c, "mb%d" % c, "X%d" % c, OFF[w]
-        two = int(t + 1 < len(o) and o[t + 1] == o[t])
-        reads = z1 + ["Z2", (x, 1)] + ([mb] if t else [])
-        u, at, mm = along.get((w, c, t)), 0, []
-        if u:
-            y = jobs[w, c, u][1]
-            at, a = (0, n) if y else (K, 0)
-            mm = [(B(pj, 0, 2 * K), sel(r, 1), B(x, a + r, a + 2 * n, 16), r == 0, False, 2 * K) for r in range(16)]
-            mm.append((B(pj, at, at + K), sh(1), B(mb, 0, K), False, False, K))
-            more, mk = marks(w, c, (u,), pj, K - at)
-            mm += more
-            reads += mk + [(x, y)]
-        for y in range(0 if u else 1 + two):
-            out = B(pj, K * y, K * y + K)
-            if t:
-                mm.append((out, sh(o[t] - o[t - 1] - y), B(mb, 0, K), True, False, K))
+        def sums_of(y):
+            out = B(pj, L * y, L * y + m)
+            mm = [(out, sh(o[t] - o[t - 1] - y), B("mb", K * cs[0], K * cs[0] + m), True, False, m)] if t else []
             for r in range(16):
-                mm.append((out, sel(r, 1 - y), B(x, n + r, 2 * n, 16), r == 0 and not t, r == 15, K))
-        P("js", reads, [pj], mm)
-        tt, li = "tt%d" % c, "li%d" % c
-        m, a = K * (1 + two), 2 * K * (10 * w + t)
-        S("ln", m, [], [pj, tt], B(tt, 0, m), B(pj, at, at + m), AF.Ln)
-        V("li", m, [tt], [(li, w, t)], "ts", B(li, a, a + m), B(tt, 0, m), float(A), float(LOW), ALU.mult, ALU.add)
-        lists[w, c, t] = (B(li, a, a + K), B(li, a + K * two, a + K * two + K), (li, w, t))
-        if t + 1 < len(o):
-            mark(w, c, t, pj, at)
-        if u:
-            alive(w, c, (u,), pj, K - at)
+                src = B("mj", L * r, L * r + L) if (w, t) == (0, 0) else B("mj", n * cs[0] + r, n * cs[-1] + n, 16)
+                mm.append((out, sel(r, 1 - y), src, r == 0 and not t, r == 15, m))
+            return mm
+        if two and ((w, t) in OPT["one"] or m < L):
+            cb, cbk = B("cb", K * cs[0], K * cs[0] + m), [("cb", c) for c in cs]
+            P("js", reads, [pj], sums_of(1))
+            decode(w, t, cs, pj, L, m, (1,))
+            S("cb", m, [], [pj] + cbk, cb, B(pj, L, L + m), AF.Copy)
+            P("cb", ["Z2"] + cbk, [pj], [(B(pj, 0, m), sh(1), cb, True, True, m)])
+            mark(w, t, cs, pj)
+            decode(w, t, cs, pj, 0, m, (0,))
+            return
+        P("js", reads, [pj], sums_of(0) + (sums_of(1) if two else []))
+        decode(w, t, cs, pj, 0, 2 * L if two else m, (0, 1))
+        mark(w, t, cs, pj)
 
-    def image(w, c, t):
-        _, lj, key = lists[w, c, t - 1]
+    def image(w, t):
         d = 8 if (w, t) == (1, 1) else OFF[w][t]
         hi, tk = (W, jk) if t == 1 else (WID, jk + dupk)
-        V("jg", GA * n, [key, ("OH", d)] + tk, [("X%d" % c, 1)], "tt", B("X%d" % c, n, 2 * n), B("JW", 0, hi).indirect(lj), B("OH", NK * d + n * c, NK * d + n * c + n), ALU.mult)
-        series(w, c, t)
+        for cs in ([0], [1]) if (w, t) in OPT["split"] else ([0, 1],):
+            tag[0] = (w, cs[0] if len(cs) == 1 else 2, t)
+            a, b, m = n * cs[0], at(w, t - 1, 1) + K * cs[0], n * len(cs)
+            V("jg", GA * m, [("li", w, t - 1, 1, c) for c in cs] + [("OH", d, c) for c in cs] + tk, [("mj", c) for c in cs], "tt", B("mj", a, a + m),
+              B("JW", 0, hi).indirect(B("li", b, b + m // 16)), B("OH", NK * d + a, NK * d + a + m), ALU.mult)
+            series(w, t, cs)
 
-    def coefs(w, c, t):
-        lc, _, key = lists[w, c, t]
-        y = t % NCC
-        out, src = B("cc%d" % c, n * y, n * y + n), B("CW", 0, WID).indirect(lc)
-        if (w, c, t) in OPT["cgv"]:
-            V("cg", GA * n, [key] + ck, [("cc", c, y)], "copy", out, src)
-        else:
-            S("cg", GA * n, [key] + ck, [("cc", c, y)], out, src, AF.Copy)
-
-    def sums(w, c, t):
-        va, pv, cc, o = ("va", "vb")[w] + str(c), "pv%d" % c, "cc%d" % c, OFF[w]
-        y = t % NCC
-        mm = [(B(pv, 0, n), sh(-o[t] - 1), B(cc, n * y, n * y + n), True, False, n)]
-        if t == 1:
-            mm.append((B(pv, 0, n), sh(-1), B(cc, 0, n), False, True, n))
-            rk = [("cc", c, 0)]
-        else:
-            mm.append((B(pv, 0, n), sh(0), B(va, n * (t - 2), n * (t - 1)), False, True, n))
-            rk = [(va, t - 1)]
-        P("add", ["Z2", ("cc", c, y)] + rk, [pv], mm)
-        v = B(va, n * (t - 1), n * t)
-        V("clip", n, [], [pv, (va, t)], "ts", v, B(pv, 0, n), 255.0, -255.0, ALU.min, ALU.max)
-        job, y = jobs[w, c, t]
-        x = "X%d" % c
-        if (w, c, t) in OPT["signv"]:
-            V("sg", n // 2, [(va, t)], [(x, y)], "ts", B(x, n * y, n * y + n), v, 0.0, 0.5, ALU.is_ge, ALU.subtract)
-        else:
-            S("sg", n, [(va, t)], [(x, y)], B(x, n * y, n * y + n), v, AF.Sign, bias=0.5)
-        if job and t == job[-1]:
-            pc, m, a = "pc%d" % c, K * len(job), n * jobs[w, c, job[0]][1]
-            mm = [(B(pc, 0, m), sel(r, 1), B(x, a + r, a + n * len(job), 16), r == 0, False, m) for r in range(16)]
-            more, mk = marks(w, c, job, pc, 0)
-            P("cnt", z1 + mk + [(x, jobs[w, c, i][1]) for i in job], [pc], mm + more)
-            alive(w, c, job, pc, 0)
-
-    def ended(w, c):
-        Tn = len(OFF[w]) - 1
-        pc, lv = "pc%d" % c, "lv%d" % c
-        mm = [(B(pc, 64, 64 + K), sh(0), T.K16[:], True, False, K)]
-        for t in range(1, Tn):
-            mm.append((B(pc, 64, 64 + K), I["I32"], akey(w, c, t)[0], False, t == Tn - 1, K))
-        P("pick", ["Z2", "K16", "I32"] + [akey(w, c, t)[1] for t in range(1, Tn)], [pc], mm)
-        V("lv", K, ["ipf"], [pc, (lv, w)], "ts", B(lv, K * w, K * w + K), B(pc, 64, 64 + K), row, None, ALU.add)
-
-    def final(w, c):
-        Tn = len(OFF[w]) - 1
-        va, lv, vf = ("va", "vb")[w] + str(c), "lv%d" % c, "vf%d" % c
-        reads, src = [(lv, w)] + [(va, t) for t in range(1, Tn + 1)], B(va, 0, n * Tn).indirect(B(lv, K * w, K * w + K))
-        if (w, c) in OPT["vfv"]:
-            V("vf", GA * n, reads, [vf], "copy", B(vf, 0, n), src)
-        else:
-            S("vf", GA * n, reads, [vf], B(vf, 0, n), src, AF.Copy)
-
-    def walk(w, c):
-        late = OPT["merge"][w][c][1] - 1
-        for u in range(len(OFF[w]) + late):
-            if 0 < u < len(OFF[w]):
-                tag[0] = (w, c, u)
-                image(w, c, u)
-            t = u - late
+    def sums(w, t):
+        va, al, e, o, y = ("va", "vb")[w], ("Aa", "Ab")[w], ("ea", "eb")[w], OFF[w], t % NCC
+        tag[0] = (w, 2, t)
+        gather("cg", OPT["cg"].get((w, t), "s"), lambda c: [("li", w, t, 0, c)] + ck, ("cc", y), "cc", NK * y, B("CW", 0, WID), "li", at(w, t, 0))
+        if not t:
+            return
+        for c in range(2):
             tag[0] = (w, c, t)
-            if t >= 0:
-                coefs(w, c, t)
-            if t > 0:
-                sums(w, c, t)
-        final(w, c)
+            pv, a = "pv%d" % c, n * c
+            mm = [(B(pv, 0, n), sh(-o[t] - 1), B("cc", NK * y + a, NK * y + a + n), True, False, n)]
+            if t == 1:
+                mm.append((B(pv, 0, n), sh(-1), B("cc", a, a + n), False, True, n))
+            else:
+                mm.append((B(pv, 0, n), sh(0), B(va, NK * (t - 2) + a, NK * (t - 2) + a + n), False, True, n))
+            P("add", ["Z2", ("cc", y, c), ("cc", 0, c) if t == 1 else (va, t - 1, c)], [pv], mm)
+            V("clip", n, [], [pv, (va, t, c)], "ts", B(va, NK * (t - 1) + a, NK * (t - 1) + a + n), B(pv, 0, n), 255.0, -255.0, ALU.min, ALU.max)
+        tag[0] = (w, 2, t)
+        mode, y = OPT["sg"].get((w, t), "s"), t % 2
+        for c, q in enumerate({"h": "sv", "ss": "ss", "vv": "vv"}.get(mode, mode)):
+            m, cs = (NK, range(2)) if mode in "sv" else (n, [c])
+            src, out = B(va, NK * (t - 1) + n * c, NK * (t - 1) + n * c + m), B("sg", NK * y + n * c, NK * y + n * c + m)
+            if q == "v":
+                V("sg", m // 2, [(va, t, x) for x in cs], [("sg", y, x) for x in cs], "ts", out, src, 0.0, 0.5, ALU.is_ge, ALU.subtract)
+            else:
+                S("sg", m, [(va, t, x) for x in cs], [("sg", y, x) for x in cs], out, src, AF.Sign, bias=0.5)
+        pc = "pc%d" % y
+        mm = [(B(pc, 0, L), I["I64"], B(e, L * (t - 1), L * t), True, False, L), (B(pc, 0, L), I["I64"], B(al, L * (t - 1), L * t), False, False, L)]
+        mm += [(B(pc, 0, L), sel(r, 0), B("sg", NK * y + r, NK * y + NK, 16), False, r == 15, L) for r in range(16)]
+        P("cnt", z1 + ["I64", (al, t - 1)] + both(e) + both("sg", y), [pc], mm)
+        S("nc", L, [], [pc, (al, t)], B(al, L * t, L * t + L), B(pc, 0, L), AF.Sign, bias=-63.25)
+        if t == len(o) - 2:
+            mm = [(B(pc, L, 2 * L), sh(0), T.K16[:], True, False, L)]
+            mm += [(B(pc, L, 2 * L), I["I512"], B(al, L * x, L * x + L), False, x == t, L) for x in range(1, t + 1)]
+            P("pick", ["Z2", "K16", "I512"] + [(al, x) for x in range(1, t + 1)], [pc], mm)
+            V("lv", L, ["ipf"], [pc, ("lv", w)], "ts", B("lv", L * w, L * w + L), B(pc, L, 2 * L), row, 512.0 * t, ALU.add, ALU.add)
 
-    tag[0] = (0, 0, 0)
-    V("jg", GA * NK, ["stu", ("ohn", 0), ("ohn", 1)] + jk, ["mj"], "tt", T.mj[:], B("JW", 0, W).indirect(B("stu", 0, 64)), T.ohn[:], ALU.mult)
-    mm = []
-    for y in range(2):
-        for r in range(16):
-            mm.append((B("pj0", 64 * y, 64 * y + 64), sel(r, 1 - y), B("mj", 64 * r, 64 * r + 64), r == 0, r == 15, 64))
-    P("js", z1 + ["mj"], ["pj0"], mm)
-    S("ln", 128, [], ["pj0", "t0"], T.t0[:], B("pj0", 0, 128), AF.Ln)
-    V("li", 128, ["t0"], ["l0"], "ts", T.l0[:], T.t0[:], float(A), float(LOW), ALU.mult, ALU.add)
-    for c in range(2):
-        lists[0, c, 0] = (B("l0", K * c, K * c + K), B("l0", 64 + K * c, 64 + K * c + K), "l0")
-        mark(0, c, 0, "pj0", K * c)
-    for c in range(2):
-        walk(0, c)
+    def walk(w):
+        va, Tn = ("va", "vb")[w], len(OFF[w]) - 1
+        for t in range(Tn + 1):
+            if t:
+                image(w, t)
+            sums(w, t)
+        gather("vf", OPT["vf"][w], lambda c: [("lv", w)] + [(va, t, x) for t in range(1, Tn + 1) for x in range(2)], ("vf",), "vf", 0, B(va, 0, NK * Tn), "lv", L * w)
+
+    tag[0] = (0, 2, 0)
+    V("jg", GA * NK, ["stu"] + both("ohn") + jk, both("mj"), "tt", T.mj[:], B("JW", 0, W).indirect(B("stu", 0, L)), T.ohn[:], ALU.mult)
+    series(0, 0, [0, 1])
+    walk(0)
+    tag[0] = (1, 2, -1)
+    ak = [("Aa", t) for t in range(9)]
+    P("eb", ["Z2", "ones", "Ip", "Im"] + both("ea") + ak, ["pw0", "pw1"],
+      [(B("pw1", 0, L), I["Ip"], B("ones", 0, L), True, False, L), (B("pw1", 0, L), I["Im"], B("Aa", 8 * L, 9 * L), False, True, L),
+       (B("pw0", 0, n), sh(0), T.ea[:], True, False, n), (B("pw0", 0, n), I["Ip"], B("Aa", 0, 8 * L), False, False, n),
+       (B("pw0", 0, n), I["Im"], B("Aa", L, 9 * L), False, True, n)])
+    S("eb", L, [], ["pw1", ("eb", 0)], B("eb", 0, L), B("pw1", 0, L), AF.Copy)
+    S("eb", n, [], ["pw0", ("eb", 1)], B("eb", L, 9 * L), B("pw0", 0, n), AF.Copy)
+    gates(1, 1, 4, "pw1")
+    gates(1, 4, 10, "pw0")
     for c in range(2):
         tag[0] = (1, c, -1)
-        aa, ea, eb, pw = "Aa%d" % c, "ea%d" % c, "eb%d" % c, "pw%d" % c
-        P("eb", ["Z2", "ones", "Ip", "Im", ea] + [(aa, t) for t in range(9)], [pw],
-          [(B(pw, 0, K), sh(0), B("ones", 0, K), True, False, K), (B(pw, 0, K), I["Im"], B(aa, 8 * K, 9 * K), False, True, K),
-           (B(pw, K, 9 * K), sh(0), B(ea, 0, 8 * K), True, False, 8 * K), (B(pw, K, 9 * K), I["Ip"], B(aa, 0, 8 * K), False, False, 8 * K),
-           (B(pw, K, 9 * K), I["Im"], B(aa, K, 9 * K), False, True, 8 * K)])
-        S("eb", 9 * K, [], [pw, eb], B(eb, 0, 9 * K), B(pw, 0, 9 * K), AF.Copy)
-        gates(1, c)
-        vf, ax, am, eq, oy, pv, pj = "vf%d" % c, "ax%d" % c, "am%d" % c, "eq%d" % c, "oy%d" % c, "pv%d" % c, "pj%d" % c
-        P("m1", ["In", "ones"], [pj], [(B(pj, 0, n), I["In"], T.ones[:], True, False, n)])
-        src, sk, wd, pos = vf, vf, n, 0
-        for bi in range(4):
-            hf = wd // 2
-            mm = []
-            for j in range(2):
-                for k in range(2):
-                    q = 4 * bi + 2 * j + k
-                    mm.append((B(pv, hf * j, hf * j + hf), B("AM", 128 * q, 128 * q + 128), B(src, pos + hf * k, pos + hf * k + hf), k == 0, k == 1, hf))
-            P("mx", [("AM", 4 * bi + y) for y in range(4)] + [sk], [pv], mm)
-            S("mx", hf, [], [pv, ax], B(ax, 0, hf), B(pv, 0, hf), AF.Copy)
-            npos = 0 if bi == 0 else pos + wd
-            V("mx", hf, [ax], [pv, (am, bi)], "tt", B(am, npos, npos + hf), B(ax, 0, hf), B(pv, hf, 2 * hf), ALU.max)
-            src, sk, wd, pos = am, (am, bi), hf, npos
-        alone = OPT["eqv"]
-        mm = [] if alone else [(B(pv, 0, n), I["In"], B(vf, 0, n), True, False, n)]
-        mm += [(B(pv, K * r, K * r + K), B("RM", 128 * r, 128 * r + 128), B(am, pos, pos + K), alone, alone or r == 15, K) for r in range(16)]
-        P("rep", rmk + ["In", vf, sk], [pv], mm)
-        if alone:
-            V("eq", n, [vf], [pv, eq], "tt", B(eq, 0, n), B(vf, 0, n), B(pv, 0, n), ALU.is_equal)
+        ax, am, pv, pj, a = "ax%d" % c, "am%d" % c, "pv%d" % c, "pj%d" % c, n * c
+        vf, eq, oy, gp, mj = (B(x, a, a + n) for x in ("vf", "eq", "oy", "Gp", "mj"))
+        old, fly = c in OPT["old"], c in OPT["fly"]
+        if old:
+            P("m1", ["Z2", ("Gp", c)], [pj], [(B(pj, 0, n), sh(0), gp, True, True, n)])
         else:
-            S("eq", n, [], [pv, eq], B(eq, 0, n), B(pv, 0, n), AF.Relu, bias=1.0, scale=-1.0)
-        P("ltr", ["M1", "Z2", eq, ("Gp", c)], [pj], [(B(pj, 0, n), T.M1[:], B(eq, 0, n), False, False, n), (B(pj, 0, n), sh(0), B("Gp", n * c, n * c + n), False, True, n)])
-        relu("m0", OPT["mjv"], n, [], [pj, ("X%d" % c, 1)], B("X%d" % c, n, 2 * n), B(pj, 0, n))
-        tag[0] = (1, c, 0)
-        series(1, c, 0)
-        P("oy", ["M1", eq], [pv], [(B(pv, 0, n), T.M1[:], B(eq, 0, n), True, True, n)])
-        relu("oy", OPT["oyv"], n, [], [pv, oy], B(oy, 0, n), B(pv, 0, n))
-        P("y1", ["Z1x", oy], [pw], [(B(pw, 0, K), sel(r, 0, "Z1x"), B(oy, r, n, 16), r == 0, r == 15, K) for r in range(16)])
-        S("y1", K, [], [pw, ("y1l", c)], B("L1", 576 + K * c, 576 + K * c + K), B(pw, 0, K), AF.Copy)
-    tag[0] = (1, 1, -1)
-    for pw, blocks in (("pw0", [0]), ("pw1", range(1, 9))):
+            P("m1", ["In", "ones"], [pj], [(B(pj, 0, n), I["In"], T.ones[:], True, False, n)])
+        if fly:
+            src, sk = vf, ("vf", c)
+            for bi in range(4):
+                P("mx", [("ROT", bi), sk], [pv], [(B(pv, 0, n), B("ROT", 128 * bi, 128 * bi + 128), src, True, True, n)])
+                out, key = ((B(am, 0, n), am), (eq, ("eq", c)), (B(am, 0, n), am), (B(pv, 0, n), pv))[bi]
+                V("mx", n, [sk], [pv, key], "tt", out, src, B(pv, 0, n), ALU.max)
+                src, sk = out, key
+        else:
+            src, sk, wd, pos = "vf", ("vf", c), n, a
+            for bi in range(4):
+                hf, mm = wd // 2, []
+                for j in range(2):
+                    for k in range(2):
+                        q = 4 * bi + 2 * j + k
+                        mm.append((B(pv, hf * j, hf * j + hf), B("AM", 128 * q, 128 * q + 128), B(src, pos + hf * k, pos + hf * k + hf), k == 0, k == 1, hf))
+                P("mx", [("AM", 4 * bi + y) for y in range(4)] + [sk], [pv], mm)
+                S("mx", hf, [], [pv, ax], B(ax, 0, hf), B(pv, 0, hf), AF.Copy)
+                npos = 0 if bi == 0 else pos + wd
+                V("mx", hf, [ax], [pv, (am, bi)], "tt", B(am, npos, npos + hf), B(ax, 0, hf), B(pv, hf, 2 * hf), ALU.max)
+                src, sk, wd, pos = am, (am, bi), hf, npos
+        on_v = fly or c in OPT["eqv"]
+        if not fly:
+            mm = [] if on_v else [(B(pv, 0, n), I["In"], vf, True, False, n)]
+            mm += [(B(pv, K * r, K * r + K), B("RM", 128 * r, 128 * r + 128), B(am, pos, pos + K), on_v, on_v or r == 15, K) for r in range(16)]
+            P("rep", rmk + ["In", ("vf", c), sk], [pv], mm)
+        if on_v:
+            V("eq", n, [("vf", c)], [pv, ("eq", c)], "tt", eq, vf, B(pv, 0, n), ALU.is_equal)
+        else:
+            S("eq", n, [], [pv, ("eq", c)], eq, B(pv, 0, n), AF.Relu, bias=1.0, scale=-1.0)
+        if not old:
+            P("ltr", ["M1", "Z2", ("eq", c), ("Gp", c)], [pj], [(B(pj, 0, n), T.M1[:], eq, False, False, n), (B(pj, 0, n), sh(0), gp, False, True, n)])
+            relu("m0", c in OPT["mjv"], n, [], [pj, ("mj", c)], mj, B(pj, 0, n))
+        P("oy", ["M1", ("eq", c)], [pv], [(B(pv, 0, n), T.M1[:], eq, True, True, n)])
+        relu("oy", c in OPT["oyv"], n, [], [pv, ("oy", c)], oy, B(pv, 0, n))
+        if old:
+            V("m0", n, [("oy", c)], [pj, ("mj", c)], "tt", mj, oy, B(pj, 0, n), ALU.mult)
+    for cs in ([0], [1]) if (1, 0) in OPT["split"] else ([0, 1],):
+        tag[0] = (1, cs[0] if len(cs) == 1 else 2, 0)
+        series(1, 0, cs)
+    tag[0] = (1, 2, -1)
+    for pw, blocks in (("pw0", range(1, 9)), ("pw1", [0])):
         mm = []
         for i, b in enumerate(blocks):
             u = -(b - 1) % N if b else 8
-            mm.append((B(pw, 64 * i, 64 * i + 64), sh(1 - b if b else 0), B("LT", 64 * u, 64 * u + 64), True, False, 64))
-            for c in range(2):
-                mm.append((B(pw, 64 * i + K * c, 64 * i + K * c + K), I["I16"], B("eb%d" % c, K * b, K * b + K), False, c == 1, K))
-        P("l1", ["Z2", "I16", "eb0", "eb1"] + ltk + yk, [pw], mm)
-        m = 64 * len(blocks)
-        S("l1", m, [], [pw, ("L1", pw)], B("L1", 64 * blocks[0], 64 * blocks[0] + m), B(pw, 0, m), AF.Copy)
-    for c in range(2):
-        walk(1, c)
-    tag[0] = (1, 1, 10)
+            mm.append((B(pw, L * i, L * i + L), sh(1 - b if b else 0), B("LT", L * u, L * u + L), True, False, L))
+            mm.append((B(pw, L * i, L * i + L), I["I16"], B("eb", L * b, L * b + L), False, True, L))
+        P("l1", ["Z2", "I16", "LT", "LY"] + both("eb"), [pw], mm)
+        m = L * len(blocks)
+        S("l1", m, [], [pw, ("L1", pw)], B("L1", L * blocks[0], L * blocks[0] + m), B(pw, 0, m), AF.Copy)
+    P("y1", ["Z1x"] + both("oy"), ["pw1"], [(B("pw1", 0, L), sel(r, 0, "Z1x"), B("oy", r, NK, 16), r == 0, r == 15, L) for r in range(16)])
+    S("y1", L, [], ["pw1", "y1"], B("L1", 9 * L, 10 * L), B("pw1", 0, L), AF.Copy)
+    walk(1)
+    tag[0] = (1, 2, 10)
     xo = {"xe": [], "xv": [], "xt": []}
 
     def stage(sem, nbytes, reads, out, in_):
         xo[sem].append((sem, len(xo[sem])))
         DM(sem, nbytes, reads, [xo[sem][-1]], out, in_)
 
-    for j, pair in enumerate(PAIRS[1]):
-        pw, a = "pw%d" % (j % 2), 64 * (pair[0] - 1)
-        last = pair[-1] == 9
-        terms = [(t - 1, t) for t in pair] + ([(0, 9)] if last else [])
-        mm = [(B(pw, 0, 64 * len(terms)), sh(0), B("L1", a, a + 64 * len(terms)), True, False, 64 * len(terms))]
-        reads = ["Z2", "Ib", ("L1", "pw0"), ("L1", "pw1")] + ([("y1l", 0), ("y1l", 1)] if last else [])
-        for i, (x, y) in enumerate(terms):
-            for c in range(2):
-                out = B(pw, 64 * i + K * c, 64 * i + K * c + K)
-                mm.append((out, sh(-1), akey(1, c, x)[0], False, False, K))
-                mm.append((out, I["Ib"], akey(1, c, y)[0], False, i + 1 == len(terms) and c == 1, K))
-                reads += [akey(1, c, x)[1], akey(1, c, y)[1]]
-        P("yl", reads, [pw], mm)
-        m = 64 * len(terms)
-        V("yl", m, [], [pw, ("YL", a)], "ts", B("YL", a, a + m), B(pw, 0, m), 16.0, None, ALU.min)
-        for t in pair:
-            d, b = t - 2, 64 * (t - 1)
+    for j, (t0, t1) in enumerate(((1, 5), (5, 7), (7, 9), (9, 10))):
+        pw, a, m, last = "pw%d" % (j % 2), L * (t0 - 1), L * (t1 - t0), t0 == 9
+        wd = m + L * last
+        mm = [(B(pw, 0, wd), sh(0), B("L1", a, a + wd), True, False, wd), (B(pw, 0, m), I["I8"], B("Ab", a, a + m), False, False, m),
+              (B(pw, 0, m), I["J8"], B("Ab", a + L, a + L + m), False, not last, m)]
+        if last:
+            mm += [(B(pw, L, 2 * L), I["I8"], B("Ab", 0, L), False, False, L), (B(pw, L, 2 * L), I["J8"], B("Ab", 9 * L, 10 * L), False, True, L)]
+        P("yl", ["Z2", "I8", "J8", ("L1", "pw0"), ("L1", "pw1"), "y1", ("Ab", 0)] + [("Ab", t) for t in range(t0 - 1, t1)], [pw], mm)
+        V("yl", wd, [], [pw, ("YL", a)], "ts", B("YL", a, a + wd), B(pw, 0, wd), 16.0, None, ALU.min)
+        for t in range(t0, t1):
+            d, b = t - 2, L * (t - 1)
             if t == 1:
-                stage("xe", 16384, [("YL", a)], T.ZE[0:8, 0:16, :], B("YL", 0, 64))
+                stage("xe", 16384, [("YL", a)], T.ZE[0:8, 0:16, :], B("YL", 0, L))
                 continue
             for i0, i1, p0 in runs(0, N, d):
                 out = T.ZE[p0:p0 + i1 - i0, 16 * (7 - d):16 * (8 - d), :] if d < 7 else T.ZT[p0:p0 + i1 - i0, 0:64, :]
-                stage("xe" if d < 7 else "xt", 2048 * (i1 - i0), [("YL", a)], out, T.YL[16 * i0:16 * i1, b:b + 64])
+                stage("xe" if d < 7 else "xt", 2048 * (i1 - i0), [("YL", a)], out, T.YL[16 * i0:16 * i1, b:b + L])
         if last:
-            stage("xt", 16384, [("YL", a)], T.ZT[0:8, 64:128, :], B("YL", 576, 640))
-    vn = []
-    for c in range(2):
-        vf = "vf%d" % c
-        for r in range(16):
-            out, src = B("VN", 64 * r + K * c, 64 * r + K * c + K), B(vf, r, n, 16)
-            vn.append(("VN", c, r))
-            if r < OPT["permv"]:
-                V("vn", K, [vf], [vn[-1]], "copy", out, src)
-            else:
-                S("vn", K, [vf], [vn[-1]], out, src, AF.Copy)
+            stage("xt", 16384, [("YL", a)], T.ZT[0:8, 64:128, :], B("YL", 9 * L, 10 * L))
+    vn = [("VN", r) for r in range(16)]
+    for r in range(16):
+        out, src = B("VN", L * r, L * r + L), B("vf", r, NK, 16)
+        if r < OPT["permv"]:
+            V("vn", K, both("vf"), [vn[r]], "copy", out, src)
+        else:
+            S("vn", L, both("vf"), [vn[r]], out, src, AF.Copy)
     stage("xv", 262144, vn, T.ZV[0:8], T.VN[:])
-    send(ALL, "re", 16384, xo["xe"], "re", lambda x: T.ZE[x - 1], lambda x: T.ZE[15 - x])
-    send(ALL, "rv", 32768, xo["xv"], "rv", lambda x: T.ZV[x - 1], lambda x: T.ZV[15 - x])
-    send(ALL, "rt", 4096, xo["xt"], "rt", lambda x: T.ZT[x - 1], lambda x: T.ZT[15 - x])
+    send(ALL, "re", 16384, xo["xe"], lambda x: T.ZE[x - 1], lambda x: T.ZE[15 - x])
+    send(ALL, "rv", 32768, xo["xv"], lambda x: T.ZV[x - 1], lambda x: T.ZV[15 - x])
+    send(ALL, "rt", 4096, xo["xt"], lambda x: T.ZT[x - 1], lambda x: T.ZT[15 - x])
     for i0, i1, g0 in runs(0, N, R):
         g1, a, z, m, s1 = g0 + i1 - i0, 7 + i0, 7 + i1, 2048 * (i1 - i0), (R + 1) % N
         for u0, u1, s0 in runs(1, N, R + 1):
@@ -606,6 +564,91 @@ def depend(ops):
 
 
 def order(ops):
+    best = now = replay(ops, order0(ops))
+    for _ in range(PASSES):
+        now = replay(ops, justify(ops, now))
+        if now[0] < best[0]:
+            best = now
+    return best[1]
+
+
+def waits(ops):
+    return [[(x, WAKE if ops[x]["q"] != o["q"] else SELF) for x in o["d"]] for o in ops]
+
+
+def replay(ops, seq):
+    pre = waits(ops)
+    for _ in range(5):
+        st, end, free, lane = [0.0] * len(ops), [0.0] * len(ops), {}, 0.0
+        for k in seq:
+            o = ops[k]
+            t = max([free.get(o["q"], 0.0)] + [end[x] + a for x, a in pre[k]])
+            st[k] = t
+            e = t + o["dur"]
+            if o["q"] != "net":
+                free[o["q"]] = e
+            if o["tail"]:
+                lane = max(lane, e) + o["tail"]
+                e = lane + o["lat"]
+            end[k] = e
+        new = sorted(seq, key=lambda k: st[k])
+        same = [k for k in new if ops[k]["tail"]] == [k for k in seq if ops[k]["tail"]]
+        seq = new
+        if same:
+            break
+    return max(end), seq, st, end
+
+
+def place(ops, key, pre, full, gap):
+    cnt = len(ops)
+    nxt, left = [[] for _ in ops], [len(p) for p in pre]
+    for k in range(cnt):
+        for x, _ in pre[k]:
+            nxt[x].append(k)
+    ready, busy, st = [k for k in range(cnt) if not left[k]], {}, [0.0] * cnt
+    while ready:
+        k = min(ready, key=lambda x: (key[x], x))
+        ready.remove(k)
+        t = max([0.0] + [st[x] + full[x] + a for x, a in pre[k]])
+        if ops[k]["q"] != "net":
+            t += gap[k]
+            row, i = busy.setdefault(ops[k]["q"], []), 0
+            while i < len(row) and row[i][0] <= t:
+                i += 1
+            if i:
+                t = max(t, row[i - 1][1])
+            while i < len(row) and t + ops[k]["dur"] > row[i][0]:
+                t = row[i][1]
+                i += 1
+            row.insert(i, (t, t + ops[k]["dur"]))
+            t -= gap[k]
+        st[k] = t
+        for y in nxt[k]:
+            left[y] -= 1
+            if not left[y]:
+                ready.append(y)
+    return st
+
+
+def justify(ops, now):
+    _, seq, st, end = now
+    cnt = len(ops)
+    full = [end[k] - st[k] for k in range(cnt)]
+    pre, back = waits(ops), [[] for _ in ops]
+    for k in range(cnt):
+        for x, a in pre[k]:
+            back[x].append((k, a))
+    for q in ("sync", "g"):
+        row = [k for k in seq if ops[k]["q"] == q]
+        for a, b in zip(row, row[1:]):
+            back[a].append((b, ops[a]["dur"] - full[a]))
+            pre[b].append((a, ops[a]["dur"] - full[a]))
+    late = place(ops, [-e for e in end], back, full, [full[k] - ops[k]["dur"] for k in range(cnt)])
+    early = place(ops, [-late[k] - full[k] for k in range(cnt)], pre, full, [0.0] * cnt)
+    return sorted(range(cnt), key=lambda k: (early[k], k))
+
+
+def order0(ops):
     cnt = len(ops)
     nxt = [[] for _ in range(cnt)]
     for k, o in enumerate(ops):
@@ -623,7 +666,7 @@ def order(ops):
         name, tg = o["tag"]
         urge.append(prio[k] + o["bonus"] + URGE.get((name,) + tg[:2] if tg else name, 0) + (URGE.get((name,) + tg, 0) if tg else 0))
     left = [len(o["d"]) for o in ops]
-    ready = [0.0] * cnt
+    ready = [float(HOLD.get(o["tag"][0], 0.0)) for o in ops]
     cand = {}
     for k in range(cnt):
         if left[k] == 0:
@@ -654,7 +697,6 @@ def order(ops):
         if o["tail"]:
             lane = max(end, lane) + o["tail"]
             end = lane + o["lat"]
-        o["at"] = (t, end)
         out.append(k)
         for y in nxt[k]:
             left[y] -= 1
@@ -709,7 +751,7 @@ def rank_program(g, core, T, topo):
             for s, c in ops[x]["know"].items():
                 mine[s] = max(mine.get(s, 0), c)
         sem = o["sem"] or QSEM.get(q)
-        for i, call in enumerate(o["calls"]):
+        for call in o["calls"]:
             ins = call(g)
             if sem == "remote":
                 sent += o["cnt"]

import math
from concourse.bass import DstId, RemoteDMATransfer
from concourse.mybir import AluOpType, ActivationFunctionType

ALU, AF = AluOpType, ActivationFunctionType
N, W, NK = 8, 4608, 1024
BW = W // N
n, K, L = 512, 32, 64
PER = 80.0
FO = 70
D = int(PER) * FO
F = 2.0 ** FO
SC = math.log(2.0) / PER
A = PER / math.log(2.0)
LOW = 63.8 * PER + 0.35
WID = D + W
OFF = [[0, 0, 1, 2, 3, 4, 5, 6, 7], [0, 0, 0, 1, 2, 3, 4, 5, 6, 7]]
NCC = 3
B16, F32, I32, U16 = "bfloat16", "float32", "int32", "uint16"

SCRATCH = {}
SEMAPHORES = ["kpe", "kv", "ks", "kg", "ls", "xl", "xs", "rl", "rs", "ll", "lst", "ls0", "jo", "co", "xy", "ry", "ly", "xe", "re", "xv", "rv", "xt", "rt", "stores"]
SEMAPHORES += ["lj%d" % _b for _b in range(N)]
SEMAPHORES += ["%s%d" % (_x, _k) for _x in ("rj", "jr", "xc", "rc", "cr") for _k in range(4)]


def sb(name, cols, dtype=B16):
    SCRATCH[name] = ("sbuf", [128, cols], dtype)


for _k, _s, _c in (("ZL", 15, 64), ("ZS", 15, 16), ("ZY", 15, 8), ("ZJ", 7, BW), ("ZC", 7, BW), ("XC", 8, BW), ("ZE", 15, 64), ("ZV", 15, 128), ("ZT", 15, 16)):
    SCRATCH[_k] = ("dram", [_s, 128, _c], B16)
SCALED = {"I64": 64.0, "I16": 16.0, "In": -1.0, "I8": 8.0, "J8": -8.0, "I512": 512.0, "Ip": 0.5, "Im": -0.5}
for _k, _c in (("JW", WID), ("CW", WID), ("JS", W), ("ones", n), ("Z1", 256), ("Z2", 256), ("ZF", 256), ("ZN", 256), ("Z1x", 256), ("IDT", 32), ("BDa", 128),
               ("BD", 128), ("LTR", 128), ("M1", 128), ("RM", 2048), ("AM", 2048), ("ROT", 512), ("rta", 512), ("IS", 128 * len(SCALED)), ("K16", L), ("b8a", 8),
               ("b8", 8), ("LT", 9 * L), ("LR", 512), ("LM", 1088), ("eR", 512), ("OH", 9 * NK), ("ohn", NK), ("G1", NK), ("Gp", NK), ("mj", NK), ("L1", 10 * L),
               ("YL", 10 * L), ("VN", NK), ("stc", 128), ("std", 128), ("cc", NCC * NK), ("sg", 2 * NK), ("va", 8 * NK), ("vb", 9 * NK), ("vf", NK), ("eq", NK),
               ("oy", NK), ("mb", L), ("cb", L), ("Aa", 9 * L), ("Ab", 10 * L), ("ea", 8 * L), ("eb", 9 * L), ("ha", 8 * L), ("hc", 9 * L)):
    sb(_k, _c)
for _k, _c, _d in (("jmi", W, I32), ("jmf", W, F32), ("stf", 128, F32), ("stg", 128, F32), ("ipi", 2, I32), ("ipj", 2, I32), ("ipf", 2, F32), ("io", L, F32),
                   ("sti", 128, I32), ("stu", 128, U16), ("LTu", 9 * L, U16), ("tt", 2 * L, F32), ("li", 20 * 2 * L, U16), ("lv", 2 * L, U16)):
    sb(_k, _c, _d)
for _c in range(2):
    sb("ax%d" % _c, n // 2)
    sb("am%d" % _c, n)
    for _k in ("pv", "pw", "pj", "pc"):
        SCRATCH["%s%d" % (_k, _c)] = ("psum", [128, 512], F32)

VF, SF, CY, PCY, PF, GA, WAKE, SELF, GAP = 45.0, 65.0, 0.88, 0.46, 20.0, 1.45, 90.0, 60.0, 150.0
HOP, LAT, GBW, CALL, ROW = 2000.0, 1800.0, 295.0, 900.0, 17.0
ROWS = {"ll": 1024, "ly": 128, "ls": 256, "xs": 256, "lj": 4 * BW, "jo": 2 * BW, "xe": 128, "xt": 128, "xv": 2048, "rj": 2 * BW}
FIRST = 1e6
PASSES = 2
HOLD = {}
OPT = {"J": ((0, 1), (2, 3)), "C": ((0,), (1,), (2, 3)), "pace": ["rj1"] * 4, "deep": 3, "old": (), "fly": (0, 1), "one": (), "ohv": ((0, 0), (1, 0), (0, 1), (1, 1), (0, 2), (1, 2)),
       "dupv": 4, "permv": 9, "eqv": (0, 1), "mjv": (0,), "oyv": (), "split": ((0, 1), (0, 2), (0, 3), (0, 4), (0, 5)), "cg": {}, "sg": {}, "vf": ("h", "h")}
URGE = {}
OPT = {'J': ((0, 1), (2, 3)), 'C': ((0,), (1,), (2, 3)), 'pace': ['rj1', 'rj1', 'rj1', 'rj1'], 'deep': 3, 'old': (), 'fly': (0, 1), 'one': ((0, 0), (1, 0), (1, 1)), 'ohv': ((0, 0), (0, 2), (0, 3), (1, 0), (1, 2)), 'dupv': 4, 'permv': 10, 'eqv': (0, 1), 'mjv': (0, 1), 'oyv': (0,), 'split': ((0, 1), (0, 2), (0, 3), (0, 4), (0, 5), (0, 6), (1, 2), (1, 6)), 'cg': {(0, 0): 'h', (0, 1): 'h', (0, 4): 'ss', (0, 5): 'ss', (0, 6): 'ss', (0, 7): 'ss', (0, 8): 'ss', (1, 9): 'h', (1, 0): 'h', (1, 1): 'h', (1, 6): 'ss', (1, 7): 'ss'}, 'sg': {(0, 2): 'h', (0, 3): 'v', (0, 6): 'vv', (0, 7): 'h', (0, 8): 'h', (1, 8): 'h', (1, 9): 'h', (0, 4): 'h', (1, 5): 'ss', (1, 3): 'ss', (1, 7): 'ss', (0, 1): 'ss', (0, 5): 'vv'}, 'vf': ('h', 'h')}
URGE = {'ltf': 29500, ('li', 0, 2): 2700, ('mb', 0, 2): 2700, ('sg', 0, 2): 200, ('jg', 0, 1): 13000, ('ln', 0, 1): 12000, ('li', 0, 1): 12000, ('ln', 0, 0): 1200, ('mb', 1, 2): 2000, ('cg', 1, 2): -2000, ('sg', 1, 2): -2000, ('pick', 1, 2): -2000, ('clip', 0, 0, 5): 4000, ('oh', 2, 0, 0): 8000, ('jg', 0, 0): 400, ('li', 0, 0): 200, ('clip', 1, 1): -3500, ('sg', 1, 2, 6): -500, ('clip', 1, 0): -8000, ('mb', 0, 1): 8000, ('add', 1, 1): 4500, ('mb', 1, 0): -500, ('jg', 0, 2): 500, ('ln', 0, 2): 500}
HOLD = {'lj2': 4000}
OPT["G1"] = "ss"
OPT = {'J': ((0, 1), (2, 3)), 'C': ((0,), (1,), (2, 3)), 'pace': ['rj1', 'rj1', 'rj1', 'rj1'], 'deep': 3, 'old': (), 'fly': (1,), 'one': ((0, 0), (1, 0), (1, 1)), 'ohv': ((0, 0), (0, 3), (0, 4), (1, 0), (1, 3)), 'dupv': 2, 'permv': 10, 'eqv': (0,), 'mjv': (0, 1), 'oyv': (0,), 'split': ((0, 1), (0, 2), (0, 3), (0, 4), (0, 5), (1, 0), (1, 1), (1, 2), (1, 3), (1, 6)), 'cg': {(0, 0): 'h', (0, 1): 'h', (0, 4): 'ss', (0, 7): 'ss', (0, 8): 'ss', (1, 9): 'h', (1, 0): 'ss', (1, 1): 'h', (1, 6): 'ss', (1, 7): 'ss'}, 'sg': {(0, 2): 'v', (0, 3): 'h', (0, 6): 'vv', (0, 7): 'h', (0, 8): 'vv', (1, 8): 'h', (1, 9): 'h', (1, 5): 'ss', (1, 3): 'ss', (1, 7): 'ss', (0, 5): 'vv'}, 'vf': ('h', 'h'), 'G1': 'ss'}
URGE = {'ltf': 2000000, ('li', 0, 2): 2700, ('mb', 0, 2): 2700, ('ln', 0, 1): 11200, ('ln', 0, 0): 1200, ('mb', 1, 2): 4000, ('cg', 1, 2): -1000, ('sg', 1, 2): -1000, ('clip', 0, 0, 5): 8000, ('clip', 1, 0): -8000, ('add', 1, 1): 4500, ('jg', 0, 2): 500, ('ln', 0, 2): 2500, 'eR': 30000, ('sg', 0, 2, 1): 500, ('jg', 1, 0): -500, ('jg', 0, 1): -800, ('li', 0, 1, 4): -1000, ('ln', 0, 2, 8): -8000, ('li', 1, 1): 4000, ('add', 1, 0, 5): -4000, ('li', 1, 0): 4000, ('sg', 0, 2): -200, ('li', 1, 2, 7): 2000, ('mb', 0, 0, 5): 4000, ('cg', 0, 2, 4): -1000, ('js', 1, 2): 2000, ('ln', 1, 2): 2000, ('li', 1, 2): 2000, ('clip', 1, 2): 2000, ('cnt', 1, 2): 2000, ('nc', 1, 2): 2000, ('vf', 1, 2): 2000, ('js', 0, 1): -1000, ('li', 0, 1): -1000, ('mb', 0, 1): -1000, ('sg', 1, 2, 4): 4000, ('mb', 0, 2, 6): 4000}
HOLD = {}


def program(R, T, topo):
    ops = []
    dies = [topo.die(c) for c in T.cores]
    pairs = [[x, y] for x in range(1, N) for y in range(x + 1, N) if all(dies[(r + x) % N] != dies[(r + y) % N] for r in range(N))]
    alone = [x for x in range(1, N) if not any(x in p for p in pairs)]
    parts = pairs + [alone]
    CALLS = {k: [[x for i in c for x in parts[i]] for c in OPT[k]] for k in "JC"}
    tag = [None]
    me = T.cores[R]

    def B(name, a, z, step=1):
        return T[name][:, a:z:step] if step > 1 else T[name][:, a:z]

    def add(q, dur, reads, writes, calls, sem=None, lat=0.0, tail=0.0, dma=False, bonus=0.0, name=""):
        ops.append({"q": q, "dur": dur, "r": list(reads), "w": list(writes), "calls": calls, "sem": sem, "lat": lat, "tail": tail, "dma": dma, "bonus": bonus,
                    "tag": (name, tag[0])})
        return len(ops) - 1

    def V(name, cyc, reads, writes, kind, *a):
        call = {"copy": lambda g: g.vector.tensor_copy(*a), "tt": lambda g: g.vector.tensor_tensor(*a),
                "ts": lambda g: g.vector.tensor_scalar(*a), "set": lambda g: g.vector.memset(*a)}[kind]
        add("v", VF + CY * max(32, cyc), reads, writes, [call], name=name)

    def S(name, cyc, reads, writes, *a, **kw):
        add("s", SF + CY * max(64, cyc), reads, writes, [lambda g: g.scalar.activation(*a, **kw)], name=name)

    def P(name, reads, writes, mms):
        cost = PF
        for m in mms:
            cost += PCY * max(64, m[5])
        add("pe", cost, reads, writes, [(lambda g, m=m: g.tensor.matmul(m[0], m[1], m[2], m[3], m[4])) for m in mms], name=name)

    def G(key, el, reads, call):
        add("g", 170 + 1.9 * el, reads, [key], [call], sem="kg", name="const")

    def pick(key, out, in_, pat, cmp_, base, cm, el, src):
        G(key, el, src, lambda g: g.affine_select(out, in_, pat, cmp_, 0.0, base, cm))

    def lane(sem, nbytes):
        return nbytes / GBW + ROW * max(1.0, nbytes / ROWS.get(sem[:2], 8192) / 16)

    def DM(sem, nbytes, reads, writes, out, in_, bonus=0.0):
        add("sync", 70.0, reads, writes, [lambda g: g.sync.dma_start(out, in_)], sem=sem, lat=LAT, tail=lane(sem, nbytes), dma=True, bonus=bonus, name=sem)

    def send(aheads, sem, nbytes, reads, src, dst, bonus=0.0):
        far = [x for x in aheads if dies[(R + x) % N] != dies[R]]
        near = [x for x in aheads if x not in far]
        turn = []
        while far or near:
            turn += far[:1] + near[:1]
            far, near = far[1:], near[1:]
        ways = 1
        while ways < len(aheads):
            ways *= 2
        trs, per = [], 0
        for i, x in enumerate(turn):
            core = T.cores[(R + x) % N]
            rid, pid, _ = topo.addr(core)
            eng = topo.engines(me, core)[i::ways]
            if len(turn) < ways and x in alone:
                eng = eng + topo.engines(me, core)[ways - 1::ways]
            per += len(eng)
            trs.append(RemoteDMATransfer(dst_ids=[DstId(rid=rid, pnc=pid)], dma_engine_mask=sum(1 << e for e in eng), remote_sem=T.sem[sem], src=src(x), dst=dst(x)))
        k = add("g", CALL, reads, [], [lambda g: g.remote_dma_fused(trs, local_sem=T.sem.ls)], sem="remote", bonus=bonus, name=sem)
        j = add("net", 0.0, [], [sem], [], sem=sem, lat=HOP, tail=lane(sem, nbytes * len(aheads)), name=sem)
        ops[j]["after"] = k
        ops[k]["cnt"] = ops[j]["cnt"] = per

    def runs(lo, hi, first):
        out, i = [], lo
        while i < hi:
            at = (first + i) % N
            z = min(hi, i + N - at)
            out.append((i, z, at))
            i = z
        return out

    def spans(c):
        out = []
        for x in sorted(c):
            if out and out[-1][1] == x:
                out[-1] = (out[-1][0], x + 1)
            else:
                out.append((x, x + 1))
        return out

    def both(*key):
        return [key + (0,), key + (1,)]

    ALL = list(range(1, N))
    xl, xs, xy = [], [], []
    for i0, i1, g0 in runs(0, N, R):
        g1 = g0 + i1 - i0
        for u0, u1, s0 in runs(0, N, R):
            xl.append(("xl", i0, u0))
            DM("xl", 2048 * (i1 - i0) * (u1 - u0), [], [xl[-1]], T.ZL[7 + i0:7 + i1, 16 * u0:16 * u1, :], T.lt[g0:g1, NK * s0:NK * (s0 + u1 - u0)], bonus=9 * FIRST)
        xy.append(("xy", i0))
        DM("xy", 2048 * (i1 - i0), [], [xy[-1]], T.ZY[7 + i0:7 + i1], T.y0[g0:g1, :], bonus=9 * FIRST)
    DM("ls0", 65536, [], ["sti"], T.sti[:], T.st[:], bonus=8.5 * FIRST)
    V("st", 128, ["sti"], ["stf"], "copy", T.stf[:], T.sti[:])
    S("st", 128, ["stf"], ["stc"], T.stc[:], T.stf[:], AF.Exp, bias=float(-LOW * SC), scale=float(SC))
    for i0, i1, g0 in runs(0, N, R):
        xs.append(("xs", i0))
        DM("xs", 4096 * (i1 - i0), ["stc"], [xs[-1]], T.ZS[7 + i0:7 + i1], T.stc[16 * g0:16 * (g0 + i1 - i0), :], bonus=8.5 * FIRST)
    send(ALL, "rl", 16384, xl, lambda x: T.ZL[7 + x], lambda x: T.ZL[7 - x], bonus=9 * FIRST)
    send(ALL, "ry", 2048, xy, lambda x: T.ZY[7 + x], lambda x: T.ZY[7 - x], bonus=8.5 * FIRST)
    send(ALL, "rs", 4096, xs, lambda x: T.ZS[7 + x], lambda x: T.ZS[7 - x], bonus=6 * FIRST)
    DM("ll", 131072, xl + ["rl"], ["LR"], T.LR[:], T.ZL[0:8], bonus=8 * FIRST)
    DM("ly", 16384, xy + ["ry"], ["LY"], B("LT", 8 * L, 9 * L), T.ZY[0:8], bonus=8 * FIRST)
    DM("lst", 32768, xs + ["rs"], ["std"], T.std[:], T.ZS[0:8], bonus=7 * FIRST)
    jorder = [x for c in CALLS["J"] for x in c] + [0]
    for i, x in enumerate(jorder):
        g0, a, z = (R + x) % N, BW * x, BW * x + BW
        DM("lj%d" % x, 128 * BW * 4, [("jmi", y) for y in jorder[i - OPT["deep"]:i - OPT["deep"] + 1] if i >= OPT["deep"]], [("jmi", x)], B("jmi", a, z),
           T.jm[16 * g0:16 * g0 + 16, :], bonus=FIRST * (8 - 0.1 * i))
        V("jmf", BW, [("jmi", x)], [("jmf", x)], "copy", B("jmf", a, z), B("jmi", a, z))
        ops[-1]["bonus"] = FIRST
        S("JS", BW, [("jmf", x)], [("JS", x)], B("JS", a, z), B("jmf", a, z), AF.Exp, bias=float(-LOW * SC), scale=float(SC))
        ops[-1]["bonus"] = FIRST
    jk = ["jo"]
    for k, c in enumerate(CALLS["J"]):
        send(c, "rj%d" % k, 128 * BW * 2, [("JS", x) for x in c], lambda x: B("JS", BW * x, BW * x + BW), lambda x: T.ZJ[7 - x], bonus=(7 - 0.1 * k) * FIRST)
        for lo, hi in spans(c):
            jk.append(("jr", lo))
            DM("jr%d" % k, 128 * BW * 2 * (hi - lo), ["rj%d" % k], [jk[-1]], T.JW[16 * (8 - hi):16 * (8 - lo), 0:W], T.ZJ[8 - hi:8 - lo], bonus=(7 - 0.1 * k) * FIRST)
    DM("jo", 128 * BW * 2, [("JS", 0)], ["jo"], T.JW[112:128, 0:W], B("JS", 0, BW), bonus=7 * FIRST)
    ck = ["co"]
    for k, c in enumerate(CALLS["C"]):
        xk, bonus = [], (3 - 0.1 * k) * FIRST
        for lo, hi in spans(c):
            for i0, i1, g0 in runs(lo, hi, R):
                xk.append(("xc", i0))
                DM("xc%d" % k, 128 * BW * 2 * (i1 - i0), [OPT["pace"][k]], [xk[-1]], T.XC[i0:i1], T.cf[16 * g0:16 * (g0 + i1 - i0), :], bonus=bonus)
        send(c, "rc%d" % k, 128 * BW * 2, xk, lambda x: T.XC[x], lambda x: T.ZC[7 - x], bonus=bonus)
        for lo, hi in spans(c):
            ck.append(("cr", lo))
            DM("cr%d" % k, 128 * BW * 2 * (hi - lo), ["rc%d" % k], [ck[-1]], T.CW[16 * (9 - hi):16 * (9 - lo), 0:W], T.ZC[8 - hi:8 - lo], bonus=bonus)
    DM("co", 128 * BW * 2, [OPT["pace"][-1]], ["co"], T.CW[0:16, 0:W], T.cf[16 * R:16 * R + 16, :], bonus=2 * FIRST)
    V("c", 256, [], ["ones"], "set", T.ones[:], 1.0)
    V("c", 128, [], ["Z10"], "set", T.Z1[:], 0.0)
    V("c", (D - W) // 2, [], ["jz"], "set", B("JW", W, D), 0.0)
    for i in range(4):
        ck.append(("cz", i))
        V("c", D // 8, [], [("cz", i)], "set", B("CW", W + D // 4 * i, W + D // 4 * (i + 1)), 0.0)
    for a in ("Aa", "Ab"):
        V("c", 32, [], [(a, 0)], "set", B(a, 0, L), 1.0)
    G("ipi", 2, [], lambda g: g.iota(T.ipi[:], [[0, 2]], 0, 1))
    G("io", L, [], lambda g: g.iota(T["io"][:], [[1, L]], 0, 0, allow_small_or_imprecise_dtypes=True))
    V("c", 2, ["ipi"], ["ipj"], "ts", T.ipj[:], T.ipi[:], 15, None, ALU.bitwise_and)
    V("c", 2, ["ipj"], ["ipf"], "copy", T.ipf[:], T.ipj[:])
    row = T.ipf[:, 0:1]
    V("c", 32, ["io", "ipf"], ["IDT"], "ts", T.IDT[:], B("io", 0, 32), row, None, ALU.is_equal)
    V("c", L, ["io"], ["K16"], "ts", T.K16[:], B("io", 0, L), 16.0, None, ALU.mult)
    pick("Z2", T.Z2[:], T.ones[:, 0:256], [[0, 2], [-1, 128]], ALU.is_equal, 0, 1, 256, ["ones"])
    pick("b8a", T.b8a[:], T.ones[:, 0:8], [[-16, 8]], ALU.is_ge, 0, 1, 8, ["ones"])
    pick("b8", T.b8[:], T.b8a[:], [[16, 8]], ALU.is_ge, 15, -1, 8, ["b8a"])
    V("c", 8, ["b8", "Z10"], ["Z1a"], "copy", B("Z1", 0, 128, 16), T.b8[:])
    V("c", 8, ["b8", "Z10"], ["Z1b"], "copy", B("Z1", 128, 256, 16), T.b8[:])
    z1 = ["Z1a", "Z1b"]
    V("c", 128, z1 + ["ipf"], ["Z1x"], "ts", T.Z1x[:], T.Z1[:], row, None, ALU.mult)
    pick("BDa", T.BDa[:], T.ones[:, 0:128], [[-16, 8], [0, 16]], ALU.is_ge, 0, 1, 128, ["ones"])
    pick("BD", T.BD[:], T.BDa[:], [[16, 8], [0, 16]], ALU.is_ge, 15, -1, 128, ["BDa"])
    pick("LTR", T.LTR[:], T.BD[:], [[1, 128]], ALU.is_gt, 0, -1, 128, ["BD"])
    rmk = [("RM", r) for r in range(16)]
    for r in range(16):
        V("c", 64, ["BD", "IDT"], [("RM", r)], "ts", B("RM", 128 * r, 128 * r + 128), T.BD[:], T.IDT[:, r:r + 1], None, ALU.mult)
    for i, be in enumerate((8, 4, 2, 1) if OPT["fly"] else ()):
        V("c", 256, ["Z2"], [("rta", i)], "tt", B("rta", 128 * i, 128 * i + 128), B("Z2", 128 - be, 256 - be), B("Z2", 16 - be, 144 - be), ALU.add)
        V("c", 256, [("rta", i), "BD"], [("ROT", i)], "tt", B("ROT", 128 * i, 128 * i + 128), B("rta", 128 * i, 128 * i + 128), T.BD[:], ALU.mult)
    for bi, be in enumerate((8, 4, 2, 1) if len(OPT["fly"]) < 2 else ()):
        for m, (step, base) in enumerate(((1000, 0), (-1000, 1000), (1000, -be), (-1000, 1000 - be))):
            j = 4 * bi + m
            pick(("AM", j), B("AM", 128 * j, 128 * j + 128), T.ones[:, 0:128], [[-2 * be, 64 // be], [step, 2], [-1, be]], ALU.is_equal, base, 1, 128,
                 ["ones", "rc%d" % (len(CALLS["C"]) - 1)])
    I = {}
    for i, k in enumerate(sorted(SCALED)):
        I[k] = B("IS", 128 * i, 128 * i + 128)
        V("c", 64, ["Z2"], [k], "ts", I[k], B("Z2", 0, 128), SCALED[k], None, ALU.mult)
    V("c", 128, ["Z2"], ["ZF"], "ts", T.ZF[:], T.Z2[:], float(F), None, ALU.mult)
    V("c", 128, ["Z2"], ["ZN"], "ts", T.ZN[:], T.Z2[:], float(-F), None, ALU.mult)
    V("c", 256, ["Z2", "LTR"], ["M1"], "tt", T.M1[:], B("Z2", 0, 128), T.LTR[:], ALU.subtract)

    def sel(r, a, name="Z1"):
        o = -(16 * a + r) % 128
        return B(name, o, o + 128)

    def sh(a, name="Z2"):
        o = -16 * a % 128
        return B(name, o, o + 128)

    def relu(name, on_v, cyc, reads, writes, out, src):
        if on_v:
            V(name, cyc, reads, writes, "ts", out, src, 0.0, None, ALU.max)
        else:
            S(name, cyc, reads, writes, out, src, AF.Relu)

    def gather(name, mode, reads, key, out, at, win, lst, la):
        for c, q in enumerate({"h": "sv", "ss": "ss", "vv": "vv"}.get(mode, mode)):
            m = NK if mode in "sv" else n
            src, dst = win.indirect(B(lst, la + K * c, la + K * c + m // 16)), B(out, at + n * c, at + n * c + m)
            cs = range(2) if mode in "sv" else [c]
            rk, wk = [y for x in cs for y in reads(x)], [key + (x,) for x in cs]
            if q == "v":
                V(name, GA * m, rk, wk, "copy", dst, src)
            else:
                S(name, GA * m, rk, wk, dst, src, AF.Copy)

    V("c", 544, [], ["LM0"], "set", T.LM[:], 0.0)
    for j in range(16):
        a = 136 * (j // 2) + 8 + 8 * (j % 2)
        V("c", 8, ["b8", "IDT", "LM0"], [("LM", j)], "ts", B("LM", a, 136 * (j // 2 + 1), 16), T.b8[:], T.IDT[:, j:j + 1], None, ALU.mult)
    P("lt", ["LR"] + [("LM", j) for j in range(16)], ["pc0"],
      [(B("pc0", L * u, L * u + L), B("LM", 136 * u + 8 - r, 136 * u + 136 - r), B("LR", L * r, L * r + L), r == 0, r == 7, L) for u in range(8) for r in range(8)])
    S("lt", n, [], ["pc0", "LT"], B("LT", 0, n), B("pc0", 0, n), AF.Copy)
    V("ltf", 288, ["LT", "LY"], ["LTu"], "ts", T.LTu[:], T.LT[:], 1.0, None, ALU.mult)
    S("stu", 128 + 1500, ["std"] + [("JS", x) for x in range(N)], ["stg"], T.stg[:], T.std[:], AF.Ln)
    V("stu", 128, ["stg"], ["stu"], "ts", T.stu[:], T.stg[:], float(A), float(LOW), ALU.mult, ALU.add)
    V("eR", 256, ["LT"], ["eR"], "ts", T.eR[:], B("LT", 0, 512), 15.5, None, ALU.is_gt)
    for d in range(9):
        u = 8 if d == 8 else -d % N
        for c in range(2):
            tag[0] = (2, c, d)
            src, out = T.IDT[:].indirect(B("LTu", L * u + K * c, L * u + K * c + K)), B("OH", NK * d + n * c, NK * d + n * c + n)
            if (c, d) in OPT["ohv"]:
                V("oh", GA * n, ["LTu", "IDT"], [("OH", d, c)], "copy", out, src)
            else:
                S("oh", GA * n, ["LTu", "IDT"], [("OH", d, c)], out, src, AF.Copy)
    tag[0] = None
    for c in range(2):
        pw = "pw%d" % c
        P("ohn", rmk + ["LY"], [pw], [(B(pw, L * r, L * r + L), B("RM", 128 * (8 * c + r), 128 * (8 * c + r + 1)), B("LT", 8 * L, 9 * L), True, True, L) for r in range(8)])
        V("ohn", n, ["ipf"], [pw, ("ohn", c)], "ts", B("ohn", n * c, n * c + n), B(pw, 0, n), row, None, ALU.is_equal)
    dupk = ["jz"]
    for i in range(8):
        a, z = BW * i, BW * i + BW
        dupk.append(("dup", i))
        if i < OPT["dupv"]:
            V("dup", BW // 2, jk, [("dup", i)], "copy", B("JW", D + a, D + z), B("JW", a, z))
        else:
            S("dup", BW, jk, [("dup", i)], B("JW", D + a, D + z), B("JW", a, z), AF.Copy)

    def gates(w, t0, t1, pw):
        e, h, mm = ("ea", "eb")[w], ("ha", "hc")[w], []
        for t in range(t0, t1):
            a, s, out = L * (t - 1), OFF[w][t - 1] + 1, B(pw, L * (t - t0), L * (t - t0 + 1))
            mm.append((out, sh(s, "ZF"), B(e, a, a + L), True, t == 1, L))
            if t > 1:
                mm.append((out, sh(s, "ZN"), B(e, a - L, a), False, False, L))
                mm.append((out, sh(s), B(e, a, a + L), False, True, L))
        P("h", ["Z2", "ZF", "ZN"] + both(e), [pw], mm)
        S("h", L * (t1 - t0), [], [pw] + [(h, t) for t in range(t0, t1)], B(h, L * (t0 - 1), L * (t1 - 1)), B(pw, 0, L * (t1 - t0)), AF.Relu)

    P("ea", ["Z2", "eR"], ["pw0"], [(B("pw0", L * d, L * d + L), sh(-d), B("eR", L * (-d % N), L * (-d % N) + L), True, True, L) for d in range(8)])
    S("ea", n, [], ["pw0"] + both("ea"), T.ea[:], B("pw0", 0, n), AF.Copy)
    gates(0, 1, 9, "pw1")
    gather("G1", OPT["G1"], lambda c: jk + ["stu"], ("G1",), "G1", 0, B("JW", 0, W), "stu", L)
    for c in range(2):
        pw = "pw%d" % c
        P("Gp", ["Z2"] + both("G1"), [pw], [(B(pw, r, n, 16), sh(0), B("G1", L * r + K * c, L * r + K * c + K), True, True, K) for r in range(16)])
        S("Gp", n, [], [pw, ("Gp", c)], B("Gp", n * c, n * c + n), B(pw, 0, n), AF.Copy)

    def at(w, t, y):
        o = OFF[w]
        return 2 * L * (10 * w + t) + (L if y and o[t + 1] == o[t] else 0)

    def decode(w, t, cs, pj, a, m, y):
        b, c0 = at(w, t, 0) + a + K * cs[0], a + K * cs[0]
        S("ln", m, [], [pj] + [("tt", x, c) for x in y for c in cs], B("tt", c0, c0 + m), B(pj, a, a + m), AF.Ln)
        V("li", m, [("tt", x, c) for x in y for c in cs], [("li", w, t, x, c) for x in y for c in cs], "ts", B("li", b, b + m), B("tt", c0, c0 + m),
          float(A), float(LOW), ALU.mult, ALU.add)

    def mark(w, t, cs, pj):
        h, a, m = ("ha", "hc")[w], K * cs[0], K * len(cs)
        if t + 1 < len(OFF[w]):
            V("mb", m, [(h, t + 1)], [pj] + [("mb", c) for c in cs], "tt", B("mb", a, a + m), B(pj, 0, m), B(h, L * t + a, L * t + a + m), ALU.mult)

    def series(w, t, cs):
        o, pj, m = OFF[w], "pj%d" % cs[0], K * len(cs)
        two = t + 1 < len(o) and o[t + 1] == o[t]
        reads = z1 + ["Z2"] + [("mj", c) for c in cs] + ([("mb", c) for c in cs] if t else [])

        def sums_of(y):
            out = B(pj, L * y, L * y + m)
            mm = [(out, sh(o[t] - o[t - 1] - y), B("mb", K * cs[0], K * cs[0] + m), True, False, m)] if t else []
            for r in range(16):
                src = B("mj", L * r, L * r + L) if (w, t) == (0, 0) else B("mj", n * cs[0] + r, n * cs[-1] + n, 16)
                mm.append((out, sel(r, 1 - y), src, r == 0 and not t, r == 15, m))
            return mm
        if two and ((w, t) in OPT["one"] or m < L):
            cb, cbk = B("cb", K * cs[0], K * cs[0] + m), [("cb", c) for c in cs]
            P("js", reads, [pj], sums_of(1))
            decode(w, t, cs, pj, L, m, (1,))
            S("cb", m, [], [pj] + cbk, cb, B(pj, L, L + m), AF.Copy)
            P("cb", ["Z2"] + cbk, [pj], [(B(pj, 0, m), sh(1), cb, True, True, m)])
            mark(w, t, cs, pj)
            decode(w, t, cs, pj, 0, m, (0,))
            return
        P("js", reads, [pj], sums_of(0) + (sums_of(1) if two else []))
        decode(w, t, cs, pj, 0, 2 * L if two else m, (0, 1))
        mark(w, t, cs, pj)

    def image(w, t):
        d = 8 if (w, t) == (1, 1) else OFF[w][t]
        hi, tk = (W, jk) if t == 1 else (WID, jk + dupk)
        for cs in ([0], [1]) if (w, t) in OPT["split"] else ([0, 1],):
            tag[0] = (w, cs[0] if len(cs) == 1 else 2, t)
            a, b, m = n * cs[0], at(w, t - 1, 1) + K * cs[0], n * len(cs)
            V("jg", GA * m, [("li", w, t - 1, 1, c) for c in cs] + [("OH", d, c) for c in cs] + tk, [("mj", c) for c in cs], "tt", B("mj", a, a + m),
              B("JW", 0, hi).indirect(B("li", b, b + m // 16)), B("OH", NK * d + a, NK * d + a + m), ALU.mult)
            series(w, t, cs)

    def sums(w, t):
        va, al, e, o, y = ("va", "vb")[w], ("Aa", "Ab")[w], ("ea", "eb")[w], OFF[w], t % NCC
        tag[0] = (w, 2, t)
        gather("cg", OPT["cg"].get((w, t), "s"), lambda c: [("li", w, t, 0, c)] + ck, ("cc", y), "cc", NK * y, B("CW", 0, WID), "li", at(w, t, 0))
        if not t:
            return
        for c in range(2):
            tag[0] = (w, c, t)
            pv, a = "pv%d" % c, n * c
            mm = [(B(pv, 0, n), sh(-o[t] - 1), B("cc", NK * y + a, NK * y + a + n), True, False, n)]
            if t == 1:
                mm.append((B(pv, 0, n), sh(-1), B("cc", a, a + n), False, True, n))
            else:
                mm.append((B(pv, 0, n), sh(0), B(va, NK * (t - 2) + a, NK * (t - 2) + a + n), False, True, n))
            P("add", ["Z2", ("cc", y, c), ("cc", 0, c) if t == 1 else (va, t - 1, c)], [pv], mm)
            V("clip", n, [], [pv, (va, t, c)], "ts", B(va, NK * (t - 1) + a, NK * (t - 1) + a + n), B(pv, 0, n), 255.0, -255.0, ALU.min, ALU.max)
        tag[0] = (w, 2, t)
        mode, y = OPT["sg"].get((w, t), "s"), t % 2
        for c, q in enumerate({"h": "sv", "ss": "ss", "vv": "vv"}.get(mode, mode)):
            m, cs = (NK, range(2)) if mode in "sv" else (n, [c])
            src, out = B(va, NK * (t - 1) + n * c, NK * (t - 1) + n * c + m), B("sg", NK * y + n * c, NK * y + n * c + m)
            if q == "v":
                V("sg", m // 2, [(va, t, x) for x in cs], [("sg", y, x) for x in cs], "ts", out, src, 0.0, 0.5, ALU.is_ge, ALU.subtract)
            else:
                S("sg", m, [(va, t, x) for x in cs], [("sg", y, x) for x in cs], out, src, AF.Sign, bias=0.5)
        pc = "pc%d" % y
        mm = [(B(pc, 0, L), I["I64"], B(e, L * (t - 1), L * t), True, False, L), (B(pc, 0, L), I["I64"], B(al, L * (t - 1), L * t), False, False, L)]
        mm += [(B(pc, 0, L), sel(r, 0), B("sg", NK * y + r, NK * y + NK, 16), False, r == 15, L) for r in range(16)]
        P("cnt", z1 + ["I64", (al, t - 1)] + both(e) + both("sg", y), [pc], mm)
        S("nc", L, [], [pc, (al, t)], B(al, L * t, L * t + L), B(pc, 0, L), AF.Sign, bias=-63.25)
        if t == len(o) - 2:
            mm = [(B(pc, L, 2 * L), sh(0), T.K16[:], True, False, L)]
            mm += [(B(pc, L, 2 * L), I["I512"], B(al, L * x, L * x + L), False, x == t, L) for x in range(1, t + 1)]
            P("pick", ["Z2", "K16", "I512"] + [(al, x) for x in range(1, t + 1)], [pc], mm)
            V("lv", L, ["ipf"], [pc, ("lv", w)], "ts", B("lv", L * w, L * w + L), B(pc, L, 2 * L), row, 512.0 * t, ALU.add, ALU.add)

    def walk(w):
        va, Tn = ("va", "vb")[w], len(OFF[w]) - 1
        for t in range(Tn + 1):
            if t:
                image(w, t)
            sums(w, t)
        gather("vf", OPT["vf"][w], lambda c: [("lv", w)] + [(va, t, x) for t in range(1, Tn + 1) for x in range(2)], ("vf",), "vf", 0, B(va, 0, NK * Tn), "lv", L * w)

    tag[0] = (0, 2, 0)
    V("jg", GA * NK, ["stu"] + both("ohn") + jk, both("mj"), "tt", T.mj[:], B("JW", 0, W).indirect(B("stu", 0, L)), T.ohn[:], ALU.mult)
    series(0, 0, [0, 1])
    walk(0)
    tag[0] = (1, 2, -1)
    ak = [("Aa", t) for t in range(9)]
    P("eb", ["Z2", "ones", "Ip", "Im"] + both("ea") + ak, ["pw0", "pw1"],
      [(B("pw1", 0, L), I["Ip"], B("ones", 0, L), True, False, L), (B("pw1", 0, L), I["Im"], B("Aa", 8 * L, 9 * L), False, True, L),
       (B("pw0", 0, n), sh(0), T.ea[:], True, False, n), (B("pw0", 0, n), I["Ip"], B("Aa", 0, 8 * L), False, False, n),
       (B("pw0", 0, n), I["Im"], B("Aa", L, 9 * L), False, True, n)])
    S("eb", L, [], ["pw1", ("eb", 0)], B("eb", 0, L), B("pw1", 0, L), AF.Copy)
    S("eb", n, [], ["pw0", ("eb", 1)], B("eb", L, 9 * L), B("pw0", 0, n), AF.Copy)
    gates(1, 1, 4, "pw1")
    gates(1, 4, 10, "pw0")
    for c in range(2):
        tag[0] = (1, c, -1)
        ax, am, pv, pj, a = "ax%d" % c, "am%d" % c, "pv%d" % c, "pj%d" % c, n * c
        vf, eq, oy, gp, mj = (B(x, a, a + n) for x in ("vf", "eq", "oy", "Gp", "mj"))
        old, fly = c in OPT["old"], c in OPT["fly"]
        if old:
            P("m1", ["Z2", ("Gp", c)], [pj], [(B(pj, 0, n), sh(0), gp, True, True, n)])
        else:
            P("m1", ["In", "ones"], [pj], [(B(pj, 0, n), I["In"], T.ones[:], True, False, n)])
        if fly:
            src, sk = vf, ("vf", c)
            for bi in range(4):
                P("mx", [("ROT", bi), sk], [pv], [(B(pv, 0, n), B("ROT", 128 * bi, 128 * bi + 128), src, True, True, n)])
                out, key = ((B(am, 0, n), am), (eq, ("eq", c)), (B(am, 0, n), am), (B(pv, 0, n), pv))[bi]
                V("mx", n, [sk], [pv, key], "tt", out, src, B(pv, 0, n), ALU.max)
                src, sk = out, key
        else:
            src, sk, wd, pos = "vf", ("vf", c), n, a
            for bi in range(4):
                hf, mm = wd // 2, []
                for j in range(2):
                    for k in range(2):
                        q = 4 * bi + 2 * j + k
                        mm.append((B(pv, hf * j, hf * j + hf), B("AM", 128 * q, 128 * q + 128), B(src, pos + hf * k, pos + hf * k + hf), k == 0, k == 1, hf))
                P("mx", [("AM", 4 * bi + y) for y in range(4)] + [sk], [pv], mm)
                S("mx", hf, [], [pv, ax], B(ax, 0, hf), B(pv, 0, hf), AF.Copy)
                npos = 0 if bi == 0 else pos + wd
                V("mx", hf, [ax], [pv, (am, bi)], "tt", B(am, npos, npos + hf), B(ax, 0, hf), B(pv, hf, 2 * hf), ALU.max)
                src, sk, wd, pos = am, (am, bi), hf, npos
        on_v = fly or c in OPT["eqv"]
        if not fly:
            mm = [] if on_v else [(B(pv, 0, n), I["In"], vf, True, False, n)]
            mm += [(B(pv, K * r, K * r + K), B("RM", 128 * r, 128 * r + 128), B(am, pos, pos + K), on_v, on_v or r == 15, K) for r in range(16)]
            P("rep", rmk + ["In", ("vf", c), sk], [pv], mm)
        if on_v:
            V("eq", n, [("vf", c)], [pv, ("eq", c)], "tt", eq, vf, B(pv, 0, n), ALU.is_equal)
        else:
            S("eq", n, [], [pv, ("eq", c)], eq, B(pv, 0, n), AF.Relu, bias=1.0, scale=-1.0)
        if not old:
            P("ltr", ["M1", "Z2", ("eq", c), ("Gp", c)], [pj], [(B(pj, 0, n), T.M1[:], eq, False, False, n), (B(pj, 0, n), sh(0), gp, False, True, n)])
            relu("m0", c in OPT["mjv"], n, [], [pj, ("mj", c)], mj, B(pj, 0, n))
        P("oy", ["M1", ("eq", c)], [pv], [(B(pv, 0, n), T.M1[:], eq, True, True, n)])
        relu("oy", c in OPT["oyv"], n, [], [pv, ("oy", c)], oy, B(pv, 0, n))
        if old:
            V("m0", n, [("oy", c)], [pj, ("mj", c)], "tt", mj, oy, B(pj, 0, n), ALU.mult)
    for cs in ([0], [1]) if (1, 0) in OPT["split"] else ([0, 1],):
        tag[0] = (1, cs[0] if len(cs) == 1 else 2, 0)
        series(1, 0, cs)
    tag[0] = (1, 2, -1)
    for pw, blocks in (("pw0", range(1, 9)), ("pw1", [0])):
        mm = []
        for i, b in enumerate(blocks):
            u = -(b - 1) % N if b else 8
            mm.append((B(pw, L * i, L * i + L), sh(1 - b if b else 0), B("LT", L * u, L * u + L), True, False, L))
            mm.append((B(pw, L * i, L * i + L), I["I16"], B("eb", L * b, L * b + L), False, True, L))
        P("l1", ["Z2", "I16", "LT", "LY"] + both("eb"), [pw], mm)
        m = L * len(blocks)
        S("l1", m, [], [pw, ("L1", pw)], B("L1", L * blocks[0], L * blocks[0] + m), B(pw, 0, m), AF.Copy)
    P("y1", ["Z1x"] + both("oy"), ["pw1"], [(B("pw1", 0, L), sel(r, 0, "Z1x"), B("oy", r, NK, 16), r == 0, r == 15, L) for r in range(16)])
    S("y1", L, [], ["pw1", "y1"], B("L1", 9 * L, 10 * L), B("pw1", 0, L), AF.Copy)
    walk(1)
    tag[0] = (1, 2, 10)
    xo = {"xe": [], "xv": [], "xt": []}

    def stage(sem, nbytes, reads, out, in_):
        xo[sem].append((sem, len(xo[sem])))
        DM(sem, nbytes, reads, [xo[sem][-1]], out, in_)

    for j, (t0, t1) in enumerate(((1, 5), (5, 7), (7, 9), (9, 10))):
        pw, a, m, last = "pw%d" % (j % 2), L * (t0 - 1), L * (t1 - t0), t0 == 9
        wd = m + L * last
        mm = [(B(pw, 0, wd), sh(0), B("L1", a, a + wd), True, False, wd), (B(pw, 0, m), I["I8"], B("Ab", a, a + m), False, False, m),
              (B(pw, 0, m), I["J8"], B("Ab", a + L, a + L + m), False, not last, m)]
        if last:
            mm += [(B(pw, L, 2 * L), I["I8"], B("Ab", 0, L), False, False, L), (B(pw, L, 2 * L), I["J8"], B("Ab", 9 * L, 10 * L), False, True, L)]
        P("yl", ["Z2", "I8", "J8", ("L1", "pw0"), ("L1", "pw1"), "y1", ("Ab", 0)] + [("Ab", t) for t in range(t0 - 1, t1)], [pw], mm)
        V("yl", wd, [], [pw, ("YL", a)], "ts", B("YL", a, a + wd), B(pw, 0, wd), 16.0, None, ALU.min)
        for t in range(t0, t1):
            d, b = t - 2, L * (t - 1)
            if t == 1:
                stage("xe", 16384, [("YL", a)], T.ZE[0:8, 0:16, :], B("YL", 0, L))
                continue
            for i0, i1, p0 in runs(0, N, d):
                out = T.ZE[p0:p0 + i1 - i0, 16 * (7 - d):16 * (8 - d), :] if d < 7 else T.ZT[p0:p0 + i1 - i0, 0:64, :]
                stage("xe" if d < 7 else "xt", 2048 * (i1 - i0), [("YL", a)], out, T.YL[16 * i0:16 * i1, b:b + L])
        if last:
            stage("xt", 16384, [("YL", a)], T.ZT[0:8, 64:128, :], B("YL", 9 * L, 10 * L))
    vn = [("VN", r) for r in range(16)]
    for r in range(16):
        out, src = B("VN", L * r, L * r + L), B("vf", r, NK, 16)
        if r < OPT["permv"]:
            V("vn", K, both("vf"), [vn[r]], "copy", out, src)
        else:
            S("vn", L, both("vf"), [vn[r]], out, src, AF.Copy)
    stage("xv", 262144, vn, T.ZV[0:8], T.VN[:])
    send(ALL, "re", 16384, xo["xe"], lambda x: T.ZE[x - 1], lambda x: T.ZE[15 - x])
    send(ALL, "rv", 32768, xo["xv"], lambda x: T.ZV[x - 1], lambda x: T.ZV[15 - x])
    send(ALL, "rt", 4096, xo["xt"], lambda x: T.ZT[x - 1], lambda x: T.ZT[15 - x])
    for i0, i1, g0 in runs(0, N, R):
        g1, a, z, m, s1 = g0 + i1 - i0, 7 + i0, 7 + i1, 2048 * (i1 - i0), (R + 1) % N
        for u0, u1, s0 in runs(1, N, R + 1):
            DM("stores", m * (u1 - u0), xo["xe"] + ["re"], [("out",)], T.yl[g0:g1, NK * s0:NK * (s0 + u1 - u0)], T.ZE[a:z, 16 * u0:16 * u1, :])
        DM("stores", m, xo["xe"] + ["re"], [("out",)], T.yi[g0:g1, 0:NK], T.ZE[a:z, 0:16, :])
        DM("stores", 16 * m, xo["xv"] + ["rv"], [("out",)], T.yv[16 * g0:16 * g1, :], T.ZV[a:z])
        DM("stores", m, xo["xt"] + ["rt"], [("out",)], T.yl[g0:g1, NK * s1:NK * s1 + NK], T.ZT[a:z, 0:64, :])
        DM("stores", m, xo["xt"] + ["rt"], [("out",)], T.yi[g0:g1, NK:2 * NK], T.ZT[a:z, 64:128, :])
    return ops


def depend(ops):
    writer, readers = {}, {}
    for k, o in enumerate(ops):
        d = {}
        for key in o["r"]:
            d[writer[key]] = True
        for key in o["w"]:
            if key == ("out",):
                continue
            for x in ([writer[key]] if key in writer else []) + readers.get(key, []):
                d.setdefault(x, False)
        if "after" in o:
            d[o["after"]] = True
        o["d"] = d
        for key in o["w"]:
            writer[key] = k
            readers[key] = []
        for key in o["r"]:
            readers.setdefault(key, []).append(k)


def order(ops):
    best = now = replay(ops, order0(ops))
    for _ in range(PASSES):
        now = replay(ops, justify(ops, now))
        if now[0] < best[0]:
            best = now
    return best[1]


def waits(ops):
    return [[(x, WAKE if ops[x]["q"] != o["q"] else SELF) for x in o["d"]] for o in ops]


def replay(ops, seq):
    pre = waits(ops)
    for _ in range(5):
        st, end, free, lane = [0.0] * len(ops), [0.0] * len(ops), {}, 0.0
        for k in seq:
            o = ops[k]
            t = max([free.get(o["q"], 0.0)] + [end[x] + a for x, a in pre[k]])
            st[k] = t
            e = t + o["dur"]
            if o["q"] != "net":
                free[o["q"]] = e
            if o["tail"]:
                lane = max(lane, e) + o["tail"]
                e = lane + o["lat"]
            end[k] = e
        new = sorted(seq, key=lambda k: st[k])
        same = [k for k in new if ops[k]["tail"]] == [k for k in seq if ops[k]["tail"]]
        seq = new
        if same:
            break
    return max(end), seq, st, end


def place(ops, key, pre, full, gap):
    cnt = len(ops)
    nxt, left = [[] for _ in ops], [len(p) for p in pre]
    for k in range(cnt):
        for x, _ in pre[k]:
            nxt[x].append(k)
    ready, busy, st = [k for k in range(cnt) if not left[k]], {}, [0.0] * cnt
    while ready:
        k = min(ready, key=lambda x: (key[x], x))
        ready.remove(k)
        t = max([0.0] + [st[x] + full[x] + a for x, a in pre[k]])
        if ops[k]["q"] != "net":
            t += gap[k]
            row, i = busy.setdefault(ops[k]["q"], []), 0
            while i < len(row) and row[i][0] <= t:
                i += 1
            if i:
                t = max(t, row[i - 1][1])
            while i < len(row) and t + ops[k]["dur"] > row[i][0]:
                t = row[i][1]
                i += 1
            row.insert(i, (t, t + ops[k]["dur"]))
            t -= gap[k]
        st[k] = t
        for y in nxt[k]:
            left[y] -= 1
            if not left[y]:
                ready.append(y)
    return st


def justify(ops, now):
    _, seq, st, end = now
    cnt = len(ops)
    full = [end[k] - st[k] for k in range(cnt)]
    pre, back = waits(ops), [[] for _ in ops]
    for k in range(cnt):
        for x, a in pre[k]:
            back[x].append((k, a))
    for q in ("sync", "g"):
        row = [k for k in seq if ops[k]["q"] == q]
        for a, b in zip(row, row[1:]):
            back[a].append((b, ops[a]["dur"] - full[a]))
            pre[b].append((a, ops[a]["dur"] - full[a]))
    late = place(ops, [-e for e in end], back, full, [full[k] - ops[k]["dur"] for k in range(cnt)])
    early = place(ops, [-late[k] - full[k] for k in range(cnt)], pre, full, [0.0] * cnt)
    return sorted(range(cnt), key=lambda k: (early[k], k))


def order0(ops):
    cnt = len(ops)
    nxt = [[] for _ in range(cnt)]
    for k, o in enumerate(ops):
        for x in o["d"]:
            nxt[x].append(k)
    prio = [0.0] * cnt
    for k in range(cnt - 1, -1, -1):
        o = ops[k]
        best = 0.0
        for y in nxt[k]:
            best = max(best, prio[y] + WAKE)
        prio[k] = best + o["dur"] + o["lat"] + o["tail"]
    urge = []
    for k, o in enumerate(ops):
        name, tg = o["tag"]
        urge.append(prio[k] + o["bonus"] + URGE.get((name,) + tg[:2] if tg else name, 0) + (URGE.get((name,) + tg, 0) if tg else 0))
    left = [len(o["d"]) for o in ops]
    ready = [float(HOLD.get(o["tag"][0], 0.0)) for o in ops]
    cand = {}
    for k in range(cnt):
        if left[k] == 0:
            cand.setdefault(ops[k]["q"], []).append(k)
    free, lane, out = {}, 0.0, []

    def rank(x):
        return urge[x]
    while cand:
        t, q = None, None
        for y in cand:
            f = max(free.get(y, 0.0) if y != "net" else 0.0, min(ready[k] for k in cand[y]))
            if t is None or f < t:
                t, q = f, y
        k = max((x for x in cand[q] if ready[x] <= t + (GAP if q != "net" else 0.0)), key=rank)
        if ready[k] > t:
            fit = [x for x in cand[q] if ready[x] <= t and t + ops[x]["dur"] <= ready[k] + 20.0]
            if fit:
                k = max(fit, key=rank)
            else:
                t = ready[k]
        cand[q].remove(k)
        if not cand[q]:
            del cand[q]
        o = ops[k]
        end = t + o["dur"]
        free[q] = end
        if o["tail"]:
            lane = max(end, lane) + o["tail"]
            end = lane + o["lat"]
        out.append(k)
        for y in nxt[k]:
            left[y] -= 1
            ready[y] = max(ready[y], end + (WAKE if ops[y]["q"] != q else SELF))
            if left[y] == 0:
                cand.setdefault(ops[y]["q"], []).append(y)
    return out


QSEM = {"pe": "kpe", "v": "kv", "s": "ks"}


def rank_program(g, core, T, topo):
    rank = T.rank_of(core)
    if rank is None:
        return
    ops = program(rank, T, topo)
    depend(ops)
    seq = order(ops)
    total = {}
    for o in ops:
        if o["dma"]:
            total[o["sem"]] = total.get(o["sem"], 0) + 16
    eng = {"pe": g.tensor, "v": g.vector, "s": g.scalar, "g": g, "sync": g.sync}
    count, sent, arrived, know = {}, 0, {}, {}
    for k in seq:
        o = ops[k]
        q = o["q"]
        if q == "net":
            o["done"] = [(o["sem"], o["cnt"])]
            o["know"] = {o["sem"]: o["cnt"]}
            arrived[o["sem"]] = o["cnt"]
            continue
        mine = know.setdefault(q, {})
        need, merge = {}, []
        for x, hard in o["d"].items():
            p = ops[x]
            if p["sem"] == "remote" or (not hard and p["q"] == q == "pe"):
                continue
            for s, c in p["done"]:
                if mine.get(s, 0) < c:
                    need[s] = max(need.get(s, 0), c)
            merge.append(x)
        for s in sorted(need):
            implied = False
            for x in merge:
                if ops[x]["know"].get(s, 0) >= need[s] and ops[x]["done"][0][0] != s:
                    implied = True
            if not implied:
                eng[q].wait_ge(T.sem[s], int(need[s]))
        for x in merge:
            for s, c in ops[x]["know"].items():
                mine[s] = max(mine.get(s, 0), c)
        sem = o["sem"] or QSEM.get(q)
        for call in o["calls"]:
            ins = call(g)
            if sem == "remote":
                sent += o["cnt"]
            elif o["dma"]:
                ins.then_inc(T.sem[sem], 16)
            else:
                count[sem] = count.get(sem, 0) + 1
                ins.then_inc(T.sem[sem], 1)
        o["know"] = dict(mine)
        if sem == "remote":
            o["done"] = []
            continue
        c = total[sem] if o["dma"] else count[sem]
        o["done"] = [(sem, c)]
        o["know"][sem] = max(o["know"].get(sem, 0), c)
    for s in ("kpe", "kv", "ks", "kg"):
        g.wait_ge(T.sem[s], int(count[s]))
    for s in sorted(total):
        g.wait_ge(T.sem[s], int(total[s]))
    for s in sorted(arrived):
        g.wait_ge(T.sem[s], int(arrived[s]))
    g.wait_ge(T.sem.ls, int(sent))
